import numpy as np, ml_dtypes
CORES = [113,118,241,246]
N = 4
BF = ml_dtypes.bfloat16
def gentries(a):
    return np.ascontiguousarray(a.reshape(8, 16, -1).transpose(0, 2, 1)).reshape(8, -1)
def gtable(e):
    e = np.asarray(e); return np.ascontiguousarray(e.reshape(8, -1, 16).transpose(0, 2, 1)).reshape(128, -1).astype(np.int32)
B, H, D, O, CAP, RO = 2048, 1024, 1024, 1280, 256, 3
K2, K3, K5 = 37, 611, 1237
def parts(rng):
    wt = (rng.choice(np.array([12, 20, 40, 64]), (N, 8, 16, 1)) * rng.random((N, 8, 16, B))).astype(np.int64)
    kid = rng.integers(0, B // 16, (N, 8, 16, B)); noise = rng.integers(0, 64, (N, 8, 16, H))
    for q in range(N):
        for g in rng.permutation(8)[:2]: kid[q, g] = rng.integers(0, B // 16, 8)[rng.integers(0, 8, (16, B))]
    room = np.minimum(rng.integers(60, 256, (N, 8, 1, D)) + rng.integers(0, 41, (N, 8, 16, D)), 255)
    room = np.where(rng.random(room.shape) < 0.01, rng.integers(0, 60, room.shape), room)
    need = (rng.integers(10, 201, (N, 8, 1, O)) * rng.random((N, 8, 16, O))).astype(np.int64)
    return wt, kid, noise, room, need, rng.integers(0, B, (N, 8, O)), rng.integers(0, H, (N, 8, O))
def sure(rng, wt, noise, q, g, win):
    noise[q, g] = rng.integers(8, 64, (16, H)); v = rng.integers(0, 8, (16, B)); v[win, np.arange(B)] = 63; wt[q, g] = v
def pack(wt, kid, noise, room, need, begin, salt):
    a = [np.ascontiguousarray(v.reshape(N, 128, -1)).astype(np.float32).astype(BF) for v in (wt, kid, noise, room, need)]
    return {"wt": a[0], "kid": a[1], "noise": a[2], "room": a[3], "need": a[4], "begin": np.stack([gtable(v) for v in begin]), "salt": np.stack([gtable(v) for v in salt])}
def setup_inputs(rng):
    return pack(*parts(rng))
def setup_inputs_cap(rng):
    wt, kid, noise, room, need, begin, salt = parts(rng)
    win = rng.integers(0, 16, (N, 8, B)); win[..., :16] = np.arange(16)
    win[:, 6] = (np.arange(B) & (N - 1)) + N * rng.integers(0, 16 // N, (N, B)); room[:, 6] = np.maximum(room[:, 6], 200)
    noise = rng.integers(8, 64, noise.shape); wt = rng.integers(0, 8, wt.shape); np.put_along_axis(wt, win[:, :, None, :], 63, 2)
    for q in range(N):
        for g in range(8):
            r = (q + 1 + int(rng.integers(0, N - 1))) % N; n = (CAP, CAP + 1, CAP - 1, 0, O, 1, CAP, CAP)[g]
            others = np.array([i for i in range(N) if i != r])
            to = rng.permutation(np.concatenate([np.full(n, r), rng.choice(others, O - n)]))
            if g < 2:
                i = np.flatnonzero(to == r)[-1]; to[i] = to[O - 1]; to[O - 1] = r
            if g == 6: to = rng.permutation(np.arange(O) & (N - 1))
            if g == 7:
                to = rng.choice(others, O); to[np.argsort(rng.permutation(16)[np.arange(O) % 16], kind="stable")[:n]] = r
            for i in range(N):
                m = np.flatnonzero(to == i); begin[q, g, m] = rng.choice(np.flatnonzero((win[q, g] & (N - 1)) == i), len(m))
    return pack(wt, kid, noise, room, need, begin, salt)
def setup_inputs_ties(rng):
    wt, kid, noise, room, need, begin, salt = parts(rng)
    wt = rng.integers(0, 3, wt.shape) * (rng.random((N, 8, 1, B)) > 0.1); noise = rng.integers(0, 3, noise.shape)
    wt = np.where(rng.random((N, 8, 1, B)) < 0.15, rng.integers(1, 3, (N, 8, 1, B)), wt)
    noise = np.where(rng.random((N, 8, 1, H)) < 0.15, rng.integers(1, 3, (N, 8, 1, H)), noise) * (rng.random((N, 8, 1, H)) > 0.05)
    room = np.where(rng.random(room.shape) < 0.003, 0, np.zeros(room.shape, np.int64) + rng.choice(np.array([99, 100, 100, 101, 255]), (N, 8, 1, D)))
    need = np.where(rng.random(need.shape) < 0.1, rng.choice(np.array([0, 99, 100, 101, 255]), (N, 8, 1, O)), 0)
    begin[:, 1::4] = rng.choice(np.array([0, B - 1]), (N, 2, O)); salt[:, 2::4] = rng.choice(np.array([0, H - 1]), (N, 2, O))
    kid[:, 7] = rng.integers(0, B // 16, (N, 16, B)); win = rng.integers(0, 16, (N, B))
    for q in range(N): sure(rng, wt, noise, q, 7, win[q])
    to = 16 * np.take_along_axis(kid[:, 7], win[:, None, :], 1)[:, 0] + win
    few = rng.integers(0, B, (N, 24)); begin[:, 7] = np.take_along_axis(few, rng.integers(0, 24, (N, O)), 1)
    need[:, 7] = np.maximum(need[:, 7], 1); room[:, 7] = 0
    for s in range(2 * (RO - 1), -1, -2):
        b = np.take_along_axis(to, (few + K5 * s) & (B - 1), 1); own = b & (N - 1)
        room[own, 7, :, to[own, b] & (D - 1)] = 255 if s == 2 * (RO - 1) else 0
    return pack(wt, kid, noise, room, need, begin, salt)
def setup_inputs_again(rng):
    wt, kid, noise, room, need, begin, salt = parts(rng)
    for q in range(N):
        for g in range(8): kid[q, g] = rng.integers(0, B // 16, 2)[rng.integers(0, 2, (16, B))]
        kid[q, 3] = rng.integers(0, B // 16); wt[q, 3] = 0; wt[q, 3, rng.integers(0, 16)] = 63
    noise[:, 3] = np.maximum(noise[:, 3], 1); room = np.maximum(room, 200)
    begin[:, ::2] = rng.choice(np.array([0, 5, B // 2, B - 1]), (N, 4, O)); salt[:, ::2] = rng.choice(np.array([0, 1, H // 2, H - 1]), (N, 4, O))
    r = int(rng.integers(0, N)); c = r + N * int(rng.integers(0, 16 // N))
    win = (np.arange(B) & (N - 1)) + N * rng.integers(0, 16 // N, (N, B)); win[r, r::N] = c; kid[r, 5, c, r::N] = kid[r, 5, c, r]
    for q in range(N): sure(rng, wt, noise, q, 5, win[q])
    begin[:, 5] = r + N * rng.integers(0, B // N, (N, O))
    return pack(wt, kid, noise, room, need, begin, salt)
def setup_inputs_full(rng):
    wt, kid, noise, room, need, begin, salt = parts(rng); q = rng.permutation(N)
    need = np.where(rng.random((N, 8, 1, O)) < 0.05, 255, np.maximum(need, 1)); room[q[0]] = 0; need[q[1]] = 0; room[q[2]] = 255
    r, a = int(q[2]), int(q[3]); walk = (K5 * np.arange(B)) & (B - 1)
    for g in range(8):
        win = rng.choice(np.array([c for c in range(16) if c & (N - 1) != r]), B); win[walk[::8]] = r + N * rng.integers(0, 16 // N, B // 8)
        sure(rng, wt, noise, a, g, win)
        at = rng.integers(1, 4, O); at[rng.permutation(O)[:CAP // 2]] = 0
        begin[a, g] = walk[8 * rng.integers(0, B // 8, O) + at]
    return pack(wt, kid, noise, room, need, begin, salt)
def setup_inputs_spread(rng):
    wt, kid, noise, room, need, begin, salt = parts(rng); ex = np.array([0.3, 1.0, 3.0])
    wt = np.minimum((64 * rng.random(wt.shape) ** rng.choice(ex, (N, 8, 1, B))).astype(np.int64), 63)
    noise = np.minimum((64 * rng.random(noise.shape) ** rng.choice(ex, (N, 8, 1, H))).astype(np.int64), 63)
    kid = np.minimum((B // 16 * rng.random(kid.shape) ** 3).astype(np.int64), B // 16 - 1)
    room = np.minimum((256 * rng.random(room.shape) ** rng.choice(np.array([0.0, 0.02, 0.1, 1.0]), (N, 8, 1, D))).astype(np.int64), 255)
    need = np.minimum((np.exp2(8 * rng.random((N, 8, 1, O))) * rng.random(need.shape)).astype(np.int64), 255)
    begin = np.minimum((B * rng.random((N, 8, O)) ** 2).astype(np.int64), B - 1); salt = np.minimum((H * rng.random((N, 8, O)) ** 3).astype(np.int64), H - 1)
    return pack(wt, kid, noise, room, need, begin, salt)
def check_inputs(d):
    bad = []
    for k, hi in (("wt", 63), ("kid", B // 16 - 1), ("noise", 63), ("room", 255), ("need", 255), ("begin", B - 1), ("salt", H - 1)):
        v = np.asarray(d[k]).astype(np.float32)
        if not np.all((v >= 0) & (v <= hi)): bad.append("range of " + k)
        if not np.all(v == np.floor(v)): bad.append("whole numbers in " + k)
    return bad
def columns(a):
    return np.ascontiguousarray(a.astype(np.float32).astype(np.int32).reshape(N, 8, 16, -1).transpose(0, 1, 3, 2))
def choose(w, k, z, r, b, h):
    g = np.arange(8)[None, :, None]
    c = np.argmax(w[r, g, b] * z[r, g, h], axis=-1)
    return 16 * k[r, g, b, c].astype(np.int64) + c
def reference(wt, kid, noise, room, need, begin, salt):
    w, k, z, rm, nd = columns(wt), columns(kid), columns(noise), columns(room), columns(need)
    be = np.stack([gentries(a) for a in begin]).astype(np.int64); sa = np.stack([gentries(a) for a in salt]).astype(np.int64)
    home = np.arange(N)[:, None, None]; g = np.arange(8)[None, :, None]
    t = np.zeros((N, 8, O), np.int64); one = np.full((N, 8, O), -1, np.int64); two = np.full((N, 8, O), -1, np.int64)
    for rnd in range(RO):
        takes = two < 0
        b0 = (be + K5 * t) & (B - 1)
        b1 = choose(w, k, z, home, b0, (sa + K2 * b0 + K3 * t) & (H - 1))
        own = b1 & (N - 1); goes = np.zeros((N, 8, O), bool)
        for r in range(N):
            m = (takes & (own == r)).astype(np.int64)
            goes = goes | ((m == 1) & (np.add.accumulate(m, axis=2) - m < CAP))
        d = choose(w, k, z, own, b1, (sa + K2 * b1 + K3 * t) & (H - 1)) & (D - 1)
        fits = np.all(nd <= rm[own, g, d], axis=-1)
        dev = own * D + d; keep = goes & fits & (dev != one)
        two = np.where(keep & (one >= 0), dev, two); one = np.where(keep & (one < 0), dev, one)
        t = t + np.where(goes, np.where(keep, 1, 2), 0)
    return {"ya": np.stack([gtable(a) for a in one]).astype(np.float32), "yb": np.stack([gtable(a) for a in two]).astype(np.float32)}

@@ -1,0 +1,584 @@
+from concourse.bass import DstId, RemoteDMATransfer
+from concourse.mybir import AluOpType as ALU, ActivationFunctionType as AF
+
+N, B, H, D, O, CAP = 4, 2048, 1024, 1024, 1280, 256
+K2, K3, K5 = 37, 611, 1237
+KH = (K3 + K2 * K5) % H
+W = O // 16
+TRI = 88
+RAW = D - 3 * TRI
+FW = B // N + TRI
+CH = [(0, (3, 2)), (5, (3, 2))]
+BIG = 1.5 * 2.0 ** 35
+
+SCRATCH = {
+    "wts": ("sbuf", [128, B], "bfloat16"), "kds": ("sbuf", [128, B], "bfloat16"), "nzs": ("sbuf", [128, H], "bfloat16"),
+    "nds": ("sbuf", [128, O], "bfloat16"), "R": ("sbuf", [128, N * D], "bfloat16"), "F": ("sbuf", [128, N * 2 * FW], "float16"),
+    "W2": ("sbuf", [128, B], "bfloat16"), "KK": ("sbuf", [128, B], "bfloat16"), "N2": ("sbuf", [128, N * H], "bfloat16"),
+    "N1": ("sbuf", [128, 2 * H], "bfloat16"), "Wg": ("sbuf", [128, O], "bfloat16"), "Kg": ("sbuf", [128, O], "bfloat16"),
+    "A": ("sbuf", [128, O], "float16"), "Z": ("sbuf", [128, O], "float32"), "Ft": ("sbuf", [128, O], "bfloat16"),
+    "pi": ("sbuf", [128, 6144], "int32"), "pf": ("sbuf", [128, 6144], "float32"), "pb": ("sbuf", [128, 10240], "bfloat16"),
+    "ph": ("sbuf", [128, 8192], "float16"), "pu": ("sbuf", [128, 2048], "uint16"),
+}
+for _b in range(8):
+    SCRATCH["ps%d" % _b] = ("psum", [128, 512], "float32")
+SEMAPHORES = (["cv", "ca", "cp", "cg", "sent"] + ["d%d" % i for i in range(14)]
+              + ["%s%d" % (a, r) for a in ("f0_", "f1_", "r0_", "r1_") for r in range(N)])
+
+OPT = {"cy": 1.0, "ga": 1.5, "pc": 0.55, "lat": 150.0, "xl": 1.5, "win": 30.0, "lead": [1000.0, 0.0, 0.0], "split": [1, 1, 1],
+       "jit": [0.0, 1], "relay": 1}
+PLAN = {}
+ORDER = [int(x) for x in """
+0 1 7 33 31 16 36 2 3 4 5 6 8 9 11 10 13 39 17 183 97 14 37 32 18 63 38 20 102 19 99 24 56 49 52 25 64 185 21 50 34 22 40 184 23 45 47
+35 53 26 57 27 65 66 70 71 48 29 72 100 58 54 30 60 28 67 73 74 75 46 101 103 41 68 96 230 134 138 69 76 77 135 106 105 110 42 12 109
+104 139 98 244 232 231 107 108 136 43 137 245 111 116 78 117 112 140 113 141 118 119 114 142 145 120 115 146 143 15 121 238 122 147
+148 144 149 218 123 213 255 260 124 150 130 151 127 152 81 82 85 86 61 62 79 83 84 80 87 163 181 239 166 169 131 189 88 128 125 172
+164 153 159 160 126 129 167 44 156 157 132 154 133 155 158 165 89 226 90 175 168 170 201 200 199 171 173 174 207 176 177 208 250 182
+186 187 188 91 92 178 179 180 210 209 249 251 252 59 246 55 214 268 161 162 51 194 190 195 202 93 94 95 219 261 212 211 254 196 191
+220 221 215 222 216 256 294 253 257 258 217 262 263 192 193 203 223 259 224 227 264 225 228 204 265 266 269 205 267 270 197 198 206
+289 235 318 229 234 236 274 323 233 271 273 237 240 275 272 241 248 242 243 276 277 247 283 285 284 281 278 279 282 287 280 290 291
+292 295 286 288 313 312 314 296 297 293 298 299 317 300 316 324 319 301 302 303 320 321 304 322 315 325 326 327 305 360 397 355 328
+306 329 308 307 330 309 368 402 349 350 351 352 310 331 311 334 332 337 335 333 353 354 336 338 356 357 361 358 359 362 363 394 392
+403 404 410 391 439 364 444 398 339 393 343 365 340 366 341 369 399 395 367 342 396 344 400 370 405 345 401 406 372 407 408 468 411
+371 409 346 347 412 374 348 413 414 473 375 376 417 373 416 377 378 418 379 383 380 384 381 419 385 415 390 433 434 435 436 420 387
+425 421 386 426 422 427 429 437 423 438 428 462 463 464 382 424 445 440 441 442 443 446 447 448 449 450 466 508 469 451 452 467 453
+458 455 454 459 456 470 471 472 457 474 465 475 476 477 460 491 478 461 479 389 513 388 430 431 432 502 503 504 505 509 549 521 480
+510 506 511 514 544 515 481 507 482 484 487 483 485 512 488 486 516 517 492 489 518 490 538 539 557 545 550 519 541 522 551 543 552
+540 495 494 496 493 542 520 553 497 546 547 548 523 526 554 524 555 525 556 528 498 558 499 559 500 560 561 564 562 501 527 565 529
+530 563 531 532 535 566 533 567 536 571 568 572 569 534 537 570 573""".split()]
+
+
+def rank_program(g, core, T, topo):
+    me = T.rank_of(core)
+    if me is None:
+        return
+    cores = list(T.cores)
+    mate = [r for r in range(N) if r != me and cores[r] in topo.cores_of(core)][0]
+    far = [r for r in range(N) if r != me and r != mate]
+    far.sort(key=lambda r: topo.die(cores[r]) != topo.die(core))
+    queue = {"v": g.vector, "a": g.scalar, "p": g.tensor, "s": g.sync, "g": g}
+    ops, lastw, readers, bank = [], {}, {}, {}
+    used = {"pi": 0, "pf": 0, "pb": 0, "ph": 0, "pu": 0}
+    ndma, tok, lead = [0], [0], [0.0]
+    LAT = OPT["lat"]
+
+    def new(pool, n):
+        a = used[pool]
+        used[pool] = a + (n + 15) // 16 * 16
+        tok[0] += 1
+        return (T[pool], a, n, "t%d" % tok[0])
+
+    def ap(x, a=0, b=None, s=1):
+        b = x[2] if b is None else b
+        return x[0][:, x[1] + a:x[1] + b:s] if s != 1 else x[0][:, x[1] + a:x[1] + b]
+
+    def op(eng, fn, rd=(), wr=(), banks=(), cost=55.0, lat=0.0, sem=None, after=()):
+        i = len(ops)
+        deps = set()
+        for t in rd:
+            t = t if isinstance(t, str) else t[3]
+            if t in lastw:
+                deps.add(lastw[t])
+            readers.setdefault(t, []).append(i)
+        for t in wr:
+            t = t if isinstance(t, str) else t[3]
+            if t in lastw:
+                deps.add(lastw[t])
+            deps.update(readers.get(t, []))
+            lastw[t] = i
+            readers[t] = []
+        for b in banks:
+            e, cur, prev = bank.get(b, (None, [], []))
+            if e != eng:
+                e, cur, prev = eng, [], cur
+            deps.update(prev)
+            bank[b] = (e, cur + [i], prev)
+        deps.discard(i)
+        c4 = cost if isinstance(cost, tuple) else (cost, 0, 0, 0)
+        ops.append({"e": eng, "fn": fn, "deps": deps, "c4": c4, "lat": lat, "sem": sem, "after": set(after), "lead": lead[0],
+                    "cost": c4[0] + OPT["cy"] * (c4[1] + OPT["ga"] * c4[2]) + OPT["pc"] * c4[3]})
+        return i
+
+    def vc(n, c=1.0, f=0.0):
+        return (f, max(64.0, n * c), 0, 0)
+
+    def gc_(n, f=50.0):
+        return (f, 0, n, 0)
+
+    def ts(out, in0, s1, s2, o0, o1, rd, wr, n, c=1.0, banks=(), gather=False):
+        if o1 is None:
+            fn = lambda: g.vector.tensor_scalar(out, in0, s1, None, o0)
+        else:
+            fn = lambda: g.vector.tensor_scalar(out, in0, s1, s2, o0, o1)
+        return op("v", fn, rd, wr, banks, gc_(n) if gather else vc(n, c))
+
+    def tt(out, in0, in1, o, rd, wr, n, c=2.0, banks=(), gather=False):
+        return op("v", lambda: g.vector.tensor_tensor(out, in0, in1, o), rd, wr, banks, gc_(n) if gather else vc(n, c))
+
+    def cp(out, in_, rd, wr, n, c=1.0, banks=(), gather=False):
+        return op("v", lambda: g.vector.tensor_copy(out, in_), rd, wr, banks, gc_(n) if gather else vc(n, c))
+
+    def fill(out, v, wr, n):
+        return op("v", lambda: g.vector.memset(out, v), (), wr, cost=vc(n))
+
+    def scan(out, d0, d1, o0, o1, rd, wr, n, c=1.0, banks=()):
+        return op("v", lambda: g.vector.tensor_tensor_scan(out, d0, d1, 0.0, o0, o1), rd, wr, banks, vc(n, c))
+
+    def act(out, in_, bias, rd, wr, n, banks=(), gather=False, func=AF.Identity, scale=1.0):
+        return op("a", lambda: g.scalar.activation(out, in_, func, bias=bias, scale=scale), rd, wr, banks,
+                  gc_(n, 65.0) if gather else vc(n, 1.0, 30.0))
+
+    def mm(terms, rd, b, after=()):
+        def fn():
+            for (o_, l_, r_, st, sp, n) in terms:
+                last = g.tensor.matmul(o_, l_, r_, st, sp)
+            return last
+        return op("p", fn, rd, (), [b], (40.0, 0, 0, sum(max(64, t[5]) for t in terms)), after=after)
+
+    def group(out, pairs, n, start=True, stop=True):
+        return [(out, l_, r_, start and i == 0, stop and i == len(pairs) - 1, n) for i, (l_, r_) in enumerate(pairs)]
+
+    def dma(eng, out, in_, rd, wr, lat):
+        s = "d%d" % ndma[0]
+        ndma[0] += 1
+        return op(eng, lambda: queue[eng].dma_start(out, in_), rd, wr, (), 60.0, lat, (s, 16))
+
+    ps = [T["ps%d" % b] for b in range(8)]
+    R, F = T.R, T.F
+
+    beg, sal = new("pi", W), new("pi", W)
+    dma("s", R[:, me * D:(me + 1) * D], T.room[:], (), ["Rraw0_%d" % me, "Rraw1_%d" % me, "Rt%d" % me], 2600)
+    dma("a", ap(beg), T.begin[:], (), [beg], 2200)
+    dma("a", ap(sal), T.salt[:], (), [sal], 2200)
+    dma("s", T.nzs[:], T.noise[:], (), ["nzs"], 3300)
+    dma("s", T.wts[:], T.wt[:], (), ["wts"], 4700)
+    dma("s", T.kds[:], T.kid[:], (), ["kds"], 6100)
+    dma("s", T.nds[:], T.need[:], (), ["nds"], 7000)
+
+    col, prt = new("pi", 144), new("pi", 8)
+    op("g", lambda: g.iota(ap(col), [[1, 144]], 0, 0), (), [col], cost=400)
+    op("g", lambda: g.iota(ap(prt), [[0, 8]], 0, 1), (), [prt], cost=150)
+    pcol, gcol = new("pf", 1), new("pf", 1)
+    plo, phi = new("pi", 8), new("pi", 8)
+    cp(ap(pcol), ap(prt, 0, 1), [prt], [pcol], 1)
+    ts(ap(plo), ap(prt), 15, None, ALU.bitwise_and, None, [prt], [plo], 8)
+    ts(ap(phi), ap(prt), 4, None, ALU.logical_shift_right, None, [prt], [phi], 8)
+    ts(ap(gcol), ap(phi, 0, 1), 16.0, 15.0, ALU.mult, ALU.add, [phi], [gcol], 1)
+    wide1 = new("pb", 240)
+    ts(ap(wide1, 0, 128), ap(col, 0, 128), ap(pcol), None, ALU.is_equal, None, [col, pcol], [wide1], 128)
+    cp(ap(wide1, 128, 240), ap(wide1, 0, 112), [wide1], ["wide1b"], 112, 0.5)
+    consts = {(1, "pb", 128): wide1[:2] + (128, wide1[3])}
+
+    def diag(v, pool, wide=128):
+        if (v, pool, wide) not in consts:
+            x = new(pool, wide)
+            if pool == "pb":
+                act(ap(x), ap(wide1, 0, wide), 0.0, [wide1], [x], wide, scale=float(v))
+            else:
+                ts(ap(x), ap(wide1, 0, wide), float(v), None, ALU.mult, None, [wide1, "wide1b"][:1 + (wide > 128)], [x], wide, 0.5)
+            consts[(v, pool, wide)] = x
+        return consts[(v, pool, wide)]
+
+    pick = new("pb", 144)
+    ts(ap(pick), ap(col), ap(gcol), None, ALU.is_equal, None, [col, gcol], [pick], 144)
+    j_, r_, m8, t1, t2, t3 = [new("pi", 8) for _ in range(6)]
+    ts(ap(t1), ap(col, 0, 8), 16.0, None, ALU.mult, None, [col], [t1], 8)
+    tt(ap(j_), ap(t1), ap(plo), ALU.add, [t1, plo], [j_], 8)
+    ts(ap(r_), ap(j_), 7, None, ALU.bitwise_and, None, [j_], [r_], 8)
+    tt(ap(m8), ap(j_), ap(r_), ALU.subtract, [j_, r_], [m8], 8)
+    tt(ap(t2), ap(phi), ap(r_), ALU.subtract, [phi, r_], [t2], 8)
+
+    def rot(sign):
+        a, b, c = new("pi", 8), new("pi", 8), new("pi", 8)
+        ts(ap(a), ap(t2), float(sign), 8.0, ALU.mult, ALU.add, [t2], [a], 8)
+        ts(ap(b), ap(a), 7, None, ALU.bitwise_and, None, [a], [b], 8)
+        tt(ap(c), ap(b), ap(m8), ALU.add, [b, m8], [c], 8)
+        return c
+    rp, rx = rot(-1), rot(1)
+    w, wp = 40, 48
+    lperm2, lperm, lext = new("pu", 8), new("pu", 8), new("pu", 8)
+    cp(ap(lperm2), ap(rp), [rp], [lperm2], 8)
+    ts(ap(lperm), ap(rp), float(w - 1), None, ALU.min, None, [rp], [lperm], 8)
+    ts(ap(t3), ap(rx), float(w - 1), None, ALU.min, None, [rx], [t3], 8)
+    ts(ap(lext), ap(t3), 16.0, 15.0, ALU.mult, ALU.add, [t3], [lext], 8)
+    pat, rst, c1536 = new("pf", 384), new("pb", N * W), new("ph", w)
+    fill(ap(pat), 128.0, [pat], 384)
+    fill(ap(pat, 0, 384, 16), -2.0 ** 25, [pat], 24)
+    fill(ap(rst), 1.0, [rst], 160)
+    fill(ap(rst, 0, N * W, W), 0.0, [rst], 4)
+    fill(ap(c1536), 1536.0, [c1536], 20)
+    blk, tri, ta, tb, tc, td = new("pb", 128), new("pb", 128), new("pi", 128), new("pf", 1), new("pb", 128), new("pb", 128)
+    ts(ap(ta), ap(col, 0, 128), 4, None, ALU.logical_shift_right, None, [col], [ta], 128)
+    cp(ap(tb), ap(phi, 0, 1), [phi], [tb], 1)
+    ts(ap(blk), ap(ta), ap(tb), None, ALU.is_equal, None, [ta, tb], [blk], 128)
+    ts(ap(tc), ap(col, 0, 128), ap(pcol), -1.0, ALU.is_lt, ALU.mult, [col, pcol], [tc], 128)
+    tt(ap(td), ap(tc), ap(blk), ALU.mult, [tc, blk], [td], 128)
+    d512 = diag(-512, "pb")
+    tt(ap(tri), ap(td), ap(d512), ALU.add, [td, d512], [tri], 128)
+    nblk, ntri = new("pb", 128), new("pb", 128)
+    act(ap(nblk), ap(blk), 0.0, [blk], [nblk], 128, scale=-1.0)
+    act(ap(ntri), ap(tri), 0.0, [tri], [ntri], 128, scale=-1.0)
+    sgn, run = new("pb", (N + 1) * W), new("pb", (N + 1) * W)
+    for j, v in ((0, 1.0), (N, -1.0)):
+        fill(ap(sgn, j * W, (j + 1) * W), v, ["sgn%d" % j], 40)
+        scan(ap(run, j * W, (j + 1) * W), ap(rst, 0, W), ap(sgn, j * W, (j + 1) * W), ALU.mult, ALU.add, ["sgn%d" % j, rst], ["run%d" % j], 40)
+
+    s37, sraw, salh = new("pi", W), new("pi", W), new("ph", W)
+    ts(ap(s37), ap(beg), float(K2), None, ALU.mult, None, [beg], [s37], W)
+    tt(ap(sraw), ap(s37), ap(sal), ALU.add, [s37, sal], [sraw], W)
+    cp(ap(salh), ap(sal), [sal], [salh], W)
+    lists, bsh = [], []
+    for c, (b0, subs) in enumerate(CH):
+        k0 = 8 * b0
+        bs, l1, bh = new("pi", 2 * w), new("pu", 2 * w), new("ph", 2 * w)
+        cp(ap(bs, 0, w), ap(beg, k0, k0 + w), [beg], [bs], w)
+        ts(ap(bs, w, 2 * w), ap(sraw, k0, k0 + w), H - 1, None, ALU.bitwise_and, None, [sraw], [bs], w)
+        cp(ap(l1), ap(bs).indirect(ap(lperm2, 0, 5)), [bs, lperm2], [l1], 2 * w, gather=True)
+        cp(ap(bh), ap(bs), [bs], [bh], 2 * w)
+        lists.append(l1)
+        bsh.append(bh)
+    mine = T.N2[:, me * H:(me + 1) * H]
+    ts(mine, T.nzs[:], -32.0, None, ALU.add, None, ["nzs"], ["N2_0_%d" % me, "N2_1_%d" % me], H, 0.5)
+    for h in range(2):
+        dma("s", T.N1[:, h * H:(h + 1) * H], mine, ["N2_0_%d" % me], ["N1_%d" % h], 3000)
+
+    I, Ih = diag(1, "pb"), diag(1, "ph")
+    q = B // N
+    f0 = me * 2 * FW
+    rt = me * D + RAW
+    rch, big = new("pb", TRI), new("pb", q)
+    ts(ap(rch), R[:, rt + 2 * TRI:rt + 3 * TRI], 1 / 16, 160 - 7.5 / 16, ALU.mult, ALU.add, ["Rt%d" % me], [rch], TRI, 0.5)
+    d16, dm16, d64, dm64, d4096 = diag(16, "pb"), diag(-16, "pb"), diag(64, "pb"), diag(-64, "pb"), diag(4096, "pb")
+    mm(group(ps[2][:, 0:TRI], [(ap(d16), R[:, rt:rt + TRI]), (ap(I), ap(rch))], TRI)
+       + group(ps[2][:, TRI:2 * TRI], [(ap(d16), R[:, rt + TRI:rt + 2 * TRI]), (ap(I), R[:, rt + 2 * TRI:rt + 3 * TRI]),
+                                       (ap(dm16), ap(rch))], TRI), ["Rt%d" % me, rch, d16, dm16, I], 2)
+    ts(F[:, f0 + q:f0 + FW], ps[2][:, 0:TRI], -2208.0, None, ALU.add, None, (), ["F0t"], TRI, banks=[2])
+    ts(F[:, f0 + FW + q:f0 + 2 * FW], ps[2][:, TRI:2 * TRI], 512.0, None, ALU.add, None, (), ["F1t"], TRI, banks=[2])
+    mm(group(ps[3][:], [(ap(I), T.nzs[:, 0:q]), (ap(d64), T.wts[:, me::N])], q), ["nzs", "wts", I, d64], 3)
+    ts(F[:, f0:f0 + q], ps[3][:], -2048.0, None, ALU.add, None, (), ["F0_%d" % me], q, banks=[3])
+    ts(ap(big), T.kds[:, me::N], 64.0, None, ALU.is_ge, None, ["kds"], [big], q, 0.5)
+    mm(group(ps[7][:], [(ap(I), T.nzs[:, q:2 * q]), (ap(dm64), T.kds[:, me::N]), (ap(d4096), ap(big))], q),
+       ["nzs", "kds", big, I, dm64, d4096], 7)
+    ts(F[:, f0 + FW:f0 + FW + q], ps[7][:], 1984.0, None, ALU.add, None, (), ["F1_%d" % me], q, banks=[7])
+
+    out_e = topo.engines(core, cores[far[0]])
+    all_e = topo.engines(core, cores[mate])
+    in_e = [e for e in all_e if e not in out_e]
+    sent, gorder = [0], []
+
+    def piece(kind, h, r):
+        if kind == "f":
+            return F[:, (2 * r + h) * FW:(2 * r + h + 1) * FW]
+        return R[:, r * D + h * (RAW // 2):r * D + (h + 1) * (RAW // 2)]
+
+    def send(items, rd, cost):
+        def fn():
+            tr = []
+            for kind, h, r, to, es in items:
+                rid, pid = topo.addr(cores[to], core)
+                tr.append(RemoteDMATransfer(dst_ids=[DstId(rid=rid, pnc=pid)], dma_engine_mask=sum(1 << e for e in es),
+                                            remote_sem=T.sem["%s%d_%d" % (kind, h, r)], src=piece(kind, h, r), dst=piece(kind, h, r)))
+            g.remote_dma_fused(tr, local_sem=T.sem.sent)
+            return None
+        sent[0] += sum(len(it[4]) for it in items)
+        i = op("g", fn, rd, (), cost=cost, sem="none", after=gorder[-1:])
+        gorder.append(i)
+        return i
+
+    def arrive(kind, h, r, n, after, lat):
+        name = ("F%d_%d" if kind == "f" else "Rraw%d_%d") % (h, r)
+        return op(None, None, (), [name], cost=0.0, lat=lat, sem=("%s%d_%d" % (kind, h, r), n), after=[after])
+
+    ho, hi_, ha = len(out_e) // 2, len(in_e) // 2, len(all_e) // 2
+    sr = send([("r", 0, me, far[0], out_e[:ho]), ("r", 1, me, far[1], out_e[ho:]), ("r", 0, me, mate, in_e[:hi_]),
+               ("r", 1, me, mate, in_e[hi_:])], ["Rraw0_%d" % me], 1500)
+    sf = [send([("f", h, me, far[h], out_e), ("f", h, me, mate, in_e)], ["F%d_%d" % (h, me), "F%dt" % h], 600) for h in range(2)]
+    for h in range(2):
+        arrive("r", h, mate, hi_, sr, 2500)
+        arrive("r", h, far[h], ho, sr, 3500)
+        arrive("f", h, mate, len(in_e), sf[h], 2200)
+        arrive("f", h, far[h], len(out_e), sf[h], 3200)
+    for h in range(2):
+        fw = send([("f", h, far[h], mate, all_e)], ["F%d_%d" % (h, far[h])], 600)
+        arrive("f", h, far[1 - h], len(all_e), fw, 2000)
+    fw = send([("r", 0, far[0], mate, all_e[:ha]), ("r", 1, far[1], mate, all_e[ha:])], ["Rraw0_%d" % far[0], "Rraw1_%d" % far[1]], 600)
+    for h in range(2):
+        arrive("r", h, far[1 - h], ha, fw, 2000)
+
+    def unpack(h, r, b):
+        tab, name = (T.W2, "W2_%d" % r) if h == 0 else (T.KK, "KK_%d" % r)
+        src = F[:, (2 * r + h) * FW:(2 * r + h) * FW + q]
+        ts(tab[:, r::N], src, 1 / 64, 192 - 31.5 / 64, ALU.mult, ALU.add, ["F%d_%d" % (h, r)], [name], q, 0.5)
+        if r != me:
+            mm(group(ps[b][:], [(ap(Ih), src), (ap(dm64), tab[:, r::N])], q), ["F%d_%d" % (h, r), name, Ih, dm64], b)
+            act(T.N2[:, r * H + h * q:r * H + (h + 1) * q], ps[b][:], 12256.0, (), ["N2_%d_%d" % (h, r)], q, banks=[b])
+
+    def unpack_rooms(r, b):
+        hh = new("ph", 2 * TRI)
+        x = [F[:, (2 * r + h) * FW + q:(2 * r + h + 1) * FW] for h in range(2)]
+        for h in range(2):
+            ts(ap(hh, h * TRI, (h + 1) * TRI), x[h], 1 / 16, 1408 - 7.5 / 16, ALU.mult, ALU.add, ["F%d_%d" % (h, r)], [hh], TRI, 0.5)
+        e16, e256, em16 = diag(16, "ph"), diag(-256, "ph"), diag(-16, "ph")
+        mm(group(ps[b][:, 0:2 * TRI], [(ap(Ih), ap(hh))], 2 * TRI)
+           + group(ps[b][:, 2 * TRI:3 * TRI], [(ap(e16), x[0]), (ap(e256), ap(hh, 0, TRI)), (ap(Ih), x[1]),
+                                               (ap(em16), ap(hh, TRI, 2 * TRI))], TRI),
+           [hh, "F0_%d" % r, "F1_%d" % r, Ih, e16, e256, em16], b)
+        a = r * D + RAW
+        act(R[:, a:a + 2 * TRI], ps[b][:, 0:2 * TRI], -1280.0, (), ["Rt%d" % r], 2 * TRI, banks=[b])
+        act(R[:, a + 2 * TRI:a + 3 * TRI], ps[b][:, 2 * TRI:3 * TRI], 17.0 * 22528, (), ["Ru%d" % r], TRI, banks=[b])
+
+    zero = diag(0, "pb")
+    e4096, d131 = diag(4096, "ph"), diag(131072, "pb")
+    rot1, rotm, rotc, dm2047 = diag(1, "ph", 240), diag(-16, "ph", 240), diag(2047, "ph", 240), diag(-2047, "ph")
+
+    def draw(c, lb, lh, wtab, ktab, ntab, bias, rw, rk, rn):
+        b0, subs = CH[c]
+        lead[0] = OPT["lead"][c]
+        cuts = [[(0, sum(subs), (0, 1))], [(0, subs[0], (0,)), (subs[0], sum(subs), (1,))]]
+        for buf, nm, tab, rd_, k in ((T.Wg, "Wg", wtab, rw, 0), (T.Kg, "Kg", ktab, rk, 1)):
+            for x0, x1, us in cuts[OPT["split"][k]]:
+                act(buf[:, 128 * (b0 + x0):128 * (b0 + x1)], tab.indirect(ap(lb[0], lb[1] + 8 * x0, lb[1] + 8 * x1)), bias, rd_ + [lb[0]],
+                    ["%s_%d_%d" % (nm, c, u) for u in us], 128 * (x1 - x0), gather=True)
+        for x0, x1, us in cuts[OPT["split"][2]]:
+            a, e = 128 * (b0 + x0), 128 * (b0 + x1)
+            tt(T.A[:, a:e], ntab.indirect(ap(lh[0], lh[1] + 8 * x0, lh[1] + 8 * x1)), T.Wg[:, a:e], ALU.mult,
+               rn + [lh[0]] + ["Wg_%d_%d" % (c, u) for u in us], ["A_%d_%d" % (c, u) for u in us], e - a, gather=True)
+        s0 = 0
+        for u, nb in enumerate(subs):
+            a, n = 128 * (b0 + s0), 128 * nb
+            tk = "_%d_%d" % (c, u)
+            bk = 4 * c + u
+            m_ = mm([(ps[bk][:, 0:n], ap(zero), T.nzs[:, 0:n], True, False, n)], [zero, "nzs"], bk)
+            for buf, nm, mat in ((T.Wg, "Wg", d131), (T.Kg, "Kg", I), (T.A, "A", e4096)):
+                m_ = mm([(ps[bk][:, 128 * m:128 * (m + 1)], buf[:, a + 128 * m:a + 128 * (m + 1)], ap(mat), False,
+                          nm == "A" and m == nb - 1, 128) for m in range(nb)], [nm + tk, mat], bk, [m_])
+            scan(T.Z[:, a:a + n], ap(pat, 0, n), ps[bk][:, 0:n], ALU.add, ALU.max, [pat], ["Z" + tk], n, banks=[bk])
+            s0 += nb
+        zs = ["Z_%d_%d" % (c, u) for u in range(len(subs))]
+        win = T.Z[:, 128 * b0:128 * (b0 + s0)]
+        hn, low = new("pf", wp), new("ph", wp)
+        ts(ap(hn), win.indirect(ap(lext, 0, 3)), BIG, -BIG, ALU.add, ALU.add, zs + [lext], [hn], wp, gather=True)
+        tt(ap(low), win.indirect(ap(lext, 0, 3)), ap(hn), ALU.subtract, zs + [lext, hn], [low], wp, gather=True)
+        return low
+
+    def turn(out, mat, x, start, stop):
+        return [(out[:, r:w:8], ap(mat, 16 * r, 16 * r + 128), ap(x, r, w, 8), start, stop if start else (stop and r == 7), 5)
+                for r in range(8)]
+
+    def parts(v):
+        top = 1 << (abs(v).bit_length() - 1)
+        return [v] if abs(v) < 256 or v % 4 == 0 and abs(v) < 1024 else [top, v - top]
+
+    st = [{"g2": [], "k": []} for _ in CH]
+    W2r, KKr = ["W2_%d" % r for r in range(N)], ["KK_%d" % r for r in range(N)]
+    N2r = ["N2_%d_%d" % (h, r) for h in range(2) for r in range(N)]
+    Rr = (["Rraw%d_%d" % (h, r) for h in range(2) for r in range(N)] + ["Rt%d" % r for r in range(N)]
+          + ["Ru%d" % r for r in range(N) if r != me])
+    unpack(0, me, 3)
+    unpack(1, me, 7)
+    for rnd in range(3):
+        own = new("pb", W)
+        ownt = [own[3] + "_%d" % c for c in range(2)]
+        l2 = []
+        for c, (b0, subs) in enumerate(CH):
+            k0, s0, s1 = 8 * b0, 4 * c + 2, 4 * c + 3
+            low = draw(c, (lists[c], 0), (lists[c], w), T.wts[:], T.kds[:], mine if rnd == 0 else T.N1[:], 0.0,
+                       ["wts"], ["kds"], ["N2_0_%d" % me] if rnd == 0 else ["N1_0", "N1_1"])
+            mm(turn(ps[s0], rot1, low, True, True), [low, rot1], s0)
+            y, b1, ow, z, hr, hm, ix = [new("pi", w) for _ in range(7)]
+            lb, lh = new("pu", wp), new("pu", wp)
+            ts(ap(y), ps[s0][:, 0:w], 2047 / 128, 15 + 63.5 / 128, ALU.mult, ALU.add, (), [y], w, banks=[s0])
+            ts(ap(b1), ap(y), B - 1, None, ALU.bitwise_and, None, [y], [b1], w)
+            cp(ap(lb), ap(b1).indirect(ap(lperm, 0, 3)), [b1, lperm], [lb], wp, gather=True)
+            ts(ap(z), ap(y), float(K2), None, ALU.mult, None, [y], [z], w)
+            if rnd == 0:
+                tt(ap(hr), ap(z), ap(sal, k0, k0 + w), ALU.add, [z, sal], [hr], w)
+            else:
+                tt(ap(hr), ap(z), ps[s1][:, 64:64 + w], ALU.add, [z], [hr], w, 1.0, banks=[s1])
+            ts(ap(hm), ap(hr), H - 1, None, ALU.bitwise_and, None, [hr], [hm], w)
+            ts(ap(ow), ap(y), N - 1, None, ALU.bitwise_and, None, [y], [ow], w)
+            ts(ap(own, k0, k0 + w), ap(ow), 1024.0, 1024.0, ALU.mult, ALU.add, [ow], [ownt[c]], w)
+            tt(ap(ix), ap(hm), ap(own, k0, k0 + w), ALU.add, [hm, ownt[c]], [ix], w)
+            ts(ap(lh), ap(ix).indirect(ap(lperm, 0, 3)), -1024.0, None, ALU.add, None, [ix, lperm], [lh], wp, gather=True)
+            l2.append((lb, lh))
+        lead[0] = OPT["lead"][2]
+        if rnd == 0:
+            for n_, (h, r) in enumerate([(0, mate), (0, far[0]), (1, mate), (1, far[1]), (0, far[1]), (1, far[0])]):
+                unpack(h, r, (3, 7)[n_ % 2])
+            for n_, r in enumerate([mate, far[0], far[1]]):
+                unpack_rooms(r, (3, 7)[n_ % 2])
+        src, srct = own, ownt
+        if rnd == 2:
+            src = new("pb", W)
+            for c, (b0, subs) in enumerate(CH):
+                k0 = 8 * b0
+                tt(ap(src, k0, k0 + w), ap(own, k0, k0 + w), ap(st[c]["takes"]), ALU.mult, [ownt[c], st[c]["takes"]], [src[3] + "_%d" % c], w)
+            srct = [src[3] + "_%d" % c for c in range(2)]
+        sg, g2 = new("pb", N * W), new("pb", W)
+        j0 = 0 if rnd == 2 else 1
+        for j in range(j0, N):
+            act(ap(sgn, j * W, (j + 1) * W), ap(src), -1024.0 * j - 512, srct, ["sgn%d" % j], W, func=AF.Sign)
+        mt = ["sgn%d" % j for j in range(N + 1)]
+        scan(ap(run, j0 * W, N * W), ap(rst, 0, (N - j0) * W), ap(sgn, j0 * W, N * W), ALU.mult, ALU.add, mt[j0:N] + [rst],
+             ["run%d" % j for j in range(j0, N)], (N - j0) * W, 0.5)
+        mm(group(ps[7][:, 128:128 + N * W], [(ap(tri), ap(sgn, 0, N * W)), (ap(ntri), ap(sgn, W, (N + 1) * W)),
+                                             (ap(blk), ap(run, 0, N * W)), (ap(nblk), ap(run, W, (N + 1) * W))], N * W),
+           mt + ["run%d" % j for j in range(N + 1)] + [blk, tri, nblk, ntri], 7)
+        act(ap(sg), ps[7][:, 128:128 + N * W], 1.0 - 2 * CAP, (), [sg], N * W, banks=[7], func=AF.Sign, scale=-1.0)
+        mm(group(ps[7][:, 0:W], [(ap(I), ap(sg, r * W, (r + 1) * W)) for r in range(N)], W), [sg, I], 7)
+        act(ap(g2), ps[7][:, 0:W], 4.0, (), [g2], W, banks=[7])
+        for c, (b0, subs) in enumerate(CH):
+            k0, s0, s1 = 8 * b0, 4 * c + 2, 4 * c + 3
+            S = st[c]
+            low = draw(c, (l2[c][0], 0), (l2[c][1], 0), T.W2[:], T.KK[:], T.N2[:], -160.0, W2r, KKr, N2r)
+            cq, lr = new("ph", wp), new("pu", w)
+            ts(ap(cq), ap(low), 1 / 128, 1536.0, ALU.mult, ALU.add, [low], [cq], wp, 0.5)
+            dv = ps[s0][:, 0:w]
+            m0 = mm(group(dv, [(ap(I), ap(own, k0, k0 + w)), (ap(dm2047), ap(c1536))], w, True, False), [ownt[c], c1536, I, dm2047], s0)
+            m1 = mm(turn(ps[s0], rotm, low, False, False), [low, rotm], s0, [m0])
+            mm(turn(ps[s0], rotc, cq, False, True), [cq, rotc], s0, [m1])
+            ts(ap(lr), dv, -1.0, None, ALU.add, None, (), [lr], w, banks=[s0])
+            extra = [(ap(I), ap(g2, k0, k0 + w))]
+            erd = [g2, I]
+            if rnd > 0:
+                ne = new("pb", w)
+                tt(ap(ne), dv, ap(S["one"]), ALU.not_equal, [S["one"]], [ne], w, 1.0, banks=[s0])
+                extra.append((ap(I), ap(ne)))
+                erd.append(ne)
+            if rnd == 2:
+                du, dw = new("pf", w), new("pf", w)
+                tt(ap(du), dv, ap(S["has"]), ALU.mult, [S["has"]], [du], w, 1.0, banks=[s0])
+                tt(ap(dw), dv, ap(du), ALU.subtract, [du], [dw], w, 1.0, banks=[s0])
+            S["g2"].append(g2)
+            lraw = ps[s0][:, 64:64 + 2 * w]
+
+            def steps(out, coef, last):
+                tm, rd = [], []
+                for x in S["g2"]:
+                    for v in parts(coef):
+                        tm.append((out, ap(diag(v, "pb")), ap(x, k0, k0 + w), False, False, w))
+                        rd += [diag(v, "pb"), x]
+                for x in S["k"][:last]:
+                    tm.append((out, ap(diag(-coef, "ph")), ap(x), False, False, w))
+                    rd += [diag(-coef, "ph"), x]
+                return tm, rd
+            if rnd < 2:
+                ta_, ra_ = steps(ps[s0][:, 64:64 + w], K5, rnd)
+                tb_, rb_ = steps(ps[s0][:, 64 + w:64 + 2 * w], KH, rnd)
+                pre = mm([(lraw, ap(Ih), ap(bsh[c]), True, False, 2 * w)] + ta_ + tb_, ra_ + rb_ + [bsh[c], Ih], s0)
+            a, n = 128 * b0, 16 * w
+            tt(T.Ft[:, a:a + n], R[:].indirect(ap(lr)), T.nds[:, a:a + n], ALU.is_ge, Rr + [lr, "nds"], ["Ft%d" % c], n, gather=True)
+            m0 = mm(group(ps[s1][:, 0:w], extra, w, True, False), erd, s1)
+            mm(group(ps[s1][:, 0:w], [(ap(pick, 15 - i, 143 - i), T.Ft[:, a + i:a + n:16]) for i in range(16)], w, False, True),
+               ["Ft%d" % c, pick], s1, [m0])
+            k = new("ph", w)
+            ts(ap(k), ps[s1][:, 0:w], 17.5 if rnd == 0 else 18.5, None, ALU.is_ge, None, (), [k], w, banks=[s1])
+            S["k"].append(k)
+            if rnd < 2:
+                mm([(ps[s0][:, 64:64 + w], ap(diag(-K5, "ph")), ap(k), False, False, w),
+                    (ps[s0][:, 64 + w:64 + 2 * w], ap(diag(-KH, "ph")), ap(k), False, True, w)],
+                   [k, diag(-K5, "ph"), diag(-KH, "ph")], s0, [pre])
+                li, lm, l1 = new("pi", 2 * w), new("pi", 2 * w), new("pu", 2 * w)
+                cp(ap(li), lraw, (), [li], 2 * w, banks=[s0])
+                ts(ap(lm), ap(li), B - 1, None, ALU.bitwise_and, None, [li], [lm], 2 * w)
+                cp(ap(l1), ap(lm).indirect(ap(lperm2, 0, 5)), [lm, lperm2], [l1], 2 * w, gather=True)
+                lists[c] = l1
+                tm, rd = steps(ps[s1][:, 64:64 + w], K3, rnd + 1)
+                tm[-1] = tm[-1][:4] + (True, w)
+                mm([(ps[s1][:, 64:64 + w], ap(Ih), ap(salh, k0, k0 + w), True, False, w)] + tm, rd + [salh, Ih], s1)
+                x = new("pf", w)
+                tt(ap(x), dv, ap(k), ALU.mult, [k], [x], w, 1.0, banks=[s0])
+            if rnd == 0:
+                S["one"] = x
+            elif rnd == 1:
+                two, sm, one, tk_, has, om, tm_ = new("pf", w), new("pf", w), new("pf", w), new("pb", w), new("pb", w), new("pf", w), new("pf", w)
+                tt(ap(two), ap(x), ap(S["k"][0]), ALU.mult, [x, S["k"][0]], [two], w)
+                tt(ap(sm), ap(x), ap(S["one"]), ALU.add, [x, S["one"]], [sm], w)
+                tt(ap(one), ap(sm), ap(two), ALU.subtract, [sm, two], [one], w)
+                ts(ap(tk_), ap(two), 0.0, None, ALU.is_equal, None, [two], [tk_], w)
+                act(ap(has), ap(one), 0.0, [one], [has], w, func=AF.Sign)
+                act(ap(om), ap(one), -1.0, [one], [om], w)
+                act(ap(tm_), ap(two), -1.0, [two], [tm_], w)
+                S.update({"one": one, "takes": tk_, "has": has, "om": om, "tm": tm_})
+            else:
+                for n_, (dd, old, out) in enumerate([(dw, S["om"], T.ya), (du, S["tm"], T.yb)]):
+                    u, y = new("pf", w), new("pf", w)
+                    tt(ap(u), ap(dd), ap(k), ALU.mult, [dd, k], [u], w)
+                    tt(ap(y), ap(u), ap(old), ALU.add, [u, old], [y], w)
+                    dma("sa"[n_], out[:, k0:k0 + w], ap(y), [y], ["out%d%d" % (c, n_)], 2000)
+
+    n = len(ops)
+    order = list(ORDER)
+    if len(order) != n:
+        succ = [[] for _ in ops]
+        for i, o_ in enumerate(ops):
+            o_["all"] = o_["deps"] | o_["after"]
+            o_["wait"] = o_["lat"] * (OPT["xl"] if o_["e"] is None else 1.0)
+            for d_ in o_["all"]:
+                succ[d_].append(i)
+        prio = [0.0] * n
+        for i in range(n - 1, -1, -1):
+            prio[i] = ops[i]["cost"] + ops[i]["wait"] + max([prio[s] + LAT for s in succ[i]] + [0.0])
+        for i in range(n):
+            prio[i] += ops[i]["lead"]
+        left = [len(o_["all"]) for o_ in ops]
+        ready = [i for i in range(n) if left[i] == 0]
+        free = {e: 0.0 for e in queue}
+        rdy, order = [0.0] * n, []
+        while ready:
+            est = {i: max(rdy[i], free.get(ops[i]["e"], 0.0)) for i in ready}
+            i0 = min(ready, key=lambda i: (est[i], i))
+            near = [i for i in ready if ops[i]["e"] == ops[i0]["e"] and est[i] <= est[i0] + OPT["win"]]
+            i = max(near, key=lambda i: (prio[i], -i)) if ops[i0]["e"] in ("v", "a", "p") else min(near)
+            o_ = ops[i]
+            if o_["e"] is not None:
+                free[o_["e"]] = est[i] + o_["cost"]
+            order.append(i)
+            ready.remove(i)
+            for s in succ[i]:
+                rdy[s] = max(rdy[s], est[i] + o_["cost"] + o_["wait"] + (LAT if i in ops[s]["deps"] else 0.0))
+                left[s] -= 1
+                if left[s] == 0:
+                    ready.append(s)
+    PLAN[me] = [(ops[i]["e"], ops[i]["c4"], ops[i]["lat"], ops[i]["deps"], ops[i]["after"], i) for i in order]
+
+    count = {e: 0 for e in queue}
+    known = {e: {} for e in queue}
+    mark, total = {}, {}
+    needed = set()
+    for o_ in ops:
+        needed |= o_["deps"]
+    place = {i: n_ for n_, i in enumerate(order)}
+    for i in order:
+        o_ = ops[i]
+        e = o_["e"]
+        if e is not None:
+            want = {}
+            for d_ in o_["deps"]:
+                s, v, _k = mark[d_]
+                if v > want.get(s, (0, None))[0]:
+                    want[s] = (v, d_)
+            for s, (v, d_) in sorted(want.items(), key=lambda x: -place[x[1][1]]):
+                if known[e].get(s, 0) < v:
+                    queue[e].wait_ge(T.sem[s], v)
+                    known[e][s] = v
+                    for s2, v2 in mark[d_][2].items():
+                        known[e][s2] = max(known[e].get(s2, 0), v2)
+            inst = o_["fn"]()
+        if o_["sem"] == "none":
+            continue
+        if o_["sem"] is not None:
+            s, v = o_["sem"]
+            if e is not None:
+                inst.then_inc(T.sem[s], v)
+        else:
+            if i not in needed:
+                continue
+            count[e] += 1
+            s, v = "c" + e, count[e]
+            inst.then_inc(T.sem[s], 1)
+        mark[i] = (s, v, dict(known[e]) if e is not None else {})
+        total[s] = v
+    total["sent"] = sent[0]
+    for s, v in total.items():
+        g.wait_ge(T.sem[s], v)

@@ -3,49 +3,160 @@ from concourse.mybir import AluOpType as ALU, ActivationFunctionType as AF
 
 N, B, H, D, O, CAP = 4, 2048, 1024, 1024, 1280, 256
 K2, K3, K5 = 37, 611, 1237
-KH = (K3 + K2 * K5) % H
+MU = pow(K2, -1, H)
+KT = K3 * MU % H
+KH = (KT + K5) % H
 W = O // 16
 TRI = 88
 RAW = D - 3 * TRI
 FW = B // N + TRI
-CH = [(0, (3, 2)), (5, (3, 2))]
 BIG = 1.5 * 2.0 ** 35
+GAP = 4096
+ALPHA = 4095 / 256
+OFF = 8192.0
 
 SCRATCH = {
-    "wts": ("sbuf", [128, B], "bfloat16"), "kds": ("sbuf", [128, B], "bfloat16"), "nzs": ("sbuf", [128, H], "bfloat16"),
-    "nds": ("sbuf", [128, O], "bfloat16"), "R": ("sbuf", [128, N * D], "bfloat16"), "F": ("sbuf", [128, N * 2 * FW], "float16"),
-    "W2": ("sbuf", [128, B], "bfloat16"), "KK": ("sbuf", [128, B], "bfloat16"), "N2": ("sbuf", [128, N * H], "bfloat16"),
-    "N1": ("sbuf", [128, 2 * H], "bfloat16"), "Wg": ("sbuf", [128, O], "bfloat16"), "Kg": ("sbuf", [128, O], "bfloat16"),
+    "NB": ("sbuf", [128, (N - 1) * GAP + H], "bfloat16"), "R": ("sbuf", [128, N * D], "bfloat16"),
+    "F": ("sbuf", [128, N * 2 * FW], "float16"), "WK": ("sbuf", [128, 2 * B], "bfloat16"),
+    "N1": ("sbuf", [128, B + 336], "bfloat16"), "Wg": ("sbuf", [128, O], "bfloat16"), "Kg": ("sbuf", [128, O], "float16"),
     "A": ("sbuf", [128, O], "float16"), "Z": ("sbuf", [128, O], "float32"), "Ft": ("sbuf", [128, O], "bfloat16"),
-    "pi": ("sbuf", [128, 6144], "int32"), "pf": ("sbuf", [128, 6144], "float32"), "pb": ("sbuf", [128, 10240], "bfloat16"),
-    "ph": ("sbuf", [128, 8192], "float16"), "pu": ("sbuf", [128, 2048], "uint16"),
+    "Z9": ("sbuf", [128, 720], "float32"), "Rl": ("sbuf", [128, 720], "float32"),
+    "pi": ("sbuf", [128, 6144], "int32"), "pf": ("sbuf", [128, 6144], "float32"), "pb": ("sbuf", [128, 12288], "bfloat16"),
+    "ph": ("sbuf", [128, 8192], "float16"), "pu": ("sbuf", [128, 4096], "uint16"),
 }
 for _b in range(8):
     SCRATCH["ps%d" % _b] = ("psum", [128, 512], "float32")
-SEMAPHORES = (["cv", "ca", "cp", "cg", "sent"] + ["d%d" % i for i in range(14)]
+SEMAPHORES = (["cv", "ca", "cp", "cg", "sent"] + ["d%d" % i for i in range(24)]
               + ["%s%d" % (a, r) for a in ("f0_", "f1_", "r0_", "r1_") for r in range(N)])
 
-OPT = {"cy": 1.0, "ga": 1.5, "pc": 0.55, "lat": 150.0, "xl": 1.5, "win": 30.0, "lead": [1000.0, 0.0, 0.0], "split": [1, 1, 1],
-       "jit": [0.0, 1], "relay": 1}
+OPT = {
+    "chunks": [(0, (3, 2), (0, 1), 2, 3), (5, (3, 2), (4, 5), 6, 7)],
+    "spare": (3, 7), "count": 7,
+    "pairs": [[0, 0], [0, 0], [0, 0]],
+    "split": [1, 1, 1],
+    "eng": {"lb": "v", "iv": "v", "lh": "v", "lr": "v", "li": "v", "l1": "v", "cq": "a", "f0": "v", "f1": "v", "mu": "a",
+            "own": "v", "carry": "v", "mod": "a", "k": "v", "n00": "a", "n01": "a", "n02": "a", "n10": "a", "n11": "a", "n12": "a"},
+    "loads": ["raw", "tri", "nz", "wt", "kd", "nd", "wx", "kx"],
+    "sends": ["r", "f0", "f1", "h0", "h1", "hr"],
+    "times": [(0.83, 1.35, 0.42, 215.0, 215.0, 1.0), (1.2, 1.9, 0.6, 200.0, 200.0, 1.2), (0.95, 1.5, 0.48, 170.0, 150.0, 1.0)],
+    "tries": 3000, "seed": 12345, "lead": 3000.0, "slack": 0.02, "mirror": 3,
+}
 PLAN = {}
-ORDER = [int(x) for x in """
-0 1 7 33 31 16 36 2 3 4 5 6 8 9 11 10 13 39 17 183 97 14 37 32 18 63 38 20 102 19 99 24 56 49 52 25 64 185 21 50 34 22 40 184 23 45 47
-35 53 26 57 27 65 66 70 71 48 29 72 100 58 54 30 60 28 67 73 74 75 46 101 103 41 68 96 230 134 138 69 76 77 135 106 105 110 42 12 109
-104 139 98 244 232 231 107 108 136 43 137 245 111 116 78 117 112 140 113 141 118 119 114 142 145 120 115 146 143 15 121 238 122 147
-148 144 149 218 123 213 255 260 124 150 130 151 127 152 81 82 85 86 61 62 79 83 84 80 87 163 181 239 166 169 131 189 88 128 125 172
-164 153 159 160 126 129 167 44 156 157 132 154 133 155 158 165 89 226 90 175 168 170 201 200 199 171 173 174 207 176 177 208 250 182
-186 187 188 91 92 178 179 180 210 209 249 251 252 59 246 55 214 268 161 162 51 194 190 195 202 93 94 95 219 261 212 211 254 196 191
-220 221 215 222 216 256 294 253 257 258 217 262 263 192 193 203 223 259 224 227 264 225 228 204 265 266 269 205 267 270 197 198 206
-289 235 318 229 234 236 274 323 233 271 273 237 240 275 272 241 248 242 243 276 277 247 283 285 284 281 278 279 282 287 280 290 291
-292 295 286 288 313 312 314 296 297 293 298 299 317 300 316 324 319 301 302 303 320 321 304 322 315 325 326 327 305 360 397 355 328
-306 329 308 307 330 309 368 402 349 350 351 352 310 331 311 334 332 337 335 333 353 354 336 338 356 357 361 358 359 362 363 394 392
-403 404 410 391 439 364 444 398 339 393 343 365 340 366 341 369 399 395 367 342 396 344 400 370 405 345 401 406 372 407 408 468 411
-371 409 346 347 412 374 348 413 414 473 375 376 417 373 416 377 378 418 379 383 380 384 381 419 385 415 390 433 434 435 436 420 387
-425 421 386 426 422 427 429 437 423 438 428 462 463 464 382 424 445 440 441 442 443 446 447 448 449 450 466 508 469 451 452 467 453
-458 455 454 459 456 470 471 472 457 474 465 475 476 477 460 491 478 461 479 389 513 388 430 431 432 502 503 504 505 509 549 521 480
-510 506 511 514 544 515 481 507 482 484 487 483 485 512 488 486 516 517 492 489 518 490 538 539 557 545 550 519 541 522 551 543 552
-540 495 494 496 493 542 520 553 497 546 547 548 523 526 554 524 555 525 556 528 498 558 499 559 500 560 561 564 562 501 527 565 529
-530 563 531 532 535 566 533 567 536 571 568 572 569 534 537 570 573""".split()]
+
+
+def make_order(ops, opt):
+    n = len(ops)
+    pre = [sorted(o["deps"] | o["after"]) for o in ops]
+    succ = [[] for _ in ops]
+    for i in range(n):
+        for d in pre[i]:
+            succ[d].append(i)
+    sets = []
+    for cy, ga, pc, hop, same, xl in opt["times"]:
+        cost = [o["c4"][0] + cy * (o["c4"][1] + ga * o["c4"][2]) + pc * o["c4"][3] for o in ops]
+        lat = [o["lat"] * (xl if o["e"] is None else 1.0) for o in ops]
+        gap = [[(-lat[d] if d not in ops[i]["deps"] else same if ops[d]["e"] == ops[i]["e"] and ops[d]["sem"] is None
+                 else hop) for d in pre[i]] for i in range(n)]
+        sets.append((cost, lat, gap))
+    eng = [o["e"] for o in ops]
+
+    def replay(order, s):
+        cost, lat, gap = sets[s]
+        end, free = [0.0] * n, {}
+        for i in order:
+            t = free.get(eng[i], 0.0)
+            for d, x in zip(pre[i], gap[i]):
+                if end[d] + x > t:
+                    t = end[d] + x
+            if eng[i] is not None:
+                free[eng[i]] = t + cost[i]
+            end[i] = t + cost[i] + lat[i]
+        return max(end), end
+
+    def place(seq, s, back):
+        cost, lat, gap = sets[s]
+        start, end, busy = [0.0] * n, [0.0] * n, {}
+        for i in seq:
+            t = 0.0
+            if back:
+                for j, x in after_[s][i]:
+                    if end[j] + x > t:
+                        t = end[j] + x
+                t += lat[i]
+            else:
+                for d, x in zip(pre[i], gap[i]):
+                    if end[d] + x > t:
+                        t = end[d] + x
+            if eng[i] is not None:
+                l = busy.setdefault(eng[i], [])
+                k = len(l)
+                while k > 0 and l[k - 1][1] > t:
+                    k -= 1
+                while k < len(l) and l[k][0] < t + cost[i]:
+                    t = max(t, l[k][1])
+                    k += 1
+                l.insert(k, (t, t + cost[i]))
+            start[i] = t
+            end[i] = t + cost[i] + (0.0 if back else lat[i])
+        return start, end
+
+    def sort(key, back):
+        need, nxt = (succ, pre) if back else (pre, succ)
+        left = [len(x) for x in need]
+        ready, seq = [i for i in range(n) if not left[i]], []
+        while ready:
+            i = min(ready, key=lambda j: (key[j], j))
+            ready.remove(i)
+            seq.append(i)
+            for j in nxt[i]:
+                left[j] -= 1
+                if not left[j]:
+                    ready.append(j)
+        return seq
+
+    after_ = []
+    for cost, lat, gap in sets:
+        x = [[] for _ in ops]
+        for i in range(n):
+            for d, y in zip(pre[i], gap[i]):
+                x[d].append((i, y))
+        after_.append(x)
+    cost, lat, gap = sets[0]
+    tail = [0.0] * n
+    for i in range(n - 1, -1, -1):
+        tail[i] = cost[i] + lat[i] + max([tail[j] + x for j, x in after_[0][i]] + [0.0])
+    PLAN["tail"] = tail
+    seed, best, ref, cur = [opt["seed"]], None, None, None
+
+    def rnd():
+        seed[0] = (seed[0] * 1103515245 + 12345) % 2 ** 31
+        return seed[0] / 2 ** 31
+
+    key = [-tail[i] - opt["lead"] * ops[i]["lead"] for i in range(n)]
+    for k in range(opt["tries"]):
+        s = k % len(sets)
+        start, end = place(sort(key, False), s, False)
+        for again in range(2):
+            order = sort(start, False)
+            ts_ = [replay(order, y)[0] for y in range(len(sets))]
+            ref = ref or ts_
+            score = sum(a / b for a, b in zip(ts_, ref))
+            if best is None or score < best[0]:
+                best = (score, order, ts_, start)
+            if cur is None or score < cur[0] + opt["slack"] * (1.0 - k / opt["tries"]) * rnd():
+                cur = (score, start)
+            if again or k % opt["mirror"]:
+                break
+            bs, be = place(sort([-x for x in end], True), s, True)
+            start, end = place(sort([-x for x in be], False), s, False)
+        size, span = 2500.0 * rnd() ** 3 + 50.0, 12000.0 * rnd()
+        lo = rnd() * max(cur[1]) - span / 2
+        shift, who = size * (2 * rnd() - 1), float(k % 2)
+        if k % 3:
+            key = [x + (size * rnd() if lo <= x <= lo + span else 0.0) for x in cur[1]]
+        else:
+            key = [x + (shift if lo <= x <= lo + span and o["lead"] == who else 0.0) for x, o in zip(cur[1], ops)]
+    return best[1], best[2]
 
 
 def rank_program(g, core, T, topo):
@@ -57,10 +168,11 @@ def rank_program(g, core, T, topo):
     far = [r for r in range(N) if r != me and r != mate]
     far.sort(key=lambda r: topo.die(cores[r]) != topo.die(core))
     queue = {"v": g.vector, "a": g.scalar, "p": g.tensor, "s": g.sync, "g": g}
-    ops, lastw, readers, bank = [], {}, {}, {}
+    ops, lastw, readers, bank, lastp = [], {}, {}, {}, {}
     used = {"pi": 0, "pf": 0, "pb": 0, "ph": 0, "pu": 0}
     ndma, tok, lead = [0], [0], [0.0]
-    LAT = OPT["lat"]
+    PLAN["ops"] = ops
+    CH, ENG = OPT["chunks"], OPT["eng"]
 
     def new(pool, n):
         a = used[pool]
@@ -72,7 +184,7 @@ def rank_program(g, core, T, topo):
         b = x[2] if b is None else b
         return x[0][:, x[1] + a:x[1] + b:s] if s != 1 else x[0][:, x[1] + a:x[1] + b]
 
-    def op(eng, fn, rd=(), wr=(), banks=(), cost=55.0, lat=0.0, sem=None, after=()):
+    def op(eng, fn, rd=(), wr=(), banks=(), cost=(55.0, 0, 0, 0), lat=0.0, sem=None, after=()):
         i = len(ops)
         deps = set()
         for t in rd:
@@ -94,9 +206,7 @@ def rank_program(g, core, T, topo):
             deps.update(prev)
             bank[b] = (e, cur + [i], prev)
         deps.discard(i)
-        c4 = cost if isinstance(cost, tuple) else (cost, 0, 0, 0)
-        ops.append({"e": eng, "fn": fn, "deps": deps, "c4": c4, "lat": lat, "sem": sem, "after": set(after), "lead": lead[0],
-                    "cost": c4[0] + OPT["cy"] * (c4[1] + OPT["ga"] * c4[2]) + OPT["pc"] * c4[3]})
+        ops.append({"e": eng, "fn": fn, "deps": deps, "c4": cost, "lat": lat, "sem": sem, "after": set(after), "lead": lead[0], "tag": (tuple(wr), tuple(banks))})
         return i
 
     def vc(n, c=1.0, f=0.0):
@@ -128,138 +238,218 @@ def rank_program(g, core, T, topo):
         return op("a", lambda: g.scalar.activation(out, in_, func, bias=bias, scale=scale), rd, wr, banks,
                   gc_(n, 65.0) if gather else vc(n, 1.0, 30.0))
 
-    def mm(terms, rd, b, after=()):
+    def lin(name, out, in_, mul, add, rd, wr, n, c=1.0, banks=(), gather=False):
+        if ENG[name] == "a":
+            return act(out, in_, float(add), rd, wr, n, banks, gather, scale=float(mul))
+        return ts(out, in_, float(mul), float(add), ALU.mult, ALU.add, rd, wr, n, c, banks, gather)
+
+    def mm(terms, rd, b):
         def fn():
             for (o_, l_, r_, st, sp, n) in terms:
                 last = g.tensor.matmul(o_, l_, r_, st, sp)
             return last
-        return op("p", fn, rd, (), [b], (40.0, 0, 0, sum(max(64, t[5]) for t in terms)), after=after)
+        i = op("p", fn, rd, (), [b], (30.0, 0, 0, sum(max(64, t[5]) for t in terms)), after=[lastp[b]] if b in lastp else [])
+        lastp[b] = i
+        return i
 
     def group(out, pairs, n, start=True, stop=True):
         return [(out, l_, r_, start and i == 0, stop and i == len(pairs) - 1, n) for i, (l_, r_) in enumerate(pairs)]
 
-    def dma(eng, out, in_, rd, wr, lat):
+    def dma(eng, out, in_, rd, wr, lat, after=()):
         s = "d%d" % ndma[0]
         ndma[0] += 1
-        return op(eng, lambda: queue[eng].dma_start(out, in_), rd, wr, (), 60.0, lat, (s, 16))
+        return op(eng, lambda: queue[eng].dma_start(out, in_), rd, wr, (), (60.0, 0, 0, 0), lat, (s, 16), after)
 
     ps = [T["ps%d" % b] for b in range(8)]
     R, F = T.R, T.F
+    q = B // N
+    f0 = me * 2 * FW
+    rt = me * D + RAW
 
     beg, sal = new("pi", W), new("pi", W)
-    dma("s", R[:, me * D:(me + 1) * D], T.room[:], (), ["Rraw0_%d" % me, "Rraw1_%d" % me, "Rt%d" % me], 2600)
-    dma("a", ap(beg), T.begin[:], (), [beg], 2200)
+    wts, kds = (T.NB, H, GAP - H, "wts"), (T.NB, GAP + H, GAP - H, "kds")
+    nzs, nds = (T.NB, 2 * GAP + H, H, "nzs"), (T.NB, 2 * GAP + 2 * H, O, "nds")
+    fill(T.NB[:, 2 * GAP + 2 * H + O:3 * GAP], 0.0, ["rest"], (GAP - 2 * H - O) // 2)
+    loads = {"tri": (R[:, rt:rt + 3 * TRI], T.room[:, RAW:D], ["Rt%d" % me], 3 * TRI),
+             "raw": (R[:, me * D:rt], T.room[:, 0:RAW], ["Rraw0_%d" % me, "Rraw1_%d" % me], RAW),
+             "nz": (ap(nzs), T.noise[:], [nzs], H), "wt": (ap(wts, 0, B), T.wt[:], [wts], B), "kd": (ap(kds, 0, B), T.kid[:], [kds], B),
+             "nd": (ap(nds), T.need[:], [nds], O), "wx": (ap(wts, B, B + H), T.wt[:, 0:H], ["wx"], H),
+             "kx": (ap(kds, B, B + H), T.kid[:, 0:H], ["kx"], H)}
+    dma("a", ap(beg), T.begin[:], (), [beg], 2100)
     dma("a", ap(sal), T.salt[:], (), [sal], 2200)
-    dma("s", T.nzs[:], T.noise[:], (), ["nzs"], 3300)
-    dma("s", T.wts[:], T.wt[:], (), ["wts"], 4700)
-    dma("s", T.kds[:], T.kid[:], (), ["kds"], 6100)
-    dma("s", T.nds[:], T.need[:], (), ["nds"], 7000)
+    due, prev = 2100.0, []
+    for name in OPT["loads"]:
+        o_, i_, wr, n = loads[name]
+        due += 0.69 * n - 60
+        prev = [dma("s", o_, i_, (), wr, due, prev)]
 
-    col, prt = new("pi", 144), new("pi", 8)
-    op("g", lambda: g.iota(ap(col), [[1, 144]], 0, 0), (), [col], cost=400)
-    op("g", lambda: g.iota(ap(prt), [[0, 8]], 0, 1), (), [prt], cost=150)
-    pcol, gcol = new("pf", 1), new("pf", 1)
+    col, prt, mui, pu_ = new("pi", 144), new("pi", 8), new("pi", 64), new("pi", 72)
+    op("g", lambda: g.iota(ap(mui), [[16 * K2, 64]], 0, K2), (), [mui], cost=(250.0, 0, 0, 0))
+    op("g", lambda: g.iota(ap(prt), [[0, 8]], 0, 1), (), [prt], cost=(150.0, 0, 0, 0))
+    op("g", lambda: g.iota(ap(col), [[1, 144]], 0, 0), (), [col], cost=(400.0, 0, 0, 0))
+    paired = any(any(x) for x in OPT["pairs"])
+    if paired:
+        op("g", lambda: g.iota(ap(pu_), [[-16, 8], [-2, 9]], 0, 1), (), [pu_], cost=(270.0, 0, 0, 0))
+    mum, lmu = new("pi", 64), new("pu", 64)
+    ts(ap(mum), ap(mui), H - 1, None, ALU.bitwise_and, None, [mui], [mum], 64)
+    cp(ap(lmu), ap(mum), [mum], [lmu], 64)
+    pcol, gcol, gneg = new("pf", 1), new("pf", 1), new("pf", 1)
     plo, phi = new("pi", 8), new("pi", 8)
     cp(ap(pcol), ap(prt, 0, 1), [prt], [pcol], 1)
     ts(ap(plo), ap(prt), 15, None, ALU.bitwise_and, None, [prt], [plo], 8)
     ts(ap(phi), ap(prt), 4, None, ALU.logical_shift_right, None, [prt], [phi], 8)
     ts(ap(gcol), ap(phi, 0, 1), 16.0, 15.0, ALU.mult, ALU.add, [phi], [gcol], 1)
+    ts(ap(gneg), ap(phi, 0, 1), -16.0, float(H), ALU.mult, ALU.add, [phi], [gneg], 1)
     wide1 = new("pb", 240)
     ts(ap(wide1, 0, 128), ap(col, 0, 128), ap(pcol), None, ALU.is_equal, None, [col, pcol], [wide1], 128)
     cp(ap(wide1, 128, 240), ap(wide1, 0, 112), [wide1], ["wide1b"], 112, 0.5)
-    consts = {(1, "pb", 128): wide1[:2] + (128, wide1[3])}
+    consts = {(1, 128): wide1[:2] + (128, wide1[3])}
 
-    def diag(v, pool, wide=128):
-        if (v, pool, wide) not in consts:
-            x = new(pool, wide)
-            if pool == "pb":
-                act(ap(x), ap(wide1, 0, wide), 0.0, [wide1], [x], wide, scale=float(v))
+    def diag(v, wide=128, eng="a"):
+        if (v, wide) not in consts:
+            m = abs(v)
+            while m % 2 == 0:
+                m //= 2
+            x = new("pb" if m < 256 and m == int(m) else "ph", wide)
+            rd = [wide1, "wide1b"][:1 + (wide > 128)]
+            if eng == "a":
+                act(ap(x), ap(wide1, 0, wide), 0.0, rd, [x], wide, scale=float(v))
             else:
-                ts(ap(x), ap(wide1, 0, wide), float(v), None, ALU.mult, None, [wide1, "wide1b"][:1 + (wide > 128)], [x], wide, 0.5)
-            consts[(v, pool, wide)] = x
-        return consts[(v, pool, wide)]
+                ts(ap(x), ap(wide1, 0, wide), float(v), None, ALU.mult, None, rd, [x], wide, 0.5)
+            consts[(v, wide)] = x
+        return consts[(v, wide)]
 
-    pick = new("pb", 144)
+    pick, pickb = new("pb", 144), new("pb", 144)
     ts(ap(pick), ap(col), ap(gcol), None, ALU.is_equal, None, [col, gcol], [pick], 144)
-    j_, r_, m8, t1, t2, t3 = [new("pi", 8) for _ in range(6)]
+    act(ap(pickb), ap(pick), 0.0, [pick], [pickb], 144, scale=OFF)
+    j_, r_, m8, t1, t2, ta, tb, rx = [new("pi", 8) for _ in range(8)]
     ts(ap(t1), ap(col, 0, 8), 16.0, None, ALU.mult, None, [col], [t1], 8)
     tt(ap(j_), ap(t1), ap(plo), ALU.add, [t1, plo], [j_], 8)
     ts(ap(r_), ap(j_), 7, None, ALU.bitwise_and, None, [j_], [r_], 8)
     tt(ap(m8), ap(j_), ap(r_), ALU.subtract, [j_, r_], [m8], 8)
     tt(ap(t2), ap(phi), ap(r_), ALU.subtract, [phi, r_], [t2], 8)
+    ts(ap(ta), ap(t2), 8.0, None, ALU.add, None, [t2], [ta], 8)
+    ts(ap(tb), ap(ta), 7, None, ALU.bitwise_and, None, [ta], [tb], 8)
+    tt(ap(rx), ap(tb), ap(m8), ALU.add, [tb, m8], [rx], 8)
+    mirror = {}
 
-    def rot(sign):
-        a, b, c = new("pi", 8), new("pi", 8), new("pi", 8)
-        ts(ap(a), ap(t2), float(sign), 8.0, ALU.mult, ALU.add, [t2], [a], 8)
-        ts(ap(b), ap(a), 7, None, ALU.bitwise_and, None, [a], [b], 8)
-        tt(ap(c), ap(b), ap(m8), ALU.add, [b, m8], [c], 8)
-        return c
-    rp, rx = rot(-1), rot(1)
-    w, wp = 40, 48
-    lperm2, lperm, lext = new("pu", 8), new("pu", 8), new("pu", 8)
-    cp(ap(lperm2), ap(rp), [rp], [lperm2], 8)
-    ts(ap(lperm), ap(rp), float(w - 1), None, ALU.min, None, [rp], [lperm], 8)
-    ts(ap(t3), ap(rx), float(w - 1), None, ALU.min, None, [rx], [t3], 8)
-    ts(ap(lext), ap(t3), 16.0, 15.0, ALU.mult, ALU.add, [t3], [lext], 8)
-    pat, rst, c1536 = new("pf", 384), new("pb", N * W), new("ph", w)
-    fill(ap(pat), 128.0, [pat], 384)
-    fill(ap(pat, 0, 384, 16), -2.0 ** 25, [pat], 24)
-    fill(ap(rst), 1.0, [rst], 160)
-    fill(ap(rst, 0, N * W, W), 0.0, [rst], 4)
-    fill(ap(c1536), 1536.0, [c1536], 20)
+    def lref(w, mul=1, add=0, twice=False):
+        if (w, mul, twice) not in mirror:
+            a, b, c = new("pi", 8), new("pu", 8), new("pi", 8)
+            if twice:
+                ts(ap(c), ap(rx), float(w), float(w), ALU.is_ge, ALU.mult, [rx], [c], 8)
+                tt(ap(a), ap(rx), ap(c), ALU.subtract, [rx, c], [a], 8)
+            elif mul == 1:
+                ts(ap(b), ap(rx), float(w - 1), None, ALU.min, None, [rx], [b], 8)
+            else:
+                ts(ap(a), ap(rx), float(w - 1), None, ALU.min, None, [rx], [a], 8)
+            if mul != 1:
+                ts(ap(b), ap(a), float(mul), float(add), ALU.mult, ALU.add, [a], [b], 8)
+            mirror[(w, mul, twice)] = b
+        x = mirror[(w, mul, twice)]
+        return x, ap(x, 0, ((1 + twice) * w + 15) // 16)
+
+    pat, c1536 = new("pf", 512), new("ph", 128)
+    if not all(all(x) for x in OPT["pairs"]):
+        nmax = 128 * max(max(c[1]) for c in CH)
+        fill(ap(pat, 0, nmax), 0.0, [pat], nmax)
+        fill(ap(pat, 0, nmax, 16), -2.0 ** 25, [pat], 32)
+    fill(ap(c1536), 1536.0, [c1536], 64)
+    bon = [new("pf", 1), new("pf", 1)]
+    for x, step, v in zip(bon, (256.0, 128.0), (-2047.0, -160.0)):
+        ts(ap(x), ap(plo, 0, 1), -step, 15 * step + v, ALU.mult, ALU.add, [plo], [x], 1)
     blk, tri, ta, tb, tc, td = new("pb", 128), new("pb", 128), new("pi", 128), new("pf", 1), new("pb", 128), new("pb", 128)
     ts(ap(ta), ap(col, 0, 128), 4, None, ALU.logical_shift_right, None, [col], [ta], 128)
     cp(ap(tb), ap(phi, 0, 1), [phi], [tb], 1)
     ts(ap(blk), ap(ta), ap(tb), None, ALU.is_equal, None, [ta, tb], [blk], 128)
     ts(ap(tc), ap(col, 0, 128), ap(pcol), -1.0, ALU.is_lt, ALU.mult, [col, pcol], [tc], 128)
     tt(ap(td), ap(tc), ap(blk), ALU.mult, [tc, blk], [td], 128)
-    d512 = diag(-512, "pb")
+    d512 = diag(-512)
     tt(ap(tri), ap(td), ap(d512), ALU.add, [td, d512], [tri], 128)
     nblk, ntri = new("pb", 128), new("pb", 128)
     act(ap(nblk), ap(blk), 0.0, [blk], [nblk], 128, scale=-1.0)
     act(ap(ntri), ap(tri), 0.0, [tri], [ntri], 128, scale=-1.0)
-    sgn, run = new("pb", (N + 1) * W), new("pb", (N + 1) * W)
-    for j, v in ((0, 1.0), (N, -1.0)):
-        fill(ap(sgn, j * W, (j + 1) * W), v, ["sgn%d" % j], 40)
-        scan(ap(run, j * W, (j + 1) * W), ap(rst, 0, W), ap(sgn, j * W, (j + 1) * W), ALU.mult, ALU.add, ["sgn%d" % j, rst], ["run%d" % j], 40)
+    sgn, run, rst = [], [], []
+    for c, ch in enumerate(CH):
+        u = 8 * sum(ch[1]) + 1
+        a, b, z = new("pb", (N + 1) * u), new("pb", (N + 1) * u), new("pb", N * u)
+        fill(ap(z), 1.0, [z], N * u // 2)
+        fill(ap(z, 0, N * u, u), 0.0, [z], 4)
+        if c == 0:
+            fill(ap(a, u, N * u, u), 0.0, ["carry0"], 4)
+        for j, v in ((0, 1.0), (N, -1.0)):
+            fill(ap(a, j * u, (j + 1) * u), v, ["sgn%d_%d" % (j, c)], 40)
+            fill(ap(a, j * u, j * u + 1), v * 8 * ch[0], ["sgn%d_%d" % (j, c)], 1)
+            scan(ap(b, j * u, (j + 1) * u), ap(z, 0, u), ap(a, j * u, (j + 1) * u), ALU.mult, ALU.add, ["sgn%d_%d" % (j, c), z],
+                 ["run%d_%d" % (j, c)], 40)
+        sgn.append(a)
+        run.append(b)
+        rst.append(z)
+    if paired:
+        e0, e1, em, MK, MW, MA = new("pb", 72), new("pb", 72), new("pb", 72), new("pb", 144), new("pb", 144), new("pb", 144)
+        for x, v in ((e0, 0.0), (e1, 1.0), (em, -2.0)):
+            ts(ap(x), ap(pu_), v, None, ALU.is_equal, None, [pu_], [x], 72)
+        fill(ap(e0, 8, 72, 9), 0.0, [e0], 8)
+        fill(ap(e1, 8, 72, 9), 0.0, [e1], 8)
+        tt(ap(MK, 0, 72), ap(e1), ap(e0), ALU.subtract, [e0, e1], ["MKa"], 72)
+        tt(ap(MK, 72, 144), ap(em), ap(e0), ALU.subtract, [e0, em], [MK], 72)
+        fill(ap(MK, 72, 144, 9), 0.0, [MK], 8)
+        act(ap(MW), ap(MK), 0.0, [MK, "MKa"], [MW], 144, scale=131072.0)
+        act(ap(MA), ap(MK), 0.0, [MK, "MKa"], [MA], 144, scale=4096.0)
+        ts(ap(MK, 72, 144, 9), ap(e0, 0, 72, 9), -32768.0, None, ALU.mult, None, [e0], [MK], 8)
 
-    s37, sraw, salh = new("pi", W), new("pi", W), new("ph", W)
-    ts(ap(s37), ap(beg), float(K2), None, ALU.mult, None, [beg], [s37], W)
-    tt(ap(sraw), ap(s37), ap(sal), ALU.add, [s37, sal], [sraw], W)
-    cp(ap(salh), ap(sal), [sal], [salh], W)
+    s1_, sm_, hb, hbm = new("pi", W), new("pi", W), new("pi", W), new("pi", W)
+    lb0, lh0, salB = new("pu", W), new("pu", W), new("ph", W)
+    cp(ap(lb0), ap(beg), [beg], [lb0], W)
+    ts(ap(s1_), ap(sal), float(MU), ap(gneg), ALU.mult, ALU.add, [sal, gneg], [s1_], W)
+    ts(ap(sm_), ap(s1_), H - 1, None, ALU.bitwise_and, None, [s1_], [sm_], W)
+    tt(ap(hb), ap(sm_), ap(beg), ALU.add, [sm_, beg], [hb], W)
+    ts(ap(hbm), ap(hb), H - 1, None, ALU.bitwise_and, None, [hb], [hbm], W)
+    cp(ap(lh0), ap(hbm), [hbm], [lh0], W)
+    x, xa = lref(W)
+    cp(ap(salB), ap(sm_).indirect(xa), [sm_, x], [salB], W, gather=True)
     lists, bsh = [], []
-    for c, (b0, subs) in enumerate(CH):
-        k0 = 8 * b0
-        bs, l1, bh = new("pi", 2 * w), new("pu", 2 * w), new("ph", 2 * w)
-        cp(ap(bs, 0, w), ap(beg, k0, k0 + w), [beg], [bs], w)
-        ts(ap(bs, w, 2 * w), ap(sraw, k0, k0 + w), H - 1, None, ALU.bitwise_and, None, [sraw], [bs], w)
-        cp(ap(l1), ap(bs).indirect(ap(lperm2, 0, 5)), [bs, lperm2], [l1], 2 * w, gather=True)
-        cp(ap(bh), ap(bs), [bs], [bh], 2 * w)
-        lists.append(l1)
+    for b0, subs, kb, s0, s1 in CH:
+        k0, w = 8 * b0, 8 * sum(subs)
+        bh = new("ph", 2 * w)
+        cp(ap(bh, 0, w), ap(beg, k0, k0 + w), [beg], [bh[3] + "a"], w)
+        cp(ap(bh, w, 2 * w), ap(hbm, k0, k0 + w), [hbm], [bh], w)
+        lists.append(((lb0, k0), (lh0, k0)))
         bsh.append(bh)
-    mine = T.N2[:, me * H:(me + 1) * H]
-    ts(mine, T.nzs[:], -32.0, None, ALU.add, None, ["nzs"], ["N2_0_%d" % me, "N2_1_%d" % me], H, 0.5)
-    for h in range(2):
-        dma("s", T.N1[:, h * H:(h + 1) * H], mine, ["N2_0_%d" % me], ["N1_%d" % h], 3000)
 
-    I, Ih = diag(1, "pb"), diag(1, "ph")
-    q = B // N
-    f0 = me * 2 * FW
-    rt = me * D + RAW
+    def nblock(r):
+        return (N - 1 - r) * GAP
+    mine = T.NB[:, nblock(me):nblock(me) + H]
+    for h in range(2):
+        lin("mu", T.NB[:, nblock(me) + h * q:nblock(me) + (h + 1) * q], ap(nzs).indirect(ap(lmu, 32 * h, 32 * h + 32)), 1, -32,
+            [nzs, lmu], ["N2_%d_%d" % (h, me)], q, gather=True)
+
+    I = diag(1)
+    pa, pb_ = OPT["spare"]
     rch, big = new("pb", TRI), new("pb", q)
     ts(ap(rch), R[:, rt + 2 * TRI:rt + 3 * TRI], 1 / 16, 160 - 7.5 / 16, ALU.mult, ALU.add, ["Rt%d" % me], [rch], TRI, 0.5)
-    d16, dm16, d64, dm64, d4096 = diag(16, "pb"), diag(-16, "pb"), diag(64, "pb"), diag(-64, "pb"), diag(4096, "pb")
-    mm(group(ps[2][:, 0:TRI], [(ap(d16), R[:, rt:rt + TRI]), (ap(I), ap(rch))], TRI)
-       + group(ps[2][:, TRI:2 * TRI], [(ap(d16), R[:, rt + TRI:rt + 2 * TRI]), (ap(I), R[:, rt + 2 * TRI:rt + 3 * TRI]),
-                                       (ap(dm16), ap(rch))], TRI), ["Rt%d" % me, rch, d16, dm16, I], 2)
-    ts(F[:, f0 + q:f0 + FW], ps[2][:, 0:TRI], -2208.0, None, ALU.add, None, (), ["F0t"], TRI, banks=[2])
-    ts(F[:, f0 + FW + q:f0 + 2 * FW], ps[2][:, TRI:2 * TRI], 512.0, None, ALU.add, None, (), ["F1t"], TRI, banks=[2])
-    mm(group(ps[3][:], [(ap(I), T.nzs[:, 0:q]), (ap(d64), T.wts[:, me::N])], q), ["nzs", "wts", I, d64], 3)
-    ts(F[:, f0:f0 + q], ps[3][:], -2048.0, None, ALU.add, None, (), ["F0_%d" % me], q, banks=[3])
-    ts(ap(big), T.kds[:, me::N], 64.0, None, ALU.is_ge, None, ["kds"], [big], q, 0.5)
-    mm(group(ps[7][:], [(ap(I), T.nzs[:, q:2 * q]), (ap(dm64), T.kds[:, me::N]), (ap(d4096), ap(big))], q),
-       ["nzs", "kds", big, I, dm64, d4096], 7)
-    ts(F[:, f0 + FW:f0 + FW + q], ps[7][:], 1984.0, None, ALU.add, None, (), ["F1_%d" % me], q, banks=[7])
+    d16, dm16, d64, dm64, d4096 = diag(16), diag(-16), diag(64), diag(-64), diag(4096)
+    pt = CH[0][3]
+    mm(group(ps[pt][:, 0:TRI], [(ap(d16), R[:, rt:rt + TRI]), (ap(I), ap(rch))], TRI)
+       + group(ps[pt][:, TRI:2 * TRI], [(ap(d16), R[:, rt + TRI:rt + 2 * TRI]), (ap(I), R[:, rt + 2 * TRI:rt + 3 * TRI]),
+                                        (ap(dm16), ap(rch))], TRI), ["Rt%d" % me, rch, d16, dm16, I], pt)
+    ts(F[:, f0 + q:f0 + FW], ps[pt][:, 0:TRI], -2208.0, None, ALU.add, None, (), ["F0t"], TRI, banks=[pt])
+    ts(F[:, f0 + FW + q:f0 + 2 * FW], ps[pt][:, TRI:2 * TRI], 512.0, None, ALU.add, None, (), ["F1t"], TRI, banks=[pt])
+
+    def kids(r):
+        return [r + N * j for j in range(16 // N)]
+
+    def blocks(b, mat, tab, step, cs, stop):
+        return [(ps[b][:, 128 * j:128 * (j + 1)], ap(mat), tab(c, step), False, stop and j == len(cs) - 1, 128) for j, c in enumerate(cs)]
+    n0 = nblock(me)
+    mm([(ps[pa][:], ap(I), T.NB[:, n0:n0 + q], True, False, q)], ["N2_0_%d" % me, I], pa)
+    mm(blocks(pa, d64, lambda c, s: ap(wts, c, B, s), 16, kids(me), True), [wts, d64], pa)
+    lin("f0", F[:, f0:f0 + q], ps[pa][:], 1, -2016, (), ["F0_%d" % me], q, banks=[pa])
+    ts(ap(big), ap(kds, me, B, N), 64.0, None, ALU.is_ge, None, [kds], [big], q, 0.5)
+    mm([(ps[pb_][:], ap(I), T.NB[:, n0 + q:n0 + 2 * q], True, False, q)], ["N2_1_%d" % me, I], pb_)
+    mm(blocks(pb_, dm64, lambda c, s: ap(kds, c, B, s), 16, kids(me), False), [kds, dm64], pb_)
+    mm(blocks(pb_, d4096, lambda c, s: ap(big, c, q, s), N, range(N), True), [big, d4096], pb_)
+    lin("f1", F[:, f0 + FW:f0 + FW + q], ps[pb_][:], 1, 2016, (), ["F1_%d" % me], q, banks=[pb_])
 
     out_e = topo.engines(core, cores[far[0]])
     all_e = topo.engines(core, cores[mate])
@@ -271,7 +461,7 @@ def rank_program(g, core, T, topo):
             return F[:, (2 * r + h) * FW:(2 * r + h + 1) * FW]
         return R[:, r * D + h * (RAW // 2):r * D + (h + 1) * (RAW // 2)]
 
-    def send(items, rd, cost):
+    def send(items, rd):
         def fn():
             tr = []
             for kind, h, r, to, es in items:
@@ -281,266 +471,288 @@ def rank_program(g, core, T, topo):
             g.remote_dma_fused(tr, local_sem=T.sem.sent)
             return None
         sent[0] += sum(len(it[4]) for it in items)
-        i = op("g", fn, rd, (), cost=cost, sem="none", after=gorder[-1:])
+        i = op("g", fn, rd, (), cost=(500.0 if gorder else 1900.0, 0, 0, 0), sem="none", after=gorder[-1:])
         gorder.append(i)
         return i
 
     def arrive(kind, h, r, n, after, lat):
         name = ("F%d_%d" if kind == "f" else "Rraw%d_%d") % (h, r)
-        return op(None, None, (), [name], cost=0.0, lat=lat, sem=("%s%d_%d" % (kind, h, r), n), after=[after])
+        return op(None, None, (), [name], cost=(0.0, 0, 0, 0), lat=lat, sem=("%s%d_%d" % (kind, h, r), n), after=[after])
 
     ho, hi_, ha = len(out_e) // 2, len(in_e) // 2, len(all_e) // 2
-    sr = send([("r", 0, me, far[0], out_e[:ho]), ("r", 1, me, far[1], out_e[ho:]), ("r", 0, me, mate, in_e[:hi_]),
-               ("r", 1, me, mate, in_e[hi_:])], ["Rraw0_%d" % me], 1500)
-    sf = [send([("f", h, me, far[h], out_e), ("f", h, me, mate, in_e)], ["F%d_%d" % (h, me), "F%dt" % h], 600) for h in range(2)]
-    for h in range(2):
-        arrive("r", h, mate, hi_, sr, 2500)
-        arrive("r", h, far[h], ho, sr, 3500)
-        arrive("f", h, mate, len(in_e), sf[h], 2200)
-        arrive("f", h, far[h], len(out_e), sf[h], 3200)
-    for h in range(2):
-        fw = send([("f", h, far[h], mate, all_e)], ["F%d_%d" % (h, far[h])], 600)
-        arrive("f", h, far[1 - h], len(all_e), fw, 2000)
-    fw = send([("r", 0, far[0], mate, all_e[:ha]), ("r", 1, far[1], mate, all_e[ha:])], ["Rraw0_%d" % far[0], "Rraw1_%d" % far[1]], 600)
-    for h in range(2):
-        arrive("r", h, far[1 - h], ha, fw, 2000)
+    for name in OPT["sends"]:
+        if name == "r":
+            i = send([("r", 0, me, far[0], out_e[:ho]), ("r", 1, me, far[1], out_e[ho:]), ("r", 0, me, mate, in_e[:hi_]),
+                      ("r", 1, me, mate, in_e[hi_:])], ["Rraw0_%d" % me])
+            for h in range(2):
+                arrive("r", h, mate, hi_, i, 3500)
+                arrive("r", h, far[h], ho, i, 4500)
+        elif name[0] == "f":
+            h = int(name[1])
+            i = send([("f", h, me, far[h], out_e), ("f", h, me, mate, in_e)], ["F%d_%d" % (h, me), "F%dt" % h])
+            arrive("f", h, mate, len(in_e), i, 2900)
+            arrive("f", h, far[h], len(out_e), i, 3300)
+        elif name == "hr":
+            i = send([("r", 0, far[0], mate, all_e[:ha]), ("r", 1, far[1], mate, all_e[ha:])], ["Rraw0_%d" % far[0], "Rraw1_%d" % far[1]])
+            for h in range(2):
+                last = arrive("r", h, far[1 - h], ha, i, 2400)
+        else:
+            h = int(name[1])
+            i = send([("f", h, far[h], mate, all_e)], ["F%d_%d" % (h, far[h])])
+            arrive("f", h, far[1 - h], len(all_e), i, 2200)
+    for h, n in enumerate((H, H, 336)):
+        dma("s", T.N1[:, h * H:h * H + n], T.NB[:, n0:n0 + n], ["N2_0_%d" % me, "N2_1_%d" % me, "Rraw0_%d" % far[1]], ["N1_%d" % h], 3000)
 
     def unpack(h, r, b):
-        tab, name = (T.W2, "W2_%d" % r) if h == 0 else (T.KK, "KK_%d" % r)
-        src = F[:, (2 * r + h) * FW:(2 * r + h) * FW + q]
-        ts(tab[:, r::N], src, 1 / 64, 192 - 31.5 / 64, ALU.mult, ALU.add, ["F%d_%d" % (h, r)], [name], q, 0.5)
+        name = ("W2_%d", "KK_%d")[h] % r
+        a = (2 * r + h) * FW
+
+        def at(c, s):
+            return T.WK[:, 256 * (15 - c) + 128 * h:256 * (15 - c) + 128 * (h + 1)]
+        for j, c in enumerate(kids(r)):
+            ts(at(c, 0), F[:, a + 128 * j:a + 128 * (j + 1)], 1 / 64, 192 - 31.5 / 64, ALU.mult, ALU.add, ["F%d_%d" % (h, r)],
+               ["%s_%d" % (name, j)], 128, 0.5)
         if r != me:
-            mm(group(ps[b][:], [(ap(Ih), src), (ap(dm64), tab[:, r::N])], q), ["F%d_%d" % (h, r), name, Ih, dm64], b)
-            act(T.N2[:, r * H + h * q:r * H + (h + 1) * q], ps[b][:], 12256.0, (), ["N2_%d_%d" % (h, r)], q, banks=[b])
+            mm([(ps[b][:], ap(I), F[:, a:a + q], True, False, q)] + blocks(b, dm64, at, 0, kids(r), True),
+               ["F%d_%d" % (h, r), I, dm64] + ["%s_%d" % (name, j) for j in range(N)], b)
+            lin("n%d%d" % (h, [mate, far[h], far[1 - h]].index(r)), T.NB[:, nblock(r) + h * q:nblock(r) + (h + 1) * q], ps[b][:], 1, 12256,
+                (), ["N2_%d_%d" % (h, r)], q, banks=[b])
 
     def unpack_rooms(r, b):
         hh = new("ph", 2 * TRI)
         x = [F[:, (2 * r + h) * FW + q:(2 * r + h + 1) * FW] for h in range(2)]
         for h in range(2):
             ts(ap(hh, h * TRI, (h + 1) * TRI), x[h], 1 / 16, 1408 - 7.5 / 16, ALU.mult, ALU.add, ["F%d_%d" % (h, r)], [hh], TRI, 0.5)
-        e16, e256, em16 = diag(16, "ph"), diag(-256, "ph"), diag(-16, "ph")
-        mm(group(ps[b][:, 0:2 * TRI], [(ap(Ih), ap(hh))], 2 * TRI)
-           + group(ps[b][:, 2 * TRI:3 * TRI], [(ap(e16), x[0]), (ap(e256), ap(hh, 0, TRI)), (ap(Ih), x[1]),
-                                               (ap(em16), ap(hh, TRI, 2 * TRI))], TRI),
-           [hh, "F0_%d" % r, "F1_%d" % r, Ih, e16, e256, em16], b)
+        dm256 = diag(-256)
+        mm(group(ps[b][:, 0:2 * TRI], [(ap(I), ap(hh))], 2 * TRI)
+           + group(ps[b][:, 2 * TRI:3 * TRI], [(ap(d16), x[0]), (ap(dm256), ap(hh, 0, TRI)), (ap(I), x[1]),
+                                               (ap(dm16), ap(hh, TRI, 2 * TRI))], TRI),
+           [hh, "F0_%d" % r, "F1_%d" % r, I, d16, dm256, dm16], b)
         a = r * D + RAW
         act(R[:, a:a + 2 * TRI], ps[b][:, 0:2 * TRI], -1280.0, (), ["Rt%d" % r], 2 * TRI, banks=[b])
         act(R[:, a + 2 * TRI:a + 3 * TRI], ps[b][:, 2 * TRI:3 * TRI], 17.0 * 22528, (), ["Ru%d" % r], TRI, banks=[b])
 
-    zero = diag(0, "pb")
-    e4096, d131 = diag(4096, "ph"), diag(131072, "pb")
-    rot1, rotm, rotc, dm2047 = diag(1, "ph", 240), diag(-16, "ph", 240), diag(2047, "ph", 240), diag(-2047, "ph")
+    d131 = diag(131072)
+    rotm, rotc = diag(-16, 240), diag(2047, 240)
 
-    def draw(c, lb, lh, wtab, ktab, ntab, bias, rw, rk, rn):
-        b0, subs = CH[c]
-        lead[0] = OPT["lead"][c]
-        cuts = [[(0, sum(subs), (0, 1))], [(0, subs[0], (0,)), (subs[0], sum(subs), (1,))]]
+    def draw(c, second, pair, lb, lh, wtab, ktab, ntab, rw, rk, rn):
+        b0, subs, kb = CH[c][:3]
+        lead[0] = float(len(CH) - 1 - c)
+        w = 8 * sum(subs)
+        wp = (w + 15) // 16 * 16 if second else 2 * w
+        bias = -160.0 if second else 0.0
+        ends = [sum(subs[:u]) for u in range(len(subs) + 1)]
+        cuts = [[(0, ends[-1], range(len(subs)))], [(ends[u], ends[u + 1], (u,)) for u in range(len(subs))]]
         for buf, nm, tab, rd_, k in ((T.Wg, "Wg", wtab, rw, 0), (T.Kg, "Kg", ktab, rk, 1)):
+            bs_ = ap(bon[second]) if k else bias
             for x0, x1, us in cuts[OPT["split"][k]]:
-                act(buf[:, 128 * (b0 + x0):128 * (b0 + x1)], tab.indirect(ap(lb[0], lb[1] + 8 * x0, lb[1] + 8 * x1)), bias, rd_ + [lb[0]],
-                    ["%s_%d_%d" % (nm, c, u) for u in us], 128 * (x1 - x0), gather=True)
+                act(buf[:, 128 * (b0 + x0):128 * (b0 + x1)], tab.indirect(ap(lb[0], lb[1] + 8 * x0, lb[1] + 8 * x1)), bs_,
+                    rd_ + [lb[0]] + ([bon[second]] if k else []), ["%s_%d_%d" % (nm, c, u) for u in us], 128 * (x1 - x0), gather=True)
         for x0, x1, us in cuts[OPT["split"][2]]:
             a, e = 128 * (b0 + x0), 128 * (b0 + x1)
             tt(T.A[:, a:e], ntab.indirect(ap(lh[0], lh[1] + 8 * x0, lh[1] + 8 * x1)), T.Wg[:, a:e], ALU.mult,
                rn + [lh[0]] + ["Wg_%d_%d" % (c, u) for u in us], ["A_%d_%d" % (c, u) for u in us], e - a, gather=True)
-        s0 = 0
         for u, nb in enumerate(subs):
-            a, n = 128 * (b0 + s0), 128 * nb
-            tk = "_%d_%d" % (c, u)
-            bk = 4 * c + u
-            m_ = mm([(ps[bk][:, 0:n], ap(zero), T.nzs[:, 0:n], True, False, n)], [zero, "nzs"], bk)
-            for buf, nm, mat in ((T.Wg, "Wg", d131), (T.Kg, "Kg", I), (T.A, "A", e4096)):
-                m_ = mm([(ps[bk][:, 128 * m:128 * (m + 1)], buf[:, a + 128 * m:a + 128 * (m + 1)], ap(mat), False,
-                          nm == "A" and m == nb - 1, 128) for m in range(nb)], [nm + tk, mat], bk, [m_])
-            scan(T.Z[:, a:a + n], ap(pat, 0, n), ps[bk][:, 0:n], ALU.add, ALU.max, [pat], ["Z" + tk], n, banks=[bk])
-            s0 += nb
-        zs = ["Z_%d_%d" % (c, u) for u in range(len(subs))]
-        win = T.Z[:, 128 * b0:128 * (b0 + s0)]
+            a, bk, tk = b0 + ends[u], kb[u], "_%d_%d" % (c, u)
+            for buf, nm, mat, mp in ((T.Wg, "Wg", d131, 0), (T.Kg, "Kg", I, 1), (T.A, "A", d4096, 2)):
+                first, last = nm == "Wg", nm == "A"
+                if pair:
+                    mat = (MW, MK, MA)[mp]
+                    mm([(ps[bk][:, 256 * y + 72 * m:256 * y + 72 * (m + 1)], buf[:, 128 * (a + m):128 * (a + m + 1)], ap(mat, 72 * y, 72 * y + 72),
+                         first and m == 0 and y == 0, last and m == nb - 1 and y == 1, 72) for m in range(nb) for y in range(2)],
+                       [nm + tk, mat, "MKa"], bk)
+                else:
+                    mm([(ps[bk][:, 128 * m:128 * (m + 1)], buf[:, 128 * (a + m):128 * (a + m + 1)], ap(mat), first and m == 0,
+                         last and m == nb - 1, 128) for m in range(nb)], [nm + tk, mat], bk)
+            if pair:
+                n = 72 * nb
+                act(T.Rl[:, 72 * a:72 * a + n], ps[bk][:, 0:n], 0.0, (), ["Rl" + tk], n, banks=[bk], func=AF.Relu)
+                scan(T.Z9[:, 72 * a:72 * a + n], ps[bk][:, 256:256 + n], T.Rl[:, 72 * a:72 * a + n], ALU.add, ALU.max, ["Rl" + tk],
+                     ["Z9" + tk], n, banks=[bk])
+            else:
+                n = 128 * nb
+                scan(T.Z[:, 128 * a:128 * a + n], ap(pat, 0, n), ps[bk][:, 0:n], ALU.add, ALU.max, [pat], ["Z" + tk], n, banks=[bk])
+        zs = ["%s_%d_%d" % ("Z9" if pair else "Z", c, u) for u in range(len(subs))]
+        win = T.Z9[:, 72 * b0:72 * (b0 + ends[-1])] if pair else T.Z[:, 128 * b0:128 * (b0 + ends[-1])]
+        x, xa = lref(w, 9, 8, not second) if pair else lref(w, 16, 15, not second)
         hn, low = new("pf", wp), new("ph", wp)
-        ts(ap(hn), win.indirect(ap(lext, 0, 3)), BIG, -BIG, ALU.add, ALU.add, zs + [lext], [hn], wp, gather=True)
-        tt(ap(low), win.indirect(ap(lext, 0, 3)), ap(hn), ALU.subtract, zs + [lext, hn], [low], wp, gather=True)
+        ts(ap(hn), win.indirect(xa), BIG, -BIG, ALU.add, ALU.add, zs + [x], [hn], wp, gather=True)
+        tt(ap(low), win.indirect(xa), ap(hn), ALU.subtract, zs + [x, hn], [low], wp, gather=True)
         return low
 
-    def turn(out, mat, x, start, stop):
-        return [(out[:, r:w:8], ap(mat, 16 * r, 16 * r + 128), ap(x, r, w, 8), start, stop if start else (stop and r == 7), 5)
+    def turn(b, at, w, mat, x, stop):
+        return [(ps[b][:, at + (-r) % 8:at + w:8], ap(mat, 16 * r, 16 * r + 128), ap(x, r, w, 8), False, stop and r == 7, w // 8)
                 for r in range(8)]
 
-    def parts(v):
-        top = 1 << (abs(v).bit_length() - 1)
-        return [v] if abs(v) < 256 or v % 4 == 0 and abs(v) < 1024 else [top, v - top]
+    def terms(out, tm, n, start, stop, b):
+        mm(group(out, [(ap(m), x) for m, _, x in tm], n, start, stop), [y for m, t, _ in tm for y in (m, t)], b)
 
-    st = [{"g2": [], "k": []} for _ in CH]
-    W2r, KKr = ["W2_%d" % r for r in range(N)], ["KK_%d" % r for r in range(N)]
-    N2r = ["N2_%d_%d" % (h, r) for h in range(2) for r in range(N)]
+    def modulo(tm, b, at, n, m):
+        z = new("pb", n)
+        terms(ps[b][:, at:at + n], tm, n, True, True, b)
+        lin("mod", ap(z), ps[b][:, at:at + n], 1 / m, 191.5 + 1 / 4096, (), [z], n, banks=[b])
+        return tm + [(diag(-m), z, ap(z)), (diag(m // 8), c1536, ap(c1536, 0, n))]
+
+    st = [{"fl": [], "fb": []} for _ in CH]
+    WKr = ["%s_%d_%d" % (x, r, j) for x in ("W2", "KK") for r in range(N) for j in range(N)]
+    N2r = ["N2_%d_%d" % (h, r) for h in range(2) for r in range(N)] + [wts, kds, "wx", "kx", nzs, nds, "rest"]
     Rr = (["Rraw%d_%d" % (h, r) for h in range(2) for r in range(N)] + ["Rt%d" % r for r in range(N)]
           + ["Ru%d" % r for r in range(N) if r != me])
-    unpack(0, me, 3)
-    unpack(1, me, 7)
+    unpack(0, me, pa)
+    unpack(1, me, pb_)
     for rnd in range(3):
-        own = new("pb", W)
-        ownt = [own[3] + "_%d" % c for c in range(2)]
-        l2 = []
-        for c, (b0, subs) in enumerate(CH):
-            k0, s0, s1 = 8 * b0, 4 * c + 2, 4 * c + 3
-            low = draw(c, (lists[c], 0), (lists[c], w), T.wts[:], T.kds[:], mine if rnd == 0 else T.N1[:], 0.0,
-                       ["wts"], ["kds"], ["N2_0_%d" % me] if rnd == 0 else ["N1_0", "N1_1"])
-            mm(turn(ps[s0], rot1, low, True, True), [low, rot1], s0)
-            y, b1, ow, z, hr, hm, ix = [new("pi", w) for _ in range(7)]
-            lb, lh = new("pu", wp), new("pu", wp)
-            ts(ap(y), ps[s0][:, 0:w], 2047 / 128, 15 + 63.5 / 128, ALU.mult, ALU.add, (), [y], w, banks=[s0])
-            ts(ap(b1), ap(y), B - 1, None, ALU.bitwise_and, None, [y], [b1], w)
-            cp(ap(lb), ap(b1).indirect(ap(lperm, 0, 3)), [b1, lperm], [lb], wp, gather=True)
-            ts(ap(z), ap(y), float(K2), None, ALU.mult, None, [y], [z], w)
+        owns, l2 = [], []
+        for c, (b0, subs, kb, s0, s1) in enumerate(CH):
+            k0, w = 8 * b0, 8 * sum(subs)
+            wp = (w + 15) // 16 * 16
             if rnd == 0:
-                tt(ap(hr), ap(z), ap(sal, k0, k0 + w), ALU.add, [z, sal], [hr], w)
+                tabs = (ap(wts, 0, B), ap(kds, 0, B), mine, [wts], [kds], ["N2_0_%d" % me, "N2_1_%d" % me])
             else:
-                tt(ap(hr), ap(z), ps[s1][:, 64:64 + w], ALU.add, [z], [hr], w, 1.0, banks=[s1])
-            ts(ap(hm), ap(hr), H - 1, None, ALU.bitwise_and, None, [hr], [hm], w)
-            ts(ap(ow), ap(y), N - 1, None, ALU.bitwise_and, None, [y], [ow], w)
-            ts(ap(own, k0, k0 + w), ap(ow), 1024.0, 1024.0, ALU.mult, ALU.add, [ow], [ownt[c]], w)
-            tt(ap(ix), ap(hm), ap(own, k0, k0 + w), ALU.add, [hm, ownt[c]], [ix], w)
-            ts(ap(lh), ap(ix).indirect(ap(lperm, 0, 3)), -1024.0, None, ALU.add, None, [ix, lperm], [lh], wp, gather=True)
+                tabs = (ap(wts), ap(kds), T.N1[:], [wts, "wx"], [kds, "kx"], ["N1_0", "N1_1", "N1_2"])
+            low = draw(c, 0, OPT["pairs"][rnd][0], lists[c][0], lists[c][1], *tabs)
+            tm = [(diag(1 / 16), salB, ap(salB, k0, k0 + w))]
+            for fb in st[c]["fb"]:
+                tm += [(diag(KT / 16), fb, ap(fb, 0, w)), (diag(-KT / 16), fb, ap(fb, w, 2 * w))]
+            if rnd:
+                tm = modulo(tm, s1, 384, w, H // 16)
+            terms(ps[s0][:, 0:w], [(I, c1536, ap(c1536, 0, w))], w, True, False, s0)
+            terms(ps[s0][:, w:2 * w], tm, w, False, False, s0)
+            mm(turn(s0, 0, 2 * w, wide1, low, True), [low, wide1, "wide1b"], s0)
+            iv, hm, lb, lh = new("pi", w), new("pi", w), new("pu", w), new("pu", w)
+            lin("lb", ap(lb), ps[s0][:, 0:w], 1, B - 1 - 1536, (), [lb], w, banks=[s0])
+            lin("iv", ap(iv), ps[s0][:, w:2 * w], ALPHA, (B - 1) * ALPHA + 15.373, (), [iv], w, banks=[s0])
+            ts(ap(hm), ap(iv), (N - 1) * GAP + H - 1, None, ALU.bitwise_and, None, [iv], [hm], w)
+            lin("lh", ap(lh), ap(hm), 1, 0, [hm], [lh], w)
+            x, xa = lref(w)
+            own = new("pb", wp)
+            lin("own", ap(own), ap(hm).indirect(xa), 1 / GAP, 194 - 0.125, [hm, x], [own], wp, gather=True)
+            owns.append(own)
             l2.append((lb, lh))
-        lead[0] = OPT["lead"][2]
         if rnd == 0:
             for n_, (h, r) in enumerate([(0, mate), (0, far[0]), (1, mate), (1, far[1]), (0, far[1]), (1, far[0])]):
-                unpack(h, r, (3, 7)[n_ % 2])
+                unpack(h, r, OPT["spare"][n_ % 2])
             for n_, r in enumerate([mate, far[0], far[1]]):
-                unpack_rooms(r, (3, 7)[n_ % 2])
-        src, srct = own, ownt
-        if rnd == 2:
-            src = new("pb", W)
-            for c, (b0, subs) in enumerate(CH):
-                k0 = 8 * b0
-                tt(ap(src, k0, k0 + w), ap(own, k0, k0 + w), ap(st[c]["takes"]), ALU.mult, [ownt[c], st[c]["takes"]], [src[3] + "_%d" % c], w)
-            srct = [src[3] + "_%d" % c for c in range(2)]
-        sg, g2 = new("pb", N * W), new("pb", W)
+                unpack_rooms(r, OPT["spare"][n_ % 2])
         j0 = 0 if rnd == 2 else 1
-        for j in range(j0, N):
-            act(ap(sgn, j * W, (j + 1) * W), ap(src), -1024.0 * j - 512, srct, ["sgn%d" % j], W, func=AF.Sign)
-        mt = ["sgn%d" % j for j in range(N + 1)]
-        scan(ap(run, j0 * W, N * W), ap(rst, 0, (N - j0) * W), ap(sgn, j0 * W, N * W), ALU.mult, ALU.add, mt[j0:N] + [rst],
-             ["run%d" % j for j in range(j0, N)], (N - j0) * W, 0.5)
-        mm(group(ps[7][:, 128:128 + N * W], [(ap(tri), ap(sgn, 0, N * W)), (ap(ntri), ap(sgn, W, (N + 1) * W)),
-                                             (ap(blk), ap(run, 0, N * W)), (ap(nblk), ap(run, W, (N + 1) * W))], N * W),
-           mt + ["run%d" % j for j in range(N + 1)] + [blk, tri, nblk, ntri], 7)
-        act(ap(sg), ps[7][:, 128:128 + N * W], 1.0 - 2 * CAP, (), [sg], N * W, banks=[7], func=AF.Sign, scale=-1.0)
-        mm(group(ps[7][:, 0:W], [(ap(I), ap(sg, r * W, (r + 1) * W)) for r in range(N)], W), [sg, I], 7)
-        act(ap(g2), ps[7][:, 0:W], 4.0, (), [g2], W, banks=[7])
-        for c, (b0, subs) in enumerate(CH):
-            k0, s0, s1 = 8 * b0, 4 * c + 2, 4 * c + 3
+        for c, (b0, subs, kb, s0, cb) in enumerate(CH):
+            w = 8 * sum(subs)
+            u = w + 1
+            lead[0] = float(len(CH) - 1 - c)
+            src, sn, rn = owns[c], sgn[c], run[c]
+            if rnd == 2:
+                src = new("pb", w)
+                tt(ap(src), ap(owns[c], 0, w), ap(st[c]["takes"]), ALU.mult, [owns[c], st[c]["takes"]], [src], w)
+            mt = ["sgn%d_%d" % (j, c) for j in range(N + 1)]
+            rt_ = ["run%d_%d" % (j, c) for j in range(N + 1)]
+            if c:
+                up = 8 * sum(CH[c - 1][1]) + 1
+                lin("carry", ap(sn, j0 * u, N * u, u), ap(run[c - 1], (j0 + 1) * up - 1, N * up, up), 1, 0,
+                    ["run%d_%d" % (j, c - 1) for j in range(j0, N)], ["carry%d" % c] + mt[:1 - j0], N)
+            for j in range(j0, N):
+                act(ap(sn, j * u + 1, (j + 1) * u), ap(src, 0, w), -193.5 - j, [src], [mt[j]], w, func=AF.Sign)
+            scan(ap(rn, j0 * u, N * u), ap(rst[c], 0, (N - j0) * u), ap(sn, j0 * u, N * u), ALU.mult, ALU.add,
+                 mt[j0:N] + [rst[c], "carry%d" % c], rt_[j0:N], (N - j0) * u, 0.5)
+            sg = new("pb", N * u)
+            mm(group(ps[cb][:, 128:128 + N * u], [(ap(tri), ap(sn, 0, N * u)), (ap(ntri), ap(sn, u, (N + 1) * u))], N * u, True, False),
+               mt + ["carry%d" % c, tri, ntri], cb)
+            mm(group(ps[cb][:, 128:128 + N * u], [(ap(blk), ap(rn, 0, N * u)), (ap(nblk), ap(rn, u, (N + 1) * u))], N * u, False, True),
+               rt_ + [blk, nblk], cb)
+            act(ap(sg), ps[cb][:, 128:128 + N * u], 1.0 - 2 * CAP, (), [sg], N * u, banks=[cb], func=AF.Sign, scale=-1.0)
+            mm(group(ps[cb][:, 64:64 + w], [(ap(I), ap(sg, r * u + 1, (r + 1) * u)) for r in range(N)], w), [sg, I], cb)
+            fl = new("pb", 2 * w)
+            act(ap(fl, 0, w), ps[cb][:, 64:64 + w], 4.0 if rnd < 2 else -15.0, (), [fl[3] + "g"], w, banks=[cb])
+            st[c]["fl"].append(fl)
+        for c, (b0, subs, kb, s0, s1) in enumerate(CH):
+            k0, w = 8 * b0, 8 * sum(subs)
+            wp = (w + 15) // 16 * 16
             S = st[c]
-            low = draw(c, (l2[c][0], 0), (l2[c][1], 0), T.W2[:], T.KK[:], T.N2[:], -160.0, W2r, KKr, N2r)
+            fl = S["fl"][rnd]
+            low = draw(c, 1, OPT["pairs"][rnd][1], (l2[c][0], 0), (l2[c][1], 0), T.WK[:, 0:2 * B - 128], T.WK[:, 128:2 * B], T.NB[:],
+                       WKr, WKr, N2r)
             cq, lr = new("ph", wp), new("pu", w)
-            ts(ap(cq), ap(low), 1 / 128, 1536.0, ALU.mult, ALU.add, [low], [cq], wp, 0.5)
-            dv = ps[s0][:, 0:w]
-            m0 = mm(group(dv, [(ap(I), ap(own, k0, k0 + w)), (ap(dm2047), ap(c1536))], w, True, False), [ownt[c], c1536, I, dm2047], s0)
-            m1 = mm(turn(ps[s0], rotm, low, False, False), [low, rotm], s0, [m0])
-            mm(turn(ps[s0], rotc, cq, False, True), [cq, rotc], s0, [m1])
-            ts(ap(lr), dv, -1.0, None, ALU.add, None, (), [lr], w, banks=[s0])
-            extra = [(ap(I), ap(g2, k0, k0 + w))]
-            erd = [g2, I]
+            lin("cq", ap(cq), ap(low), 1 / 128, 1536, [low], [cq], wp, 0.5)
+            dv = ps[s0][:, 128:128 + w]
+            terms(dv, [(diag(-D), owns[c], ap(owns[c], 0, w)), (diag(132 - 2047), c1536, ap(c1536, 0, w))], w, True, False, s0)
+            mm(turn(s0, 128, w, rotm, low, False), [low, rotm], s0)
+            mm(turn(s0, 128, w, rotc, cq, True), [cq, rotc], s0)
+            lin("lr", ap(lr), dv, 1, -1, (), [lr], w, banks=[s0])
+            one_ = I if rnd < 2 else diag(OFF)
+            extra = [(ap(one_), ap(fl, 0, w))]
+            erd = [fl[3] + "g", one_]
             if rnd > 0:
                 ne = new("pb", w)
                 tt(ap(ne), dv, ap(S["one"]), ALU.not_equal, [S["one"]], [ne], w, 1.0, banks=[s0])
-                extra.append((ap(I), ap(ne)))
+                extra.append((ap(one_), ap(ne)))
                 erd.append(ne)
             if rnd == 2:
-                du, dw = new("pf", w), new("pf", w)
-                tt(ap(du), dv, ap(S["has"]), ALU.mult, [S["has"]], [du], w, 1.0, banks=[s0])
-                tt(ap(dw), dv, ap(du), ALU.subtract, [du], [dw], w, 1.0, banks=[s0])
-            S["g2"].append(g2)
-            lraw = ps[s0][:, 64:64 + 2 * w]
-
-            def steps(out, coef, last):
-                tm, rd = [], []
-                for x in S["g2"]:
-                    for v in parts(coef):
-                        tm.append((out, ap(diag(v, "pb")), ap(x, k0, k0 + w), False, False, w))
-                        rd += [diag(v, "pb"), x]
-                for x in S["k"][:last]:
-                    tm.append((out, ap(diag(-coef, "ph")), ap(x), False, False, w))
-                    rd += [diag(-coef, "ph"), x]
-                return tm, rd
-            if rnd < 2:
-                ta_, ra_ = steps(ps[s0][:, 64:64 + w], K5, rnd)
-                tb_, rb_ = steps(ps[s0][:, 64 + w:64 + 2 * w], KH, rnd)
-                pre = mm([(lraw, ap(Ih), ap(bsh[c]), True, False, 2 * w)] + ta_ + tb_, ra_ + rb_ + [bsh[c], Ih], s0)
+                da, db = new("pf", w), new("pf", w)
+                tt(ap(da), dv, ap(S["ha"]), ALU.add, [S["ha"]], [da], w, 1.0, banks=[s0])
+                tt(ap(db), dv, ap(S["hb"]), ALU.add, [S["hb"]], [db], w, 1.0, banks=[s0])
+            else:
+                lraw = ps[s0][:, 192:192 + 2 * w]
+                z = new("pb", 2 * w)
+                for b, at in ((s1, 256), (s0, 192)):
+                    tm, rd = [(ps[b][:, at:at + 2 * w], ap(I), ap(bsh[c]), True, False, 2 * w)], [bsh[c], bsh[c][3] + "a", I]
+                    for n_, f in enumerate(S["fl"]):
+                        for y, (go, back) in enumerate(((K5, B - K5), (KH, H - KH))):
+                            o_ = ps[b][:, at + y * w:at + (y + 1) * w]
+                            tm.append((o_, ap(diag(go)), ap(f, 0, w), False, False, w))
+                            rd += [diag(go), f[3] + "g"]
+                            if n_ < rnd:
+                                tm.append((o_, ap(diag(back)), ap(f, w, 2 * w), False, False, w))
+                                rd += [diag(back), f]
+                    if b == s1:
+                        mm(tm[:-1] + [tm[-1][:4] + (True, w)], rd, b)
+                        lin("mod", ap(z), ps[b][:, at:at + 2 * w], 1 / B, 191.5 + 1 / 4096, (), [z], 2 * w, banks=[b])
+                    else:
+                        mm(tm + [(lraw, ap(diag(-B)), ap(z), False, False, 2 * w)], rd + [diag(-B), z], b)
             a, n = 128 * b0, 16 * w
-            tt(T.Ft[:, a:a + n], R[:].indirect(ap(lr)), T.nds[:, a:a + n], ALU.is_ge, Rr + [lr, "nds"], ["Ft%d" % c], n, gather=True)
-            m0 = mm(group(ps[s1][:, 0:w], extra, w, True, False), erd, s1)
-            mm(group(ps[s1][:, 0:w], [(ap(pick, 15 - i, 143 - i), T.Ft[:, a + i:a + n:16]) for i in range(16)], w, False, True),
-               ["Ft%d" % c, pick], s1, [m0])
-            k = new("ph", w)
-            ts(ap(k), ps[s1][:, 0:w], 17.5 if rnd == 0 else 18.5, None, ALU.is_ge, None, (), [k], w, banks=[s1])
-            S["k"].append(k)
+            tt(T.Ft[:, a:a + n], R[:].indirect(ap(lr)), ap(nds, a, a + n), ALU.is_ge, Rr + [lr, nds], ["Ft%d" % c], n, gather=True)
+            cnt = ps[s1][:, 0:w]
+            pk = pick if rnd < 2 else pickb
+            mm(group(cnt, extra, w, True, False), erd, s1)
+            mm(group(cnt, [(ap(pk, 15 - i, 143 - i), T.Ft[:, a + i:a + n:16]) for i in range(16)], w, False, True), ["Ft%d" % c, pk], s1)
             if rnd < 2:
-                mm([(ps[s0][:, 64:64 + w], ap(diag(-K5, "ph")), ap(k), False, False, w),
-                    (ps[s0][:, 64 + w:64 + 2 * w], ap(diag(-KH, "ph")), ap(k), False, True, w)],
-                   [k, diag(-K5, "ph"), diag(-KH, "ph")], s0, [pre])
-                li, lm, l1 = new("pi", 2 * w), new("pi", 2 * w), new("pu", 2 * w)
-                cp(ap(li), lraw, (), [li], 2 * w, banks=[s0])
-                ts(ap(lm), ap(li), B - 1, None, ALU.bitwise_and, None, [li], [lm], 2 * w)
-                cp(ap(l1), ap(lm).indirect(ap(lperm2, 0, 5)), [lm, lperm2], [l1], 2 * w, gather=True)
-                lists[c] = l1
-                tm, rd = steps(ps[s1][:, 64:64 + w], K3, rnd + 1)
-                tm[-1] = tm[-1][:4] + (True, w)
-                mm([(ps[s1][:, 64:64 + w], ap(Ih), ap(salh, k0, k0 + w), True, False, w)] + tm, rd + [salh, Ih], s1)
-                x = new("pf", w)
-                tt(ap(x), dv, ap(k), ALU.mult, [k], [x], w, 1.0, banks=[s0])
+                k = ap(fl, w, 2 * w)
+                if ENG["k"] == "a":
+                    act(k, cnt, -17.0 - rnd, (), [fl], w, banks=[s1], func=AF.Relu)
+                else:
+                    ts(k, cnt, 17.5 + rnd, None, ALU.is_ge, None, (), [fl], w, banks=[s1])
+                mm([(ps[s0][:, 192 + y * w:192 + (y + 1) * w], ap(diag(back)), k, False, y == 1, w) for y, back in enumerate((B - K5, H - KH))],
+                   [fl, diag(B - K5), diag(H - KH)], s0)
+                l1, fb, x = new("pu", 2 * w), new("pb", 2 * w), new("pf", w)
+                lin("l1", ap(l1), lraw, 1, 192 * B, (), [l1], 2 * w, banks=[s0])
+                lists[c] = ((l1, 0), (l1, w))
+                tt(ap(x), dv, k, ALU.mult, [fl], [x], w, 1.0, banks=[s0])
+                y, ya = lref(2 * w)
+                act(ap(fb), ap(fl).indirect(ya), 0.0, [fl, fl[3] + "g", y], [fb], 2 * w, gather=True)
+                S["fb"].append(fb)
             if rnd == 0:
                 S["one"] = x
             elif rnd == 1:
-                two, sm, one, tk_, has, om, tm_ = new("pf", w), new("pf", w), new("pf", w), new("pb", w), new("pb", w), new("pf", w), new("pf", w)
-                tt(ap(two), ap(x), ap(S["k"][0]), ALU.mult, [x, S["k"][0]], [two], w)
+                two, sm, one, has, om, tm_, ha_, hb_ = [new("pf", w) for _ in range(8)]
+                tk_ = new("pb", w)
+                tt(ap(two), ap(x), ap(S["fl"][0], w, 2 * w), ALU.mult, [x, S["fl"][0]], [two], w)
                 tt(ap(sm), ap(x), ap(S["one"]), ALU.add, [x, S["one"]], [sm], w)
                 tt(ap(one), ap(sm), ap(two), ALU.subtract, [sm, two], [one], w)
                 ts(ap(tk_), ap(two), 0.0, None, ALU.is_equal, None, [two], [tk_], w)
                 act(ap(has), ap(one), 0.0, [one], [has], w, func=AF.Sign)
+                act(ap(ha_), ap(has), -1.0, [has], [ha_], w, scale=-OFF)
+                act(ap(hb_), ap(has), -1.0 - OFF, [has], [hb_], w, scale=OFF)
                 act(ap(om), ap(one), -1.0, [one], [om], w)
                 act(ap(tm_), ap(two), -1.0, [two], [tm_], w)
-                S.update({"one": one, "takes": tk_, "has": has, "om": om, "tm": tm_})
+                S.update({"one": one, "takes": tk_, "ha": ha_, "hb": hb_, "om": om, "tm": tm_})
             else:
-                for n_, (dd, old, out) in enumerate([(dw, S["om"], T.ya), (du, S["tm"], T.yb)]):
+                for n_, (dd, old, out) in enumerate([(da, S["om"], T.ya), (db, S["tm"], T.yb)]):
                     u, y = new("pf", w), new("pf", w)
-                    tt(ap(u), ap(dd), ap(k), ALU.mult, [dd, k], [u], w)
-                    tt(ap(y), ap(u), ap(old), ALU.add, [u, old], [y], w)
+                    tt(ap(u), cnt, ap(dd), ALU.add, [dd], [u], w, 1.0, banks=[s1])
+                    tt(ap(y), ap(u), ap(old), ALU.max, [u, old], [y], w)
                     dma("sa"[n_], out[:, k0:k0 + w], ap(y), [y], ["out%d%d" % (c, n_)], 2000)
 
-    n = len(ops)
-    order = list(ORDER)
-    if len(order) != n:
-        succ = [[] for _ in ops]
-        for i, o_ in enumerate(ops):
-            o_["all"] = o_["deps"] | o_["after"]
-            o_["wait"] = o_["lat"] * (OPT["xl"] if o_["e"] is None else 1.0)
-            for d_ in o_["all"]:
-                succ[d_].append(i)
-        prio = [0.0] * n
-        for i in range(n - 1, -1, -1):
-            prio[i] = ops[i]["cost"] + ops[i]["wait"] + max([prio[s] + LAT for s in succ[i]] + [0.0])
-        for i in range(n):
-            prio[i] += ops[i]["lead"]
-        left = [len(o_["all"]) for o_ in ops]
-        ready = [i for i in range(n) if left[i] == 0]
-        free = {e: 0.0 for e in queue}
-        rdy, order = [0.0] * n, []
-        while ready:
-            est = {i: max(rdy[i], free.get(ops[i]["e"], 0.0)) for i in ready}
-            i0 = min(ready, key=lambda i: (est[i], i))
-            near = [i for i in ready if ops[i]["e"] == ops[i0]["e"] and est[i] <= est[i0] + OPT["win"]]
-            i = max(near, key=lambda i: (prio[i], -i)) if ops[i0]["e"] in ("v", "a", "p") else min(near)
-            o_ = ops[i]
-            if o_["e"] is not None:
-                free[o_["e"]] = est[i] + o_["cost"]
-            order.append(i)
-            ready.remove(i)
-            for s in succ[i]:
-                rdy[s] = max(rdy[s], est[i] + o_["cost"] + o_["wait"] + (LAT if i in ops[s]["deps"] else 0.0))
-                left[s] -= 1
-                if left[s] == 0:
-                    ready.append(s)
-    PLAN[me] = [(ops[i]["e"], ops[i]["c4"], ops[i]["lat"], ops[i]["deps"], ops[i]["after"], i) for i in order]
+    if PLAN.get("n") != len(ops):
+        PLAN["n"] = len(ops)
+        PLAN["order"], PLAN["times"] = make_order(ops, OPT)
+    order = PLAN["order"]
 
     count = {e: 0 for e in queue}
     known = {e: {} for e in queue}

@@ -9,15 +9,17 @@ KH = (KT + K5) % H
 W = O // 16
 TRI = 88
 RAW = D - 3 * TRI
-FW = B // N + TRI
+PIECE = {"n": (0, 128 + TRI), "w": (2 * (128 + TRI), 256), "k": (2 * (128 + TRI) + 512, 128)}
+FW = 2 * sum(x[1] for x in PIECE.values())
 BIG = 1.5 * 2.0 ** 35
 GAP = 4096
 ALPHA = 4095 / 256
 OFF = 8192.0
 
 SCRATCH = {
-    "NB": ("sbuf", [128, (N - 1) * GAP + H], "bfloat16"), "R": ("sbuf", [128, N * D], "bfloat16"),
-    "F": ("sbuf", [128, N * 2 * FW], "float16"), "WK": ("sbuf", [128, 2 * B], "bfloat16"),
+    "wts": ("sbuf", [128, B + H], "bfloat16"), "kds": ("sbuf", [128, B + H], "bfloat16"), "nzs": ("sbuf", [128, H], "bfloat16"),
+    "nds": ("sbuf", [128, O], "bfloat16"), "N2": ("sbuf", [128, (N - 1) * GAP + H], "bfloat16"), "R": ("sbuf", [128, N * D], "bfloat16"),
+    "F": ("sbuf", [128, N * FW], "float16"), "W2": ("sbuf", [128, 2 * B], "bfloat16"), "KK": ("sbuf", [128, 2 * B], "bfloat16"),
     "N1": ("sbuf", [128, B + 336], "bfloat16"), "Wg": ("sbuf", [128, O], "bfloat16"), "Kg": ("sbuf", [128, O], "float16"),
     "A": ("sbuf", [128, O], "float16"), "Z": ("sbuf", [128, O], "float32"), "Ft": ("sbuf", [128, O], "bfloat16"),
     "Z9": ("sbuf", [128, 720], "float32"), "Rl": ("sbuf", [128, 720], "float32"),
@@ -27,19 +29,19 @@ SCRATCH = {
 for _b in range(8):
     SCRATCH["ps%d" % _b] = ("psum", [128, 512], "float32")
 SEMAPHORES = (["cv", "ca", "cp", "cg", "sent"] + ["d%d" % i for i in range(24)]
-              + ["%s%d" % (a, r) for a in ("f0_", "f1_", "r0_", "r1_") for r in range(N)])
+              + ["%s%d_%d" % (a, h, r) for a in "rsnwk" for h in range(2) for r in range(N)])
 
 OPT = {
     "chunks": [(0, (3, 2), (0, 1), 2, 3), (5, (3, 2), (4, 5), 6, 7)],
-    "spare": (3, 7), "count": 7,
+    "pack": (3, 7, 2, 6), "spare": (3, 7, 1, 5, 0, 4),
     "pairs": [[0, 0], [0, 0], [0, 0]],
-    "split": [1, 1, 1],
-    "eng": {"lb": "v", "iv": "v", "lh": "v", "lr": "v", "li": "v", "l1": "v", "cq": "a", "f0": "v", "f1": "v", "mu": "a",
-            "own": "v", "carry": "v", "mod": "a", "k": "v", "n00": "a", "n01": "a", "n02": "a", "n10": "a", "n11": "a", "n12": "a"},
-    "loads": ["raw", "tri", "nz", "wt", "kd", "nd", "wx", "kx"],
-    "sends": ["r", "f0", "f1", "h0", "h1", "hr"],
-    "times": [(0.83, 1.35, 0.42, 215.0, 215.0, 1.0), (1.2, 1.9, 0.6, 200.0, 200.0, 1.2), (0.95, 1.5, 0.48, 170.0, 150.0, 1.0)],
-    "tries": 3000, "seed": 12345, "lead": 3000.0, "slack": 0.02, "mirror": 3,
+    "split": [1, 1, 1], "cq": 1,
+    "loads": ["ra", "tri", "nz", "wt", "kd", "rb", "nd", "wx", "kx"], "early": 192,
+    "sends": [("r", 2200, 2400), ("n", 2500, 2800), ("w", 2700, 3300), ("k", 2300, 3000), ("N", 2100, 0), ("W", 2200, 0), ("s", 2700, 3000),
+              ("R", 2500, 0), ("S", 2200, 0)],
+    "direct": "k", "hand": "in",
+    "times": [(0.83, 1.35, 0.42, 215.0, 1.0), (1.2, 1.9, 0.6, 200.0, 1.2), (0.95, 1.5, 0.48, 200.0, 1.0)],
+    "tries": 9000, "seed": 12345, "lead": 3000.0, "slack": 0.02, "mirror": 3, "lean": 1000.0,
 }
 PLAN = {}
 
@@ -47,84 +49,77 @@ PLAN = {}
 def make_order(ops, opt):
     n = len(ops)
     pre = [sorted(o["deps"] | o["after"]) for o in ops]
-    succ = [[] for _ in ops]
-    for i in range(n):
-        for d in pre[i]:
-            succ[d].append(i)
     sets = []
-    for cy, ga, pc, hop, same, xl in opt["times"]:
-        cost = [o["c4"][0] + cy * (o["c4"][1] + ga * o["c4"][2]) + pc * o["c4"][3] for o in ops]
-        lat = [o["lat"] * (xl if o["e"] is None else 1.0) for o in ops]
-        gap = [[(-lat[d] if d not in ops[i]["deps"] else same if ops[d]["e"] == ops[i]["e"] and ops[d]["sem"] is None
-                 else hop) for d in pre[i]] for i in range(n)]
-        sets.append((cost, lat, gap))
-    eng = [o["e"] for o in ops]
+    for cy, ga, pc, hop, xl in opt["times"]:
+        cost = [[c[0] + cy * (c[1] + ga * c[2]) + pc * c[3] for _, _, c in o["alt"]] for o in ops]
+        lat = [o["lat"] * (xl if o["alt"][0][0] is None else 1.0) for o in ops]
+        fore = [[(d, lat[d] + hop if d in ops[i]["deps"] else 0.0) for d in pre[i]] for i in range(n)]
+        back = [[] for _ in ops]
+        for i in range(n):
+            for d, x in fore[i]:
+                back[d].append((i, x))
+        sets.append((cost, lat, fore, back))
+    engs = [[a[0] for a in o["alt"]] for o in ops]
 
-    def replay(order, s):
-        cost, lat, gap = sets[s]
-        end, free = [0.0] * n, {}
+    def replay(order, pick, s):
+        cost, lat, fore, back = sets[s]
+        end, free, last = [0.0] * n, {}, 0.0
         for i in order:
-            t = free.get(eng[i], 0.0)
-            for d, x in zip(pre[i], gap[i]):
+            e = engs[i][pick[i]]
+            t = free.get(e, 0.0)
+            for d, x in fore[i]:
                 if end[d] + x > t:
                     t = end[d] + x
-            if eng[i] is not None:
-                free[eng[i]] = t + cost[i]
-            end[i] = t + cost[i] + lat[i]
-        return max(end), end
+            t += cost[i][pick[i]]
+            if e is not None:
+                free[e] = t
+            end[i] = t
+            if t + lat[i] > last:
+                last = t + lat[i]
+        return last
 
-    def place(seq, s, back):
-        cost, lat, gap = sets[s]
-        start, end, busy = [0.0] * n, [0.0] * n, {}
+    def place(seq, pick, s, mirrored, lean):
+        cost, lat, fore, back = sets[s]
+        need = back if mirrored else fore
+        start, end, busy, pick = [0.0] * n, [0.0] * n, {e: [] for e in "vapsg"}, list(pick)
         for i in seq:
-            t = 0.0
-            if back:
-                for j, x in after_[s][i]:
-                    if end[j] + x > t:
-                        t = end[j] + x
-                t += lat[i]
-            else:
-                for d, x in zip(pre[i], gap[i]):
-                    if end[d] + x > t:
-                        t = end[d] + x
-            if eng[i] is not None:
-                l = busy.setdefault(eng[i], [])
-                k = len(l)
-                while k > 0 and l[k - 1][1] > t:
-                    k -= 1
-                while k < len(l) and l[k][0] < t + cost[i]:
-                    t = max(t, l[k][1])
-                    k += 1
-                l.insert(k, (t, t + cost[i]))
-            start[i] = t
-            end[i] = t + cost[i] + (0.0 if back else lat[i])
-        return start, end
+            t0 = lat[i] if mirrored else 0.0
+            for d, x in need[i]:
+                if end[d] + x > t0:
+                    t0 = end[d] + x
+            best = None
+            for a in (range(len(engs[i])) if lean and lean[i] is not None else (pick[i],)):
+                e, c, t, k = engs[i][a], cost[i][a], t0, 0
+                if e is not None:
+                    l = busy[e]
+                    k = len(l)
+                    while k > 0 and l[k - 1][1] > t:
+                        k -= 1
+                    while k < len(l) and l[k][0] < t + c:
+                        if l[k][1] > t:
+                            t = l[k][1]
+                        k += 1
+                y = t + c + (lean[i] if a and lean and lean[i] is not None else 0.0)
+                if best is None or y < best[0]:
+                    best = (y, a, e, t, c, k)
+            y, a, e, t, c, k = best
+            if e is not None:
+                busy[e].insert(k, (t, t + c))
+            pick[i], start[i], end[i] = a, t, t + c
+        return start, end, pick
 
-    def sort(key, back):
-        need, nxt = (succ, pre) if back else (pre, succ)
-        left = [len(x) for x in need]
-        ready, seq = [i for i in range(n) if not left[i]], []
-        while ready:
-            i = min(ready, key=lambda j: (key[j], j))
-            ready.remove(i)
-            seq.append(i)
-            for j in nxt[i]:
-                left[j] -= 1
-                if not left[j]:
-                    ready.append(j)
-        return seq
+    def sort(key, mirrored):
+        need, key = sets[0][3 if mirrored else 2], list(key)
+        for i in (range(n - 1, -1, -1) if mirrored else range(n)):
+            for d, x in need[i]:
+                if key[d] >= key[i]:
+                    key[i] = key[d] + 0.001
+        return sorted(range(n), key=lambda i: key[i])
 
-    after_ = []
-    for cost, lat, gap in sets:
-        x = [[] for _ in ops]
-        for i in range(n):
-            for d, y in zip(pre[i], gap[i]):
-                x[d].append((i, y))
-        after_.append(x)
-    cost, lat, gap = sets[0]
+    cost, lat, fore, back = sets[0]
     tail = [0.0] * n
     for i in range(n - 1, -1, -1):
-        tail[i] = cost[i] + lat[i] + max([tail[j] + x for j, x in after_[0][i]] + [0.0])
+        tail[i] = cost[i][0] + max([tail[j] + x for j, x in back[i]] + [lat[i]])
     PLAN["tail"] = tail
     seed, best, ref, cur = [opt["seed"]], None, None, None
 
@@ -132,31 +127,33 @@ def make_order(ops, opt):
         seed[0] = (seed[0] * 1103515245 + 12345) % 2 ** 31
         return seed[0] / 2 ** 31
 
-    key = [-tail[i] - opt["lead"] * ops[i]["lead"] for i in range(n)]
+    key, pick, lean = [-tail[i] - opt["lead"] * ops[i]["lead"] for i in range(n)], [o["first"] for o in ops], None
     for k in range(opt["tries"]):
         s = k % len(sets)
-        start, end = place(sort(key, False), s, False)
+        start, end, pick = place(sort(key, False), pick, s, False, lean)
         for again in range(2):
             order = sort(start, False)
-            ts_ = [replay(order, y)[0] for y in range(len(sets))]
+            ts_ = [replay(order, pick, y) for y in range(len(sets))]
             ref = ref or ts_
             score = sum(a / b for a, b in zip(ts_, ref))
             if best is None or score < best[0]:
-                best = (score, order, ts_, start)
+                best = (score, order, ts_, pick)
             if cur is None or score < cur[0] + opt["slack"] * (1.0 - k / opt["tries"]) * rnd():
-                cur = (score, start)
+                cur = (score, start, pick)
             if again or k % opt["mirror"]:
                 break
-            bs, be = place(sort([-x for x in end], True), s, True)
-            start, end = place(sort([-x for x in be], False), s, False)
-        size, span = 2500.0 * rnd() ** 3 + 50.0, 12000.0 * rnd()
+            bs, be, _ = place(sort([-x for x in end], True), pick, s, True, None)
+            start, end, pick = place(sort([-x for x in be], False), pick, s, False, None)
+        size, span = 2500.0 * rnd() ** 3 + 50.0, 12000.0 * rnd() ** 2
         lo = rnd() * max(cur[1]) - span / 2
-        shift, who = size * (2 * rnd() - 1), float(k % 2)
+        shift, who, pick, lean = size * (2 * rnd() - 1), float(k % 2), cur[2], None
         if k % 3:
             key = [x + (size * rnd() if lo <= x <= lo + span else 0.0) for x in cur[1]]
         else:
             key = [x + (shift if lo <= x <= lo + span and o["lead"] == who else 0.0) for x, o in zip(cur[1], ops)]
-    return best[1], best[2]
+        if k % 4 == 0:
+            lean = [opt["lean"] * (rnd() - 0.1) if lo <= x <= lo + span and rnd() < 0.5 else None for x in cur[1]]
+    return best[1], best[3], best[2]
 
 
 def rank_program(g, core, T, topo):
@@ -172,7 +169,7 @@ def rank_program(g, core, T, topo):
     used = {"pi": 0, "pf": 0, "pb": 0, "ph": 0, "pu": 0}
     ndma, tok, lead = [0], [0], [0.0]
     PLAN["ops"] = ops
-    CH, ENG = OPT["chunks"], OPT["eng"]
+    CH = OPT["chunks"]
 
     def new(pool, n):
         a = used[pool]
@@ -184,7 +181,7 @@ def rank_program(g, core, T, topo):
         b = x[2] if b is None else b
         return x[0][:, x[1] + a:x[1] + b:s] if s != 1 else x[0][:, x[1] + a:x[1] + b]
 
-    def op(eng, fn, rd=(), wr=(), banks=(), cost=(55.0, 0, 0, 0), lat=0.0, sem=None, after=()):
+    def op(eng, fn, rd=(), wr=(), banks=(), cost=(55.0, 0, 0, 0), lat=0.0, sem=None, after=(), alt=(), first=0):
         i = len(ops)
         deps = set()
         for t in rd:
@@ -201,12 +198,13 @@ def rank_program(g, core, T, topo):
             readers[t] = []
         for b in banks:
             e, cur, prev = bank.get(b, (None, [], []))
-            if e != eng:
-                e, cur, prev = eng, [], cur
+            if e != eng or alt:
+                e, cur, prev = (i if alt else eng), [], cur
             deps.update(prev)
             bank[b] = (e, cur + [i], prev)
         deps.discard(i)
-        ops.append({"e": eng, "fn": fn, "deps": deps, "c4": cost, "lat": lat, "sem": sem, "after": set(after), "lead": lead[0], "tag": (tuple(wr), tuple(banks))})
+        ops.append({"alt": [(eng, fn, cost)] + list(alt), "deps": deps, "lat": lat, "sem": sem, "after": set(after), "lead": lead[0],
+                    "first": first, "tag": (tuple(wr), tuple(banks))})
         return i
 
     def vc(n, c=1.0, f=0.0):
@@ -225,23 +223,25 @@ def rank_program(g, core, T, topo):
     def tt(out, in0, in1, o, rd, wr, n, c=2.0, banks=(), gather=False):
         return op("v", lambda: g.vector.tensor_tensor(out, in0, in1, o), rd, wr, banks, gc_(n) if gather else vc(n, c))
 
-    def cp(out, in_, rd, wr, n, c=1.0, banks=(), gather=False):
-        return op("v", lambda: g.vector.tensor_copy(out, in_), rd, wr, banks, gc_(n) if gather else vc(n, c))
-
     def fill(out, v, wr, n):
         return op("v", lambda: g.vector.memset(out, v), (), wr, cost=vc(n))
 
     def scan(out, d0, d1, o0, o1, rd, wr, n, c=1.0, banks=()):
         return op("v", lambda: g.vector.tensor_tensor_scan(out, d0, d1, 0.0, o0, o1), rd, wr, banks, vc(n, c))
 
-    def act(out, in_, bias, rd, wr, n, banks=(), gather=False, func=AF.Identity, scale=1.0):
-        return op("a", lambda: g.scalar.activation(out, in_, func, bias=bias, scale=scale), rd, wr, banks,
-                  gc_(n, 65.0) if gather else vc(n, 1.0, 30.0))
+    def act(out, in_, bias, rd, wr, n, func, banks=(), scale=1.0):
+        return op("a", lambda: g.scalar.activation(out, in_, func, bias=bias, scale=scale), rd, wr, banks, vc(n, 1.0, 30.0))
 
-    def lin(name, out, in_, mul, add, rd, wr, n, c=1.0, banks=(), gather=False):
-        if ENG[name] == "a":
-            return act(out, in_, float(add), rd, wr, n, banks, gather, scale=float(mul))
-        return ts(out, in_, float(mul), float(add), ALU.mult, ALU.add, rd, wr, n, c, banks, gather)
+    def lin(out, in_, mul, add, rd, wr, n, c=1.0, banks=(), gather=False, on="a", cut=False):
+        mul, add = float(mul), float(add) if isinstance(add, (int, float)) else add
+        a = ("a", lambda: g.scalar.activation(out, in_, AF.Relu if cut else AF.Identity, bias=add, scale=mul),
+             gc_(n, 65.0) if gather else vc(n, 1.0, 30.0))
+        v = ("v", lambda: (g.vector.tensor_scalar(out, in_, add, 0.0, ALU.add, ALU.max) if cut else
+                           g.vector.tensor_scalar(out, in_, mul, add, ALU.mult, ALU.add)), gc_(n) if gather else vc(n, c))
+        if on in "AV":
+            x = a if on == "A" else v
+            return op(x[0], x[1], rd, wr, banks, x[2])
+        return op(a[0], a[1], rd, wr, banks, a[2], alt=[v], first=int(on == "v"))
 
     def mm(terms, rd, b):
         def fn():
@@ -255,6 +255,9 @@ def rank_program(g, core, T, topo):
     def group(out, pairs, n, start=True, stop=True):
         return [(out, l_, r_, start and i == 0, stop and i == len(pairs) - 1, n) for i, (l_, r_) in enumerate(pairs)]
 
+    def terms(out, tm, n, start, stop, b):
+        mm(group(out, [(ap(m), x) for m, _, x in tm], n, start, stop), [y for m, t, _ in tm for y in (m, t)], b)
+
     def dma(eng, out, in_, rd, wr, lat, after=()):
         s = "d%d" % ndma[0]
         ndma[0] += 1
@@ -262,16 +265,14 @@ def rank_program(g, core, T, topo):
 
     ps = [T["ps%d" % b] for b in range(8)]
     R, F = T.R, T.F
-    q = B // N
-    f0 = me * 2 * FW
-    rt = me * D + RAW
+    rt, RA = me * D + RAW, OPT["early"]
 
     beg, sal = new("pi", W), new("pi", W)
-    wts, kds = (T.NB, H, GAP - H, "wts"), (T.NB, GAP + H, GAP - H, "kds")
-    nzs, nds = (T.NB, 2 * GAP + H, H, "nzs"), (T.NB, 2 * GAP + 2 * H, O, "nds")
-    fill(T.NB[:, 2 * GAP + 2 * H + O:3 * GAP], 0.0, ["rest"], (GAP - 2 * H - O) // 2)
+    wts, kds = (T.wts, 0, B + H, "wts"), (T.kds, 0, B + H, "kds")
+    nzs, nds = (T.nzs, 0, H, "nzs"), (T.nds, 0, O, "nds")
     loads = {"tri": (R[:, rt:rt + 3 * TRI], T.room[:, RAW:D], ["Rt%d" % me], 3 * TRI),
-             "raw": (R[:, me * D:rt], T.room[:, 0:RAW], ["Rraw0_%d" % me, "Rraw1_%d" % me], RAW),
+             "ra": (R[:, me * D:me * D + RA], T.room[:, 0:RA], ["r0_%d" % me, "r1_%d" % me], RA),
+             "rb": (R[:, me * D + RA:rt], T.room[:, RA:RAW], ["s0_%d" % me, "s1_%d" % me], RAW - RA),
              "nz": (ap(nzs), T.noise[:], [nzs], H), "wt": (ap(wts, 0, B), T.wt[:], [wts], B), "kd": (ap(kds, 0, B), T.kid[:], [kds], B),
              "nd": (ap(nds), T.need[:], [nds], O), "wx": (ap(wts, B, B + H), T.wt[:, 0:H], ["wx"], H),
              "kx": (ap(kds, B, B + H), T.kid[:, 0:H], ["kx"], H)}
@@ -292,43 +293,39 @@ def rank_program(g, core, T, topo):
         op("g", lambda: g.iota(ap(pu_), [[-16, 8], [-2, 9]], 0, 1), (), [pu_], cost=(270.0, 0, 0, 0))
     mum, lmu = new("pi", 64), new("pu", 64)
     ts(ap(mum), ap(mui), H - 1, None, ALU.bitwise_and, None, [mui], [mum], 64)
-    cp(ap(lmu), ap(mum), [mum], [lmu], 64)
+    lin(ap(lmu), ap(mum), 1, 0, [mum], [lmu], 64)
     pcol, gcol, gneg = new("pf", 1), new("pf", 1), new("pf", 1)
     plo, phi = new("pi", 8), new("pi", 8)
-    cp(ap(pcol), ap(prt, 0, 1), [prt], [pcol], 1)
+    lin(ap(pcol), ap(prt, 0, 1), 1, 0, [prt], [pcol], 1)
     ts(ap(plo), ap(prt), 15, None, ALU.bitwise_and, None, [prt], [plo], 8)
     ts(ap(phi), ap(prt), 4, None, ALU.logical_shift_right, None, [prt], [phi], 8)
-    ts(ap(gcol), ap(phi, 0, 1), 16.0, 15.0, ALU.mult, ALU.add, [phi], [gcol], 1)
-    ts(ap(gneg), ap(phi, 0, 1), -16.0, float(H), ALU.mult, ALU.add, [phi], [gneg], 1)
+    lin(ap(gcol), ap(phi, 0, 1), 16, 15, [phi], [gcol], 1)
+    lin(ap(gneg), ap(phi, 0, 1), -16, H, [phi], [gneg], 1)
     wide1 = new("pb", 240)
     ts(ap(wide1, 0, 128), ap(col, 0, 128), ap(pcol), None, ALU.is_equal, None, [col, pcol], [wide1], 128)
-    cp(ap(wide1, 128, 240), ap(wide1, 0, 112), [wide1], ["wide1b"], 112, 0.5)
+    lin(ap(wide1, 128, 240), ap(wide1, 0, 112), 1, 0, [wide1], ["wide1b"], 112, 0.5, on="v")
     consts = {(1, 128): wide1[:2] + (128, wide1[3])}
 
-    def diag(v, wide=128, eng="a"):
+    def diag(v, wide=128):
         if (v, wide) not in consts:
-            m = abs(v)
+            m = abs(v) * 4096
             while m % 2 == 0:
                 m //= 2
-            x = new("pb" if m < 256 and m == int(m) else "ph", wide)
-            rd = [wide1, "wide1b"][:1 + (wide > 128)]
-            if eng == "a":
-                act(ap(x), ap(wide1, 0, wide), 0.0, rd, [x], wide, scale=float(v))
-            else:
-                ts(ap(x), ap(wide1, 0, wide), float(v), None, ALU.mult, None, rd, [x], wide, 0.5)
+            x = new("pb" if m < 256 else "ph", wide)
+            lin(ap(x), ap(wide1, 0, wide), v, 0, [wide1, "wide1b"][:1 + (wide > 128)], [x], wide, 0.5)
             consts[(v, wide)] = x
         return consts[(v, wide)]
 
     pick, pickb = new("pb", 144), new("pb", 144)
     ts(ap(pick), ap(col), ap(gcol), None, ALU.is_equal, None, [col, gcol], [pick], 144)
-    act(ap(pickb), ap(pick), 0.0, [pick], [pickb], 144, scale=OFF)
+    lin(ap(pickb), ap(pick), OFF, 0, [pick], [pickb], 144, 0.5)
     j_, r_, m8, t1, t2, ta, tb, rx = [new("pi", 8) for _ in range(8)]
-    ts(ap(t1), ap(col, 0, 8), 16.0, None, ALU.mult, None, [col], [t1], 8)
+    lin(ap(t1), ap(col, 0, 8), 16, 0, [col], [t1], 8)
     tt(ap(j_), ap(t1), ap(plo), ALU.add, [t1, plo], [j_], 8)
     ts(ap(r_), ap(j_), 7, None, ALU.bitwise_and, None, [j_], [r_], 8)
     tt(ap(m8), ap(j_), ap(r_), ALU.subtract, [j_, r_], [m8], 8)
     tt(ap(t2), ap(phi), ap(r_), ALU.subtract, [phi, r_], [t2], 8)
-    ts(ap(ta), ap(t2), 8.0, None, ALU.add, None, [t2], [ta], 8)
+    lin(ap(ta), ap(t2), 1, 8, [t2], [ta], 8)
     ts(ap(tb), ap(ta), 7, None, ALU.bitwise_and, None, [ta], [tb], 8)
     tt(ap(rx), ap(tb), ap(m8), ALU.add, [tb, m8], [rx], 8)
     mirror = {}
@@ -344,7 +341,7 @@ def rank_program(g, core, T, topo):
             else:
                 ts(ap(a), ap(rx), float(w - 1), None, ALU.min, None, [rx], [a], 8)
             if mul != 1:
-                ts(ap(b), ap(a), float(mul), float(add), ALU.mult, ALU.add, [a], [b], 8)
+                lin(ap(b), ap(a), mul, add, [a], [b], 8)
             mirror[(w, mul, twice)] = b
         x = mirror[(w, mul, twice)]
         return x, ap(x, 0, ((1 + twice) * w + 15) // 16)
@@ -357,18 +354,18 @@ def rank_program(g, core, T, topo):
     fill(ap(c1536), 1536.0, [c1536], 64)
     bon = [new("pf", 1), new("pf", 1)]
     for x, step, v in zip(bon, (256.0, 128.0), (-2047.0, -160.0)):
-        ts(ap(x), ap(plo, 0, 1), -step, 15 * step + v, ALU.mult, ALU.add, [plo], [x], 1)
+        lin(ap(x), ap(plo, 0, 1), -step, 15 * step + v, [plo], [x], 1)
     blk, tri, ta, tb, tc, td = new("pb", 128), new("pb", 128), new("pi", 128), new("pf", 1), new("pb", 128), new("pb", 128)
     ts(ap(ta), ap(col, 0, 128), 4, None, ALU.logical_shift_right, None, [col], [ta], 128)
-    cp(ap(tb), ap(phi, 0, 1), [phi], [tb], 1)
+    lin(ap(tb), ap(phi, 0, 1), 1, 0, [phi], [tb], 1)
     ts(ap(blk), ap(ta), ap(tb), None, ALU.is_equal, None, [ta, tb], [blk], 128)
     ts(ap(tc), ap(col, 0, 128), ap(pcol), -1.0, ALU.is_lt, ALU.mult, [col, pcol], [tc], 128)
     tt(ap(td), ap(tc), ap(blk), ALU.mult, [tc, blk], [td], 128)
     d512 = diag(-512)
     tt(ap(tri), ap(td), ap(d512), ALU.add, [td, d512], [tri], 128)
     nblk, ntri = new("pb", 128), new("pb", 128)
-    act(ap(nblk), ap(blk), 0.0, [blk], [nblk], 128, scale=-1.0)
-    act(ap(ntri), ap(tri), 0.0, [tri], [ntri], 128, scale=-1.0)
+    lin(ap(nblk), ap(blk), -1, 0, [blk], [nblk], 128, 0.5)
+    lin(ap(ntri), ap(tri), -1, 0, [tri], [ntri], 128, 0.5)
     sgn, run, rst = [], [], []
     for c, ch in enumerate(CH):
         u = 8 * sum(ch[1]) + 1
@@ -394,62 +391,68 @@ def rank_program(g, core, T, topo):
         tt(ap(MK, 0, 72), ap(e1), ap(e0), ALU.subtract, [e0, e1], ["MKa"], 72)
         tt(ap(MK, 72, 144), ap(em), ap(e0), ALU.subtract, [e0, em], [MK], 72)
         fill(ap(MK, 72, 144, 9), 0.0, [MK], 8)
-        act(ap(MW), ap(MK), 0.0, [MK, "MKa"], [MW], 144, scale=131072.0)
-        act(ap(MA), ap(MK), 0.0, [MK, "MKa"], [MA], 144, scale=4096.0)
-        ts(ap(MK, 72, 144, 9), ap(e0, 0, 72, 9), -32768.0, None, ALU.mult, None, [e0], [MK], 8)
+        lin(ap(MW), ap(MK), 131072, 0, [MK, "MKa"], [MW], 144, 0.5)
+        lin(ap(MA), ap(MK), 4096, 0, [MK, "MKa"], [MA], 144, 0.5)
+        lin(ap(MK, 72, 144, 9), ap(e0, 0, 72, 9), -32768, 0, [e0], [MK], 8)
 
     s1_, sm_, hb, hbm = new("pi", W), new("pi", W), new("pi", W), new("pi", W)
     lb0, lh0, salB = new("pu", W), new("pu", W), new("ph", W)
-    cp(ap(lb0), ap(beg), [beg], [lb0], W)
-    ts(ap(s1_), ap(sal), float(MU), ap(gneg), ALU.mult, ALU.add, [sal, gneg], [s1_], W)
+    lin(ap(lb0), ap(beg), 1, 0, [beg], [lb0], W)
+    lin(ap(s1_), ap(sal), MU, ap(gneg), [sal, gneg], [s1_], W)
     ts(ap(sm_), ap(s1_), H - 1, None, ALU.bitwise_and, None, [s1_], [sm_], W)
     tt(ap(hb), ap(sm_), ap(beg), ALU.add, [sm_, beg], [hb], W)
     ts(ap(hbm), ap(hb), H - 1, None, ALU.bitwise_and, None, [hb], [hbm], W)
-    cp(ap(lh0), ap(hbm), [hbm], [lh0], W)
+    lin(ap(lh0), ap(hbm), 1, 0, [hbm], [lh0], W)
     x, xa = lref(W)
-    cp(ap(salB), ap(sm_).indirect(xa), [sm_, x], [salB], W, gather=True)
+    lin(ap(salB), ap(sm_).indirect(xa), 1, 0, [sm_, x], [salB], W, gather=True)
     lists, bsh = [], []
     for b0, subs, kb, s0, s1 in CH:
         k0, w = 8 * b0, 8 * sum(subs)
         bh = new("ph", 2 * w)
-        cp(ap(bh, 0, w), ap(beg, k0, k0 + w), [beg], [bh[3] + "a"], w)
-        cp(ap(bh, w, 2 * w), ap(hbm, k0, k0 + w), [hbm], [bh], w)
+        lin(ap(bh, 0, w), ap(beg, k0, k0 + w), 1, 0, [beg], [bh[3] + "a"], w)
+        lin(ap(bh, w, 2 * w), ap(hbm, k0, k0 + w), 1, 0, [hbm], [bh], w)
         lists.append(((lb0, k0), (lh0, k0)))
         bsh.append(bh)
 
-    def nblock(r):
-        return (N - 1 - r) * GAP
-    mine = T.NB[:, nblock(me):nblock(me) + H]
-    for h in range(2):
-        lin("mu", T.NB[:, nblock(me) + h * q:nblock(me) + (h + 1) * q], ap(nzs).indirect(ap(lmu, 32 * h, 32 * h + 32)), 1, -32,
-            [nzs, lmu], ["N2_%d_%d" % (h, me)], q, gather=True)
+    def noise(r, a, b):
+        return T.N2[:, (N - 1 - r) * GAP + a:(N - 1 - r) * GAP + b]
 
-    I = diag(1)
-    pa, pb_ = OPT["spare"]
-    rch, big = new("pb", TRI), new("pb", q)
-    ts(ap(rch), R[:, rt + 2 * TRI:rt + 3 * TRI], 1 / 16, 160 - 7.5 / 16, ALU.mult, ALU.add, ["Rt%d" % me], [rch], TRI, 0.5)
-    d16, dm16, d64, dm64, d4096 = diag(16), diag(-16), diag(64), diag(-64), diag(4096)
-    pt = CH[0][3]
-    mm(group(ps[pt][:, 0:TRI], [(ap(d16), R[:, rt:rt + TRI]), (ap(I), ap(rch))], TRI)
-       + group(ps[pt][:, TRI:2 * TRI], [(ap(d16), R[:, rt + TRI:rt + 2 * TRI]), (ap(I), R[:, rt + 2 * TRI:rt + 3 * TRI]),
-                                        (ap(dm16), ap(rch))], TRI), ["Rt%d" % me, rch, d16, dm16, I], pt)
-    ts(F[:, f0 + q:f0 + FW], ps[pt][:, 0:TRI], -2208.0, None, ALU.add, None, (), ["F0t"], TRI, banks=[pt])
-    ts(F[:, f0 + FW + q:f0 + 2 * FW], ps[pt][:, TRI:2 * TRI], 512.0, None, ALU.add, None, (), ["F1t"], TRI, banks=[pt])
+    def ntok(r, parts=("w0", "w1", "h0", "h1", "l0", "l1")):
+        return ["N%s_%d" % (x, r) for x in parts]
+    for a, parts in ((512, ("h0", "h1", "l0", "l1")), (0, ("w0", "w1"))):
+        lin(noise(me, a, a + 512), ap(nzs).indirect(ap(lmu, a // 16, a // 16 + 32)), 1, -32, [nzs, lmu], ntok(me, parts), 512, gather=True)
+
+    def word(kind, h, r, a=0, b=None):
+        at, n = PIECE[kind]
+        at += r * FW + h * n
+        return F[:, at + a:at + (n if b is None else b)]
 
     def kids(r):
         return [r + N * j for j in range(16 // N)]
-
-    def blocks(b, mat, tab, step, cs, stop):
-        return [(ps[b][:, 128 * j:128 * (j + 1)], ap(mat), tab(c, step), False, stop and j == len(cs) - 1, 128) for j, c in enumerate(cs)]
-    n0 = nblock(me)
-    mm([(ps[pa][:], ap(I), T.NB[:, n0:n0 + q], True, False, q)], ["N2_0_%d" % me, I], pa)
-    mm(blocks(pa, d64, lambda c, s: ap(wts, c, B, s), 16, kids(me), True), [wts, d64], pa)
-    lin("f0", F[:, f0:f0 + q], ps[pa][:], 1, -2016, (), ["F0_%d" % me], q, banks=[pa])
-    ts(ap(big), ap(kds, me, B, N), 64.0, None, ALU.is_ge, None, [kds], [big], q, 0.5)
-    mm([(ps[pb_][:], ap(I), T.NB[:, n0 + q:n0 + 2 * q], True, False, q)], ["N2_1_%d" % me, I], pb_)
-    mm(blocks(pb_, dm64, lambda c, s: ap(kds, c, B, s), 16, kids(me), False), [kds, dm64], pb_)
-    mm(blocks(pb_, d4096, lambda c, s: ap(big, c, q, s), N, range(N), True), [big, d4096], pb_)
-    lin("f1", F[:, f0 + FW:f0 + FW + q], ps[pb_][:], 1, 2016, (), ["F1_%d" % me], q, banks=[pb_])
+    I = diag(1)
+    pn, pw, pt, pk_ = OPT["pack"]
+    rch, big = new("pb", TRI), new("pb", B // N)
+    lin(ap(rch), R[:, rt + 2 * TRI:rt + 3 * TRI], 1 / 16, 160 - 7.5 / 16, ["Rt%d" % me], [rch], TRI, 0.5, on="v")
+    d16, dm16, d64, dm64, d4096, dm1 = diag(16), diag(-16), diag(64), diag(-64), diag(4096), diag(-1)
+    mm(group(ps[pt][:, 0:TRI], [(ap(d16), R[:, rt:rt + TRI]), (ap(I), ap(rch))], TRI)
+       + group(ps[pt][:, TRI:2 * TRI], [(ap(d16), R[:, rt + TRI:rt + 2 * TRI]), (ap(I), R[:, rt + 2 * TRI:rt + 3 * TRI]),
+                                        (ap(dm16), ap(rch))], TRI), ["Rt%d" % me, rch, d16, dm16, I], pt)
+    for h, v in enumerate((-2208, 512)):
+        lin(word("n", h, me, 128), ps[pt][:, h * TRI:(h + 1) * TRI], 1, v, (), ["t%d_%d" % (h, me)], TRI, banks=[pt], on="V")
+    terms(ps[pn][:, 0:256], [(d64, "Nh0_%d" % me, noise(me, 512, 768)), (I, "Nl0_%d" % me, noise(me, 768, 1024))], 256, True, True, pn)
+    for h in range(2):
+        lin(word("n", h, me, 0, 128), ps[pn][:, 128 * h:128 * (h + 1)], 1, 32, (), ["n%d_%d" % (h, me)], 128, banks=[pn], on="V")
+    terms(ps[pw][:], [(I, "Nw0_%d" % me, noise(me, 0, 512))], 512, True, False, pw)
+    mm([(ps[pw][:, 128 * j:128 * (j + 1)], ap(d64), ap(wts, c, B, 16), False, j == 3, 128) for j, c in enumerate(kids(me))], [wts, d64], pw)
+    at = me * FW + PIECE["w"][0]
+    lin(F[:, at:at + 512], ps[pw][:], 1, -2016, (), ["w0_%d" % me, "w1_%d" % me], 512, banks=[pw], on="v")
+    ts(ap(big), ap(kds, me, B, N), 64.0, None, ALU.is_ge, None, [kds], [big], B // N, 0.5)
+    mm([(ps[pk_][:, 128 * (j % 2):128 * (j % 2 + 1)], ap(dm1 if j > 1 else dm64), ap(kds, c, B, 16), j == 0, False, 128)
+        for j, c in enumerate(kids(me))], [kds, dm64, dm1], pk_)
+    mm([(ps[pk_][:, 128 * (j % 2):128 * (j % 2 + 1)], ap(d64 if j > 1 else d4096), ap(big, j, B // N, N), False, j == 3, 128)
+        for j in range(N)], [big, d64, d4096], pk_)
+    at = me * FW + PIECE["k"][0]
+    lin(F[:, at:at + 256], ps[pk_][:, 0:256], 1, 2047, (), ["k0_%d" % me, "k1_%d" % me], 256, banks=[pk_], on="v")
 
     out_e = topo.engines(core, cores[far[0]])
     all_e = topo.engines(core, cores[mate])
@@ -457,9 +460,10 @@ def rank_program(g, core, T, topo):
     sent, gorder = [0], []
 
     def piece(kind, h, r):
-        if kind == "f":
-            return F[:, (2 * r + h) * FW:(2 * r + h + 1) * FW]
-        return R[:, r * D + h * (RAW // 2):r * D + (h + 1) * (RAW // 2)]
+        if kind in "rs":
+            a, n = (0, RA // 2) if kind == "r" else (RA, (RAW - RA) // 2)
+            return R[:, r * D + a + h * n:r * D + a + (h + 1) * n]
+        return word(kind, h, r)
 
     def send(items, rd):
         def fn():
@@ -471,83 +475,109 @@ def rank_program(g, core, T, topo):
             g.remote_dma_fused(tr, local_sem=T.sem.sent)
             return None
         sent[0] += sum(len(it[4]) for it in items)
-        i = op("g", fn, rd, (), cost=(500.0 if gorder else 1900.0, 0, 0, 0), sem="none", after=gorder[-1:])
+        i = op("g", fn, rd, (), cost=(400.0 if gorder else 1900.0, 0, 0, 0), sem="none", after=gorder[-1:])
         gorder.append(i)
         return i
 
     def arrive(kind, h, r, n, after, lat):
-        name = ("F%d_%d" if kind == "f" else "Rraw%d_%d") % (h, r)
-        return op(None, None, (), [name], cost=(0.0, 0, 0, 0), lat=lat, sem=("%s%d_%d" % (kind, h, r), n), after=[after])
+        name = "%s%d_%d" % (kind, h, r)
+        return op(None, None, (), [name], cost=(0.0, 0, 0, 0), lat=lat, sem=(name, n), after=[after])
 
-    ho, hi_, ha = len(out_e) // 2, len(in_e) // 2, len(all_e) // 2
-    for name in OPT["sends"]:
-        if name == "r":
-            i = send([("r", 0, me, far[0], out_e[:ho]), ("r", 1, me, far[1], out_e[ho:]), ("r", 0, me, mate, in_e[:hi_]),
-                      ("r", 1, me, mate, in_e[hi_:])], ["Rraw0_%d" % me])
+    def part(es, k, n):
+        return es[k * len(es) // n:(k + 1) * len(es) // n]
+    landed = []
+    for kind, near, away in OPT["sends"]:
+        if kind.islower():
+            rd = ["%s%d_%d" % (x, h, me) for x in (kind + "t" if kind == "n" else kind) for h in range(2)]
+            outs = [(h, f) for h in range(2) for f in range(2) if f == h or kind in OPT["direct"]]
+            i = send([(kind, h, me, far[f], part(out_e, n_, len(outs))) for n_, (h, f) in enumerate(outs)]
+                     + [(kind, h, me, mate, part(in_e, h, 2)) for h in range(2)], rd)
             for h in range(2):
-                arrive("r", h, mate, hi_, i, 3500)
-                arrive("r", h, far[h], ho, i, 4500)
-        elif name[0] == "f":
-            h = int(name[1])
-            i = send([("f", h, me, far[h], out_e), ("f", h, me, mate, in_e)], ["F%d_%d" % (h, me), "F%dt" % h])
-            arrive("f", h, mate, len(in_e), i, 2900)
-            arrive("f", h, far[h], len(out_e), i, 3300)
-        elif name == "hr":
-            i = send([("r", 0, far[0], mate, all_e[:ha]), ("r", 1, far[1], mate, all_e[ha:])], ["Rraw0_%d" % far[0], "Rraw1_%d" % far[1]])
-            for h in range(2):
-                last = arrive("r", h, far[1 - h], ha, i, 2400)
+                arrive(kind, h, mate, len(in_e) // 2, i, near)
+            for h, f in outs:
+                arrive(kind, h, far[f], len(out_e) // len(outs), i, away)
+            landed += [(kind, (0, 1), mate)] + ([(kind, (0, 1), f) for f in far] if kind in OPT["direct"] else
+                                                [(kind, (h,), far[h]) for h in range(2)])
         else:
-            h = int(name[1])
-            i = send([("f", h, far[h], mate, all_e)], ["F%d_%d" % (h, far[h])])
-            arrive("f", h, far[1 - h], len(all_e), i, 2200)
+            kind = kind.lower()
+            es = all_e if OPT["hand"] == "all" else in_e
+            i = send([(kind, h, far[h], mate, part(es, h, 2)) for h in range(2)], ["%s%d_%d" % (kind, h, far[h]) for h in range(2)])
+            for h in range(2):
+                arrive(kind, h, far[1 - h], len(es) // 2, i, near)
+            landed += [(kind, (h,), far[1 - h]) for h in range(2)]
     for h, n in enumerate((H, H, 336)):
-        dma("s", T.N1[:, h * H:h * H + n], T.NB[:, n0:n0 + n], ["N2_0_%d" % me, "N2_1_%d" % me, "Rraw0_%d" % far[1]], ["N1_%d" % h], 3000)
+        dma("s", T.N1[:, h * H:h * H + n], noise(me, 0, n), ntok(me) + ["s0_%d" % far[1]], ["N1_%d" % h], 3000)
 
-    def unpack(h, r, b):
-        name = ("W2_%d", "KK_%d")[h] % r
-        a = (2 * r + h) * FW
+    turnb = [0]
 
-        def at(c, s):
-            return T.WK[:, 256 * (15 - c) + 128 * h:256 * (15 - c) + 128 * (h + 1)]
-        for j, c in enumerate(kids(r)):
-            ts(at(c, 0), F[:, a + 128 * j:a + 128 * (j + 1)], 1 / 64, 192 - 31.5 / 64, ALU.mult, ALU.add, ["F%d_%d" % (h, r)],
-               ["%s_%d" % (name, j)], 128, 0.5)
-        if r != me:
-            mm([(ps[b][:], ap(I), F[:, a:a + q], True, False, q)] + blocks(b, dm64, at, 0, kids(r), True),
-               ["F%d_%d" % (h, r), I, dm64] + ["%s_%d" % (name, j) for j in range(N)], b)
-            lin("n%d%d" % (h, [mate, far[h], far[1 - h]].index(r)), T.NB[:, nblock(r) + h * q:nblock(r) + (h + 1) * q], ps[b][:], 1, 12256,
-                (), ["N2_%d_%d" % (h, r)], q, banks=[b])
+    def spare():
+        turnb[0] += 1
+        return OPT["spare"][turnb[0] % len(OPT["spare"])]
 
-    def unpack_rooms(r, b):
-        hh = new("ph", 2 * TRI)
-        x = [F[:, (2 * r + h) * FW + q:(2 * r + h + 1) * FW] for h in range(2)]
+    def block(tab, c):
+        return tab[:, 256 * (15 - c):256 * (15 - c) + 128]
+
+    def unpack(kind, hs, r):
+        if kind in "rs":
+            return
+        b, n, ks = spare(), PIECE[kind][1] if kind != "n" else 128, kids(r)
+        tm, rd = [], [I, dm64]
+        for n_, h in enumerate(hs):
+            src = "%s%d_%d" % (kind, h, r)
+            tm.append((ps[b][:, n_ * n:(n_ + 1) * n], ap(I), word(kind, h, r, 0, n), n_ == 0, False, n))
+            rd.append(src)
+            for y in range(n // 128):
+                if kind == "n":
+                    z = new("pb", 128)
+                    hi, name = ap(z), z
+                else:
+                    j = 2 * h + y if kind == "w" else h
+                    hi, name = block(T.W2 if kind == "w" else T.KK, ks[j]), "%s%d_%d" % (kind.upper(), j, r)
+                lin(hi, word(kind, h, r, 128 * y, 128 * (y + 1)), 1 / 64, 192 - 31.5 / 64, [src], [name], 128, 0.5, on="v")
+                if kind == "n":
+                    lin(noise(r, 512 + 128 * h, 640 + 128 * h), hi, 1, -192, [z], ["Nh%d_%d" % (h, r)], 128, 0.5, on="v")
+                tm.append((ps[b][:, n_ * n + 128 * y:n_ * n + 128 * (y + 1)], ap(dm64), hi, False, False, 128))
+                rd.append(name)
+        if kind == "w" and r == me:
+            return
+        mm(tm[:-1] + [tm[-1][:4] + (True, 128)], rd, b)
+        if kind == "k":
+            for n_, h in enumerate(hs):
+                lin(block(T.KK, ks[h + 2]), ps[b][:, 128 * n_:128 * (n_ + 1)], 1, 12448, (), ["K%d_%d" % (h + 2, r)], 128, banks=[b])
+        else:
+            a = (0 if kind == "w" else 768) + n * hs[0]
+            lin(noise(r, a, a + n * len(hs)), ps[b][:, 0:n * len(hs)], 1, 12256, (),
+                ["N%s%d_%d" % ("w" if kind == "w" else "l", h, r) for h in hs], n * len(hs), banks=[b])
+
+    def unpack_rooms(r):
+        b, hh = spare(), new("ph", 2 * TRI)
+        x = [word("n", h, r, 128) for h in range(2)]
         for h in range(2):
-            ts(ap(hh, h * TRI, (h + 1) * TRI), x[h], 1 / 16, 1408 - 7.5 / 16, ALU.mult, ALU.add, ["F%d_%d" % (h, r)], [hh], TRI, 0.5)
+            lin(ap(hh, h * TRI, (h + 1) * TRI), x[h], 1 / 16, 1408 - 7.5 / 16, ["n%d_%d" % (h, r)], [hh[3] + str(h)], TRI, 0.5, on="v")
         dm256 = diag(-256)
         mm(group(ps[b][:, 0:2 * TRI], [(ap(I), ap(hh))], 2 * TRI)
            + group(ps[b][:, 2 * TRI:3 * TRI], [(ap(d16), x[0]), (ap(dm256), ap(hh, 0, TRI)), (ap(I), x[1]),
                                                (ap(dm16), ap(hh, TRI, 2 * TRI))], TRI),
-           [hh, "F0_%d" % r, "F1_%d" % r, I, d16, dm256, dm16], b)
+           [hh[3] + "0", hh[3] + "1", "n0_%d" % r, "n1_%d" % r, I, d16, dm256, dm16], b)
         a = r * D + RAW
-        act(R[:, a:a + 2 * TRI], ps[b][:, 0:2 * TRI], -1280.0, (), ["Rt%d" % r], 2 * TRI, banks=[b])
-        act(R[:, a + 2 * TRI:a + 3 * TRI], ps[b][:, 2 * TRI:3 * TRI], 17.0 * 22528, (), ["Ru%d" % r], TRI, banks=[b])
+        lin(R[:, a:a + 2 * TRI], ps[b][:, 0:2 * TRI], 1, -1280, (), ["Rt%d" % r], 2 * TRI, banks=[b])
+        lin(R[:, a + 2 * TRI:a + 3 * TRI], ps[b][:, 2 * TRI:3 * TRI], 1, 17 * 22528, (), ["Ru%d" % r], TRI, banks=[b])
 
     d131 = diag(131072)
-    rotm, rotc = diag(-16, 240), diag(2047, 240)
+    rotm, rotc = diag(-16, 240), diag(2047 if OPT["cq"] else 2047 / 128, 240)
 
     def draw(c, second, pair, lb, lh, wtab, ktab, ntab, rw, rk, rn):
         b0, subs, kb = CH[c][:3]
         lead[0] = float(len(CH) - 1 - c)
         w = 8 * sum(subs)
         wp = (w + 15) // 16 * 16 if second else 2 * w
-        bias = -160.0 if second else 0.0
         ends = [sum(subs[:u]) for u in range(len(subs) + 1)]
         cuts = [[(0, ends[-1], range(len(subs)))], [(ends[u], ends[u + 1], (u,)) for u in range(len(subs))]]
         for buf, nm, tab, rd_, k in ((T.Wg, "Wg", wtab, rw, 0), (T.Kg, "Kg", ktab, rk, 1)):
-            bs_ = ap(bon[second]) if k else bias
             for x0, x1, us in cuts[OPT["split"][k]]:
-                act(buf[:, 128 * (b0 + x0):128 * (b0 + x1)], tab.indirect(ap(lb[0], lb[1] + 8 * x0, lb[1] + 8 * x1)), bs_,
-                    rd_ + [lb[0]] + ([bon[second]] if k else []), ["%s_%d_%d" % (nm, c, u) for u in us], 128 * (x1 - x0), gather=True)
+                lin(buf[:, 128 * (b0 + x0):128 * (b0 + x1)], tab.indirect(ap(lb[0], lb[1] + 8 * x0, lb[1] + 8 * x1)), 1,
+                    ap(bon[second]) if k else -160 * second, rd_ + [lb[0]] + ([bon[second]] if k else []),
+                    ["%s_%d_%d" % (nm, c, u) for u in us], 128 * (x1 - x0), gather=True)
         for x0, x1, us in cuts[OPT["split"][2]]:
             a, e = 128 * (b0 + x0), 128 * (b0 + x1)
             tt(T.A[:, a:e], ntab.indirect(ap(lh[0], lh[1] + 8 * x0, lh[1] + 8 * x1)), T.Wg[:, a:e], ALU.mult,
@@ -566,7 +596,7 @@ def rank_program(g, core, T, topo):
                          last and m == nb - 1, 128) for m in range(nb)], [nm + tk, mat], bk)
             if pair:
                 n = 72 * nb
-                act(T.Rl[:, 72 * a:72 * a + n], ps[bk][:, 0:n], 0.0, (), ["Rl" + tk], n, banks=[bk], func=AF.Relu)
+                act(T.Rl[:, 72 * a:72 * a + n], ps[bk][:, 0:n], 0.0, (), ["Rl" + tk], n, AF.Relu, banks=[bk])
                 scan(T.Z9[:, 72 * a:72 * a + n], ps[bk][:, 256:256 + n], T.Rl[:, 72 * a:72 * a + n], ALU.add, ALU.max, ["Rl" + tk],
                      ["Z9" + tk], n, banks=[bk])
             else:
@@ -575,41 +605,43 @@ def rank_program(g, core, T, topo):
         zs = ["%s_%d_%d" % ("Z9" if pair else "Z", c, u) for u in range(len(subs))]
         win = T.Z9[:, 72 * b0:72 * (b0 + ends[-1])] if pair else T.Z[:, 128 * b0:128 * (b0 + ends[-1])]
         x, xa = lref(w, 9, 8, not second) if pair else lref(w, 16, 15, not second)
-        hn, low = new("pf", wp), new("ph", wp)
+        hn, low, cq = new("pf", wp), new("ph", wp), new("ph", wp)
         ts(ap(hn), win.indirect(xa), BIG, -BIG, ALU.add, ALU.add, zs + [x], [hn], wp, gather=True)
         tt(ap(low), win.indirect(xa), ap(hn), ALU.subtract, zs + [x, hn], [low], wp, gather=True)
-        return low
+        if second and OPT["cq"]:
+            lin(ap(cq), ap(low), 1 / 128, 1536, [low], [cq], wp, 0.5)
+        elif second:
+            h2 = new("pf", wp)
+            ts(ap(h2), win.indirect(xa), BIG / 32, -BIG / 32, ALU.add, ALU.add, zs + [x], [h2], wp, gather=True)
+            tt(ap(cq), ap(h2), ap(hn), ALU.subtract, [h2, hn], [cq], wp)
+        return low, cq
 
     def turn(b, at, w, mat, x, stop):
         return [(ps[b][:, at + (-r) % 8:at + w:8], ap(mat, 16 * r, 16 * r + 128), ap(x, r, w, 8), False, stop and r == 7, w // 8)
                 for r in range(8)]
 
-    def terms(out, tm, n, start, stop, b):
-        mm(group(out, [(ap(m), x) for m, _, x in tm], n, start, stop), [y for m, t, _ in tm for y in (m, t)], b)
-
     def modulo(tm, b, at, n, m):
         z = new("pb", n)
         terms(ps[b][:, at:at + n], tm, n, True, True, b)
-        lin("mod", ap(z), ps[b][:, at:at + n], 1 / m, 191.5 + 1 / 4096, (), [z], n, banks=[b])
+        lin(ap(z), ps[b][:, at:at + n], 1 / m, 191.5 + 1 / 4096, (), [z], n, banks=[b])
         return tm + [(diag(-m), z, ap(z)), (diag(m // 8), c1536, ap(c1536, 0, n))]
 
     st = [{"fl": [], "fb": []} for _ in CH]
-    WKr = ["%s_%d_%d" % (x, r, j) for x in ("W2", "KK") for r in range(N) for j in range(N)]
-    N2r = ["N2_%d_%d" % (h, r) for h in range(2) for r in range(N)] + [wts, kds, "wx", "kx", nzs, nds, "rest"]
-    Rr = (["Rraw%d_%d" % (h, r) for h in range(2) for r in range(N)] + ["Rt%d" % r for r in range(N)]
+    W2r, KKr = [["%s%d_%d" % (x, j, r) for r in range(N) for j in range(N)] for x in "WK"]
+    N2r = [x for r in range(N) for x in ntok(r)]
+    Rr = (["%s%d_%d" % (x, h, r) for x in "rs" for h in range(2) for r in range(N)] + ["Rt%d" % r for r in range(N)]
           + ["Ru%d" % r for r in range(N) if r != me])
-    unpack(0, me, pa)
-    unpack(1, me, pb_)
+    unpack("w", (0, 1), me)
     for rnd in range(3):
         owns, l2 = [], []
         for c, (b0, subs, kb, s0, s1) in enumerate(CH):
             k0, w = 8 * b0, 8 * sum(subs)
             wp = (w + 15) // 16 * 16
             if rnd == 0:
-                tabs = (ap(wts, 0, B), ap(kds, 0, B), mine, [wts], [kds], ["N2_0_%d" % me, "N2_1_%d" % me])
+                tabs = (ap(wts, 0, B), ap(kds, 0, B), noise(me, 0, H), [wts], [kds], ntok(me))
             else:
                 tabs = (ap(wts), ap(kds), T.N1[:], [wts, "wx"], [kds, "kx"], ["N1_0", "N1_1", "N1_2"])
-            low = draw(c, 0, OPT["pairs"][rnd][0], lists[c][0], lists[c][1], *tabs)
+            low, _ = draw(c, 0, OPT["pairs"][rnd][0], lists[c][0], lists[c][1], *tabs)
             tm = [(diag(1 / 16), salB, ap(salB, k0, k0 + w))]
             for fb in st[c]["fb"]:
                 tm += [(diag(KT / 16), fb, ap(fb, 0, w)), (diag(-KT / 16), fb, ap(fb, w, 2 * w))]
@@ -619,20 +651,25 @@ def rank_program(g, core, T, topo):
             terms(ps[s0][:, w:2 * w], tm, w, False, False, s0)
             mm(turn(s0, 0, 2 * w, wide1, low, True), [low, wide1, "wide1b"], s0)
             iv, hm, lb, lh = new("pi", w), new("pi", w), new("pu", w), new("pu", w)
-            lin("lb", ap(lb), ps[s0][:, 0:w], 1, B - 1 - 1536, (), [lb], w, banks=[s0])
-            lin("iv", ap(iv), ps[s0][:, w:2 * w], ALPHA, (B - 1) * ALPHA + 15.373, (), [iv], w, banks=[s0])
+            lin(ap(lb), ps[s0][:, 0:w], 1, B - 1 - 1536, (), [lb], w, banks=[s0], on="V")
+            lin(ap(iv), ps[s0][:, w:2 * w], ALPHA, (B - 1) * ALPHA + 15.373, (), [iv], w, banks=[s0], on="V")
             ts(ap(hm), ap(iv), (N - 1) * GAP + H - 1, None, ALU.bitwise_and, None, [iv], [hm], w)
-            lin("lh", ap(lh), ap(hm), 1, 0, [hm], [lh], w)
+            lin(ap(lh), ap(hm), 1, 0, [hm], [lh], w, on="v")
             x, xa = lref(w)
             own = new("pb", wp)
-            lin("own", ap(own), ap(hm).indirect(xa), 1 / GAP, 194 - 0.125, [hm, x], [own], wp, gather=True)
+            lin(ap(own), ap(hm).indirect(xa), 1 / GAP, 194 - 0.125, [hm, x], [own], wp, gather=True)
             owns.append(own)
             l2.append((lb, lh))
         if rnd == 0:
-            for n_, (h, r) in enumerate([(0, mate), (0, far[0]), (1, mate), (1, far[1]), (0, far[1]), (1, far[0])]):
-                unpack(h, r, OPT["spare"][n_ % 2])
-            for n_, r in enumerate([mate, far[0], far[1]]):
-                unpack_rooms(r, OPT["spare"][n_ % 2])
+            lead[0] = float(len(CH) - 1)
+            unpack("k", (0, 1), me)
+            seen = {}
+            for kind, hs, r in landed:
+                unpack(kind, hs, r)
+                seen[(kind, r)] = seen.get((kind, r), 0) + len(hs)
+            for kind, hs, r in landed:
+                if kind == "n" and seen.pop((kind, r), 0):
+                    unpack_rooms(r)
         j0 = 0 if rnd == 2 else 1
         for c, (b0, subs, kb, s0, cb) in enumerate(CH):
             w = 8 * sum(subs)
@@ -646,10 +683,10 @@ def rank_program(g, core, T, topo):
             rt_ = ["run%d_%d" % (j, c) for j in range(N + 1)]
             if c:
                 up = 8 * sum(CH[c - 1][1]) + 1
-                lin("carry", ap(sn, j0 * u, N * u, u), ap(run[c - 1], (j0 + 1) * up - 1, N * up, up), 1, 0,
+                lin(ap(sn, j0 * u, N * u, u), ap(run[c - 1], (j0 + 1) * up - 1, N * up, up), 1, 0,
                     ["run%d_%d" % (j, c - 1) for j in range(j0, N)], ["carry%d" % c] + mt[:1 - j0], N)
             for j in range(j0, N):
-                act(ap(sn, j * u + 1, (j + 1) * u), ap(src, 0, w), -193.5 - j, [src], [mt[j]], w, func=AF.Sign)
+                act(ap(sn, j * u + 1, (j + 1) * u), ap(src, 0, w), -193.5 - j, [src], [mt[j]], w, AF.Sign)
             scan(ap(rn, j0 * u, N * u), ap(rst[c], 0, (N - j0) * u), ap(sn, j0 * u, N * u), ALU.mult, ALU.add,
                  mt[j0:N] + [rst[c], "carry%d" % c], rt_[j0:N], (N - j0) * u, 0.5)
             sg = new("pb", N * u)
@@ -657,33 +694,28 @@ def rank_program(g, core, T, topo):
                mt + ["carry%d" % c, tri, ntri], cb)
             mm(group(ps[cb][:, 128:128 + N * u], [(ap(blk), ap(rn, 0, N * u)), (ap(nblk), ap(rn, u, (N + 1) * u))], N * u, False, True),
                rt_ + [blk, nblk], cb)
-            act(ap(sg), ps[cb][:, 128:128 + N * u], 1.0 - 2 * CAP, (), [sg], N * u, banks=[cb], func=AF.Sign, scale=-1.0)
+            act(ap(sg), ps[cb][:, 128:128 + N * u], 1.0 - 2 * CAP, (), [sg], N * u, AF.Sign, banks=[cb], scale=-1.0)
             mm(group(ps[cb][:, 64:64 + w], [(ap(I), ap(sg, r * u + 1, (r + 1) * u)) for r in range(N)], w), [sg, I], cb)
             fl = new("pb", 2 * w)
-            act(ap(fl, 0, w), ps[cb][:, 64:64 + w], 4.0 if rnd < 2 else -15.0, (), [fl[3] + "g"], w, banks=[cb])
+            lin(ap(fl, 0, w), ps[cb][:, 64:64 + w], 1, 4 if rnd < 2 else -15, (), [fl[3] + "g"], w, banks=[cb])
             st[c]["fl"].append(fl)
         for c, (b0, subs, kb, s0, s1) in enumerate(CH):
             k0, w = 8 * b0, 8 * sum(subs)
-            wp = (w + 15) // 16 * 16
             S = st[c]
             fl = S["fl"][rnd]
-            low = draw(c, 1, OPT["pairs"][rnd][1], (l2[c][0], 0), (l2[c][1], 0), T.WK[:, 0:2 * B - 128], T.WK[:, 128:2 * B], T.NB[:],
-                       WKr, WKr, N2r)
-            cq, lr = new("ph", wp), new("pu", w)
-            lin("cq", ap(cq), ap(low), 1 / 128, 1536, [low], [cq], wp, 0.5)
+            low, cq = draw(c, 1, OPT["pairs"][rnd][1], (l2[c][0], 0), (l2[c][1], 0), T.W2[:], T.KK[:], T.N2[:], W2r, KKr, N2r)
+            lr = new("pu", w)
             dv = ps[s0][:, 128:128 + w]
-            terms(dv, [(diag(-D), owns[c], ap(owns[c], 0, w)), (diag(132 - 2047), c1536, ap(c1536, 0, w))], w, True, False, s0)
+            terms(dv, [(diag(-D), owns[c], ap(owns[c], 0, w)), (diag(132 - 2047 * OPT["cq"]), c1536, ap(c1536, 0, w))], w, True, False, s0)
             mm(turn(s0, 128, w, rotm, low, False), [low, rotm], s0)
             mm(turn(s0, 128, w, rotc, cq, True), [cq, rotc], s0)
-            lin("lr", ap(lr), dv, 1, -1, (), [lr], w, banks=[s0])
+            lin(ap(lr), dv, 1, -1, (), [lr], w, banks=[s0], on="V")
             one_ = I if rnd < 2 else diag(OFF)
-            extra = [(ap(one_), ap(fl, 0, w))]
-            erd = [fl[3] + "g", one_]
+            extra = [(one_, fl[3] + "g", ap(fl, 0, w))]
             if rnd > 0:
                 ne = new("pb", w)
                 tt(ap(ne), dv, ap(S["one"]), ALU.not_equal, [S["one"]], [ne], w, 1.0, banks=[s0])
-                extra.append((ap(one_), ap(ne)))
-                erd.append(ne)
+                extra.append((one_, ne, ap(ne)))
             if rnd == 2:
                 da, db = new("pf", w), new("pf", w)
                 tt(ap(da), dv, ap(S["ha"]), ALU.add, [S["ha"]], [da], w, 1.0, banks=[s0])
@@ -703,29 +735,26 @@ def rank_program(g, core, T, topo):
                                 rd += [diag(back), f]
                     if b == s1:
                         mm(tm[:-1] + [tm[-1][:4] + (True, w)], rd, b)
-                        lin("mod", ap(z), ps[b][:, at:at + 2 * w], 1 / B, 191.5 + 1 / 4096, (), [z], 2 * w, banks=[b])
+                        lin(ap(z), ps[b][:, at:at + 2 * w], 1 / B, 191.5 + 1 / 4096, (), [z], 2 * w, banks=[b])
                     else:
                         mm(tm + [(lraw, ap(diag(-B)), ap(z), False, False, 2 * w)], rd + [diag(-B), z], b)
             a, n = 128 * b0, 16 * w
             tt(T.Ft[:, a:a + n], R[:].indirect(ap(lr)), ap(nds, a, a + n), ALU.is_ge, Rr + [lr, nds], ["Ft%d" % c], n, gather=True)
             cnt = ps[s1][:, 0:w]
             pk = pick if rnd < 2 else pickb
-            mm(group(cnt, extra, w, True, False), erd, s1)
+            terms(cnt, extra, w, True, False, s1)
             mm(group(cnt, [(ap(pk, 15 - i, 143 - i), T.Ft[:, a + i:a + n:16]) for i in range(16)], w, False, True), ["Ft%d" % c, pk], s1)
             if rnd < 2:
                 k = ap(fl, w, 2 * w)
-                if ENG["k"] == "a":
-                    act(k, cnt, -17.0 - rnd, (), [fl], w, banks=[s1], func=AF.Relu)
-                else:
-                    ts(k, cnt, 17.5 + rnd, None, ALU.is_ge, None, (), [fl], w, banks=[s1])
+                lin(k, cnt, 1, -17 - rnd, (), [fl], w, banks=[s1], on="v", cut=True)
                 mm([(ps[s0][:, 192 + y * w:192 + (y + 1) * w], ap(diag(back)), k, False, y == 1, w) for y, back in enumerate((B - K5, H - KH))],
                    [fl, diag(B - K5), diag(H - KH)], s0)
                 l1, fb, x = new("pu", 2 * w), new("pb", 2 * w), new("pf", w)
-                lin("l1", ap(l1), lraw, 1, 192 * B, (), [l1], 2 * w, banks=[s0])
+                lin(ap(l1), lraw, 1, 192 * B, (), [l1], 2 * w, banks=[s0], on="V")
                 lists[c] = ((l1, 0), (l1, w))
                 tt(ap(x), dv, k, ALU.mult, [fl], [x], w, 1.0, banks=[s0])
                 y, ya = lref(2 * w)
-                act(ap(fb), ap(fl).indirect(ya), 0.0, [fl, fl[3] + "g", y], [fb], 2 * w, gather=True)
+                lin(ap(fb), ap(fl).indirect(ya), 1, 0, [fl, fl[3] + "g", y], [fb], 2 * w, gather=True)
                 S["fb"].append(fb)
             if rnd == 0:
                 S["one"] = x
@@ -736,11 +765,11 @@ def rank_program(g, core, T, topo):
                 tt(ap(sm), ap(x), ap(S["one"]), ALU.add, [x, S["one"]], [sm], w)
                 tt(ap(one), ap(sm), ap(two), ALU.subtract, [sm, two], [one], w)
                 ts(ap(tk_), ap(two), 0.0, None, ALU.is_equal, None, [two], [tk_], w)
-                act(ap(has), ap(one), 0.0, [one], [has], w, func=AF.Sign)
-                act(ap(ha_), ap(has), -1.0, [has], [ha_], w, scale=-OFF)
-                act(ap(hb_), ap(has), -1.0 - OFF, [has], [hb_], w, scale=OFF)
-                act(ap(om), ap(one), -1.0, [one], [om], w)
-                act(ap(tm_), ap(two), -1.0, [two], [tm_], w)
+                act(ap(has), ap(one), 0.0, [one], [has], w, AF.Sign)
+                lin(ap(ha_), ap(has), -OFF, -1, [has], [ha_], w)
+                lin(ap(hb_), ap(has), OFF, -1 - OFF, [has], [hb_], w)
+                lin(ap(om), ap(one), 1, -1, [one], [om], w)
+                lin(ap(tm_), ap(two), 1, -1, [two], [tm_], w)
                 S.update({"one": one, "takes": tk_, "ha": ha_, "hb": hb_, "om": om, "tm": tm_})
             else:
                 for n_, (dd, old, out) in enumerate([(da, S["om"], T.ya), (db, S["tm"], T.yb)]):
@@ -751,7 +780,7 @@ def rank_program(g, core, T, topo):
 
     if PLAN.get("n") != len(ops):
         PLAN["n"] = len(ops)
-        PLAN["order"], PLAN["times"] = make_order(ops, OPT)
+        PLAN["order"], PLAN["pick"], PLAN["times"] = make_order(ops, OPT)
     order = PLAN["order"]
 
     count = {e: 0 for e in queue}
@@ -763,7 +792,7 @@ def rank_program(g, core, T, topo):
     place = {i: n_ for n_, i in enumerate(order)}
     for i in order:
         o_ = ops[i]
-        e = o_["e"]
+        e, fn, _c = o_["alt"][PLAN["pick"][i]]
         if e is not None:
             want = {}
             for d_ in o_["deps"]:
@@ -776,7 +805,7 @@ def rank_program(g, core, T, topo):
                     known[e][s] = v
                     for s2, v2 in mark[d_][2].items():
                         known[e][s2] = max(known[e].get(s2, 0), v2)
-            inst = o_["fn"]()
+            inst = fn()
         if o_["sem"] == "none":
             continue
         if o_["sem"] is not None:

@@ -9,46 +9,58 @@ KH = (KT + K5) % H
 W = O // 16
 TRI = 88
 RAW = D - 3 * TRI
-PIECE = {"n": (0, 128 + TRI), "w": (2 * (128 + TRI), 256), "k": (2 * (128 + TRI) + 512, 128)}
-FW = 2 * sum(x[1] for x in PIECE.values())
-BIG = 1.5 * 2.0 ** 35
+PIECE = {"n": (0, 256), "w": (512, 128), "k": (768, 128), "x": (512, 256), "t": (1024, TRI)}
+FW = 1024 + 2 * TRI
+EPS, TINY = 2.0 ** -17, 2.0 ** -24
+UNIT = 2.0 ** -12
 GAP = 4096
 ALPHA = 4095 / 256
+MORE = 1280
 OFF = 8192.0
 
 SCRATCH = {
-    "wts": ("sbuf", [128, B + H], "bfloat16"), "kds": ("sbuf", [128, B + H], "bfloat16"), "nzs": ("sbuf", [128, H], "bfloat16"),
+    "wts": ("sbuf", [128, B + 2 * MORE], "bfloat16"), "kds": ("sbuf", [128, B + 2 * MORE], "bfloat16"), "nzs": ("sbuf", [128, H], "bfloat16"),
     "nds": ("sbuf", [128, O], "bfloat16"), "N2": ("sbuf", [128, (N - 1) * GAP + H], "bfloat16"), "R": ("sbuf", [128, N * D], "bfloat16"),
     "F": ("sbuf", [128, N * FW], "float16"), "W2": ("sbuf", [128, 2 * B], "bfloat16"), "KK": ("sbuf", [128, 2 * B], "bfloat16"),
-    "N1": ("sbuf", [128, B + 336], "bfloat16"), "Wg": ("sbuf", [128, O], "bfloat16"), "Kg": ("sbuf", [128, O], "float16"),
+    "N1": ("sbuf", [128, B + 384], "bfloat16"), "Wg": ("sbuf", [128, O], "bfloat16"), "Kg": ("sbuf", [128, O], "float16"),
     "A": ("sbuf", [128, O], "float16"), "Z": ("sbuf", [128, O], "float32"), "Ft": ("sbuf", [128, O], "bfloat16"),
+    "P1": ("sbuf", [128, B + 2 * MORE], "float32"), "P2": ("sbuf", [128, 2 * B], "float32"), "Pg": ("sbuf", [128, O], "float32"),
     "Z9": ("sbuf", [128, 720], "float32"), "Rl": ("sbuf", [128, 720], "float32"),
-    "pi": ("sbuf", [128, 6144], "int32"), "pf": ("sbuf", [128, 6144], "float32"), "pb": ("sbuf", [128, 12288], "bfloat16"),
-    "ph": ("sbuf", [128, 8192], "float16"), "pu": ("sbuf", [128, 4096], "uint16"),
+    "pi": ("sbuf", [128, 3072], "int32"), "pf": ("sbuf", [128, 4096], "float32"), "pb": ("sbuf", [128, 16384], "bfloat16"),
+    "ph": ("sbuf", [128, 4096], "float16"), "pu": ("sbuf", [128, 3072], "uint16"),
 }
 for _b in range(8):
     SCRATCH["ps%d" % _b] = ("psum", [128, 512], "float32")
 SEMAPHORES = (["cv", "ca", "cp", "cg", "sent"] + ["d%d" % i for i in range(24)]
-              + ["%s%d_%d" % (a, h, r) for a in "rsnwk" for h in range(2) for r in range(N)])
+              + ["%s%d_%d" % (a, h, r) for a in "rstnwkx" for h in range(2) for r in range(N)])
 
 OPT = {
-    "chunks": [(0, (3, 2), (0, 1), 2, 3), (5, (3, 2), (4, 5), 6, 7)],
-    "pack": (3, 7, 2, 6), "spare": (3, 7, 1, 5, 0, 4),
+    "chunks": [(0, (3, 2), (0, 1), 2, 3, 3), (5, (3, 2), (4, 5), 6, 7, 7)],
+    "pack": (3, 7, 2, 6), "spare": ((3, 7), (1, 5, 0, 4)),
     "pairs": [[0, 0], [0, 0], [0, 0]],
-    "split": [1, 1, 1], "cq": 1,
-    "loads": ["ra", "tri", "nz", "wt", "kd", "rb", "nd", "wx", "kx"], "early": 192,
-    "sends": [("r", 2200, 2400), ("n", 2500, 2800), ("w", 2700, 3300), ("k", 2300, 3000), ("N", 2100, 0), ("W", 2200, 0), ("s", 2700, 3000),
-              ("R", 2500, 0), ("S", 2200, 0)],
-    "direct": "k", "hand": "in",
-    "times": [(0.83, 1.35, 0.42, 215.0, 1.0), (1.2, 1.9, 0.6, 200.0, 1.2), (0.95, 1.5, 0.48, 200.0, 1.0)],
-    "tries": 9000, "seed": 12345, "lead": 3000.0, "slack": 0.02, "mirror": 3, "lean": 1000.0,
+    "split": [[(3, 2), (3, 2), (3, 2), (5,)]] * 2, "cq": 1,
+    "loads": ["ra", "nz", "tri", "wt", "kd", "rb", "nd", "wx", "kx"], "early": 2 * TRI,
+    "sends": [("r", 2000, 2100), ("n", 2700, 3300), ("w", 2700, 4500), ("k", 2300, 4400), ("N", 2700, 0), ("t", 2600, 3100),
+              ("s", 3400, 4700), ("RT", 2300, 0), ("S", 2200, 0)],
+    "direct": "wk", "hand": "S", "fuse": 1, "lr": "V", "one": [[0, 0], [0, 0], [0, 0]], "build": (2, 6), "soon": 2,
+    "times": [(0.83, 1.35, 0.42, 215.0, 1.0), (1.0, 1.6, 0.5, 205.0, 1.05), (1.2, 1.9, 0.6, 200.0, 1.15)],
+    "tries": 2000, "seed": 2, "leads": (500.0, 1000.0, 1500.0, 2500.0), "short": 600, "slack": 0.007, "mirror": 3, "lean": 3000.0, "aim": 0.7, "slow": 0.24, "near": 0.02, "even": 1,
+    "swaps": 1500, "cycles": 4, "more": {"tries": 1800, "swaps": 300, "slack": 0.008, "even": 0.5}, "stale": 600, "keep": 20, "gain": 0.003,
 }
 PLAN = {}
 
 
-def make_order(ops, opt):
+def make_order(ops, opt, begin=None):
     n = len(ops)
-    pre = [sorted(o["deps"] | o["after"]) for o in ops]
+    pre, above = [], []
+    for o in ops:
+        up = 0
+        for d in o["deps"]:
+            up |= above[d]
+        pre.append(sorted([d for d in o["deps"] if not up >> d & 1] + [d for d in o["after"] - o["deps"] if not up >> d & 1]))
+        for d in o["deps"]:
+            up |= 1 << d
+        above.append(up)
     sets = []
     for cy, ga, pc, hop, xl in opt["times"]:
         cost = [[c[0] + cy * (c[1] + ga * c[2]) + pc * c[3] for _, _, c in o["alt"]] for o in ops]
@@ -78,6 +90,32 @@ def make_order(ops, opt):
                 last = t + lat[i]
         return last
 
+    def loads(pick):
+        x = {"a": 0.0, "v": 0.0}
+        for e, c, k in zip(engs, sets[-1][0], pick):
+            if e[k] in x:
+                x[e[k]] += c[k]
+        return x["a"], x["v"]
+
+    def chain(order, pick, s):
+        cost, lat, fore, back = sets[s]
+        end, free, by = [0.0] * n, {}, [None] * n
+        for i in order:
+            e = engs[i][pick[i]]
+            t, by[i] = free.get(e, (0.0, None))
+            for d, x in fore[i]:
+                if end[d] + x > t:
+                    t, by[i] = end[d] + x, d
+            end[i] = t + cost[i][pick[i]]
+            if e is not None:
+                free[e] = (end[i], i)
+        i, pairs = max(range(n), key=lambda j: end[j] + lat[j]), []
+        while by[i] is not None:
+            if by[i] not in pre[i]:
+                pairs.append((by[i], i))
+            i = by[i]
+        return pairs or [(0, 0)]
+
     def place(seq, pick, s, mirrored, lean):
         cost, lat, fore, back = sets[s]
         need = back if mirrored else fore
@@ -88,7 +126,21 @@ def make_order(ops, opt):
                 if end[d] + x > t0:
                     t0 = end[d] + x
             best = None
-            for a in (range(len(engs[i])) if lean and lean[i] is not None else (pick[i],)):
+            if not lean or lean[i] is None:
+                e, c = engs[i][pick[i]], cost[i][pick[i]]
+                if e is not None:
+                    l = busy[e]
+                    k = m = len(l)
+                    while k > 0 and l[k - 1][1] > t0:
+                        k -= 1
+                    while k < m and l[k][0] < t0 + c:
+                        if l[k][1] > t0:
+                            t0 = l[k][1]
+                        k += 1
+                    l.insert(k, (t0, t0 + c))
+                start[i], end[i] = t0, t0 + c
+                continue
+            for a in range(len(engs[i])):
                 e, c, t, k = engs[i][a], cost[i][a], t0, 0
                 if e is not None:
                     l = busy[e]
@@ -114,7 +166,7 @@ def make_order(ops, opt):
             for d, x in need[i]:
                 if key[d] >= key[i]:
                     key[i] = key[d] + 0.001
-        return sorted(range(n), key=lambda i: key[i])
+        return [i for _, i in sorted(zip(key, range(n)))]
 
     cost, lat, fore, back = sets[0]
     tail = [0.0] * n
@@ -127,32 +179,168 @@ def make_order(ops, opt):
         seed[0] = (seed[0] * 1103515245 + 12345) % 2 ** 31
         return seed[0] / 2 ** 31
 
-    key, pick, lean = [-tail[i] - opt["lead"] * ops[i]["lead"] for i in range(n)], [o["first"] for o in ops], None
-    for k in range(opt["tries"]):
+    ref, found = [1.2 * max(tail) * (1.0 + y * opt["slow"]) for y in range(len(sets))], [begin] if begin else []
+    turns = [(x, k, opt["short"]) for x in opt["leads"] for k in range(opt["short"])] + [(None, k, opt["tries"]) for k in range(opt["tries"])]
+    for lead, k, tries in turns:
+        if k == 0:
+            found += [best] if best else []
+            best, cur, lean = None, None, None
+            if lead is None:
+                key, pick = [0.0] * n, min(found)[3]
+                for x, i in enumerate(min(found)[1]):
+                    key[i] = float(x)
+            else:
+                key, pick = [-tail[i] - lead * ops[i]["lead"] for i in range(n)], [o["first"] for o in ops]
         s = k % len(sets)
         start, end, pick = place(sort(key, False), pick, s, False, lean)
         for again in range(2):
-            order = sort(start, False)
-            ts_ = [replay(order, pick, y) for y in range(len(sets))]
-            ref = ref or ts_
-            score = sum(a / b for a, b in zip(ts_, ref))
-            if best is None or score < best[0]:
-                best = (score, order, ts_, pick)
-            if cur is None or score < cur[0] + opt["slack"] * (1.0 - k / opt["tries"]) * rnd():
-                cur = (score, start, pick)
+            span = max(a + b for a, b in zip(end, sets[s][1]))
+            if cur is None or span < best[2][s] * (1.0 + opt["near"]):
+                order = [i for _, i in sorted(zip(start, range(n)))]
+                ts_ = [span if y == s else replay(order, pick, y) for y in range(len(sets))]
+                score = sum(a / b for a, b in zip(ts_, ref)) + opt["even"] * max(loads(pick)) / ref[-1]
+                if best is None or score < best[0]:
+                    best = (score, order, ts_, pick)
+                if cur is None or score < cur[0] + opt["slack"] * (1.0 - k / tries) * rnd():
+                    cur = (score, start, pick, order)
             if again or k % opt["mirror"]:
                 break
             bs, be, _ = place(sort([-x for x in end], True), pick, s, True, None)
             start, end, pick = place(sort([-x for x in be], False), pick, s, False, None)
         size, span = 2500.0 * rnd() ** 3 + 50.0, 12000.0 * rnd() ** 2
         lo = rnd() * max(cur[1]) - span / 2
-        shift, who, pick, lean = size * (2 * rnd() - 1), float(k % 2), cur[2], None
+        shift, who, pick, lean = size * (2 * rnd() - 1), float(int(rnd() * len(opt["chunks"]))), cur[2], None
         if k % 3:
             key = [x + (size * rnd() if lo <= x <= lo + span else 0.0) for x in cur[1]]
         else:
             key = [x + (shift if lo <= x <= lo + span and o["lead"] == who else 0.0) for x, o in zip(cur[1], ops)]
         if k % 4 == 0:
             lean = [opt["lean"] * (rnd() - 0.1) if lo <= x <= lo + span and rnd() < 0.5 else None for x in cur[1]]
+        if rnd() < opt["aim"]:
+            if len(cur) == 4:
+                cur = cur + ([chain(cur[3], cur[2], y) for y in range(len(sets))],)
+            pairs = cur[4][(k + 1) % len(sets)]
+            key, pick, lean = list(cur[1]), list(cur[2]), None
+            for _ in range(1 + int(2.5 * rnd() ** 2)):
+                a, b = pairs[int(rnd() * len(pairs))]
+                y = rnd()
+                if y < 0.3 and len(engs[a]) > 1:
+                    pick[a] = 1 - pick[a]
+                elif y > 0.7 and len(engs[b]) > 1:
+                    pick[b] = 1 - pick[b]
+                else:
+                    key[a] = key[b] + 1.0
+
+    best = min(found + [best])
+    score, order, ts_, pick = best
+    pick, tabu, ns, stale = list(pick), {}, range(len(sets)), 0
+    for it in range(opt["swaps"]):
+        mp, ms, lastq = [None] * n, [None] * n, {}
+        for i in order:
+            e = engs[i][pick[i]]
+            if e is not None:
+                j = lastq.get(e)
+                if j is not None:
+                    mp[i], ms[j] = j, i
+                lastq[e] = i
+        P, Hd, Tl, Jh, Jt, ts_ = [], [], [], [], [], []
+        for s in ns:
+            cost, lat, fore, back = sets[s]
+            p = [c[k] for c, k in zip(cost, pick)]
+            end, jh, tl, jt = [0.0] * n, [0.0] * n, [0.0] * n, [0.0] * n
+            for i in order:
+                t = 0.0
+                for d, x in fore[i]:
+                    if end[d] + x > t:
+                        t = end[d] + x
+                jh[i] = t
+                j = mp[i]
+                if j is not None and end[j] > t:
+                    t = end[j]
+                end[i] = t + p[i]
+            for i in reversed(order):
+                t = lat[i]
+                for d, x in back[i]:
+                    if tl[d] + x > t:
+                        t = tl[d] + x
+                jt[i] = t
+                j = ms[i]
+                if j is not None and tl[j] > t:
+                    t = tl[j]
+                tl[i] = t + p[i]
+            P.append(p), Hd.append(end), Tl.append(tl), Jh.append(jh), Jt.append(jt), ts_.append(max(tl))
+        ld = loads(pick)
+        score = sum(a / b for a, b in zip(ts_, ref)) + opt["even"] * max(ld) / ref[-1]
+        stale += 1
+        if score < best[0]:
+            best, stale = (score, order, ts_, list(pick)), 0
+        if stale > opt["stale"]:
+            order, pick, stale, tabu = best[1], list(best[3]), 0, {}
+            continue
+        moves = {}
+        for s in ns:
+            for b in range(n):
+                if Hd[s][b] + Tl[s][b] - P[s][b] > ts_[s] - 0.01:
+                    a = mp[b]
+                    if a is not None and Hd[s][a] > Jh[s][b] + 0.01 and a not in pre[b]:
+                        moves[(a, b)] = 1
+                    if len(engs[b]) > 1:
+                        moves[(b, None)] = 1
+        where = {i: k for k, i in enumerate(order)}
+        choice = None
+        for a, b in moves:
+            v = 0.0
+            if b is None:
+                e, k = engs[a][1 - pick[a]], where[a]
+                x, y = k - 1, k + 1
+                while x >= 0 and engs[order[x]][pick[order[x]]] != e:
+                    x -= 1
+                while y < n and engs[order[y]][pick[order[y]]] != e:
+                    y += 1
+            for s in ns:
+                p, end, tl, jh, jt = P[s], Hd[s], Tl[s], Jh[s], Jt[s]
+                if b is None:
+                    t = (max(jh[a], end[order[x]] if x >= 0 else 0.0) + sets[s][0][a][1 - pick[a]]
+                         + max(jt[a], tl[order[y]] if y < n else 0.0))
+                    if mp[a] is not None and ms[a] is not None:
+                        t = max(t, end[mp[a]] + tl[ms[a]])
+                else:
+                    eb = max(jh[b], end[mp[a]] if mp[a] is not None else 0.0) + p[b]
+                    ta = max(jt[a], tl[ms[b]] if ms[b] is not None else 0.0) + p[a]
+                    t = max(eb + max(jt[b], ta), max(jh[a], eb) + ta)
+                if end[a] + tl[a] - p[a] < ts_[s] - 0.01:
+                    t = max(t, ts_[s])
+                v += max(t, ts_[s] * (1.0 - opt["gain"])) / ref[s]
+            if b is None:
+                c = sets[-1][0][a]
+                v += opt["even"] * (max(ld[0] + c[0], ld[1] - c[1]) if pick[a] else max(ld[0] - c[0], ld[1] + c[1])) / ref[-1]
+            else:
+                v += opt["even"] * max(ld) / ref[-1]
+            v += 1e-5 * rnd()
+            if (tabu.get((a, b), -1) < it or v < best[0] - 0.002) and (choice is None or v < choice[0]):
+                choice = (v, a, b)
+        if choice is None:
+            tabu = {}
+            continue
+        v, a, b = choice
+        if b is None:
+            pick[a] = 1 - pick[a]
+            tabu[(a, None)] = it + 8 + int(opt["keep"] * rnd())
+        else:
+            key = list(range(n))
+            for k, i in enumerate(order):
+                key[i] = k
+            key[a] = key[b] + 0.5
+            for i in order[where[a] + 1:where[b]]:
+                for d, x in sets[0][2][i]:
+                    if key[d] > key[i]:
+                        key[i] = key[d] + 0.0001
+                if mp[i] is not None and key[mp[i]] > key[i]:
+                    key[i] = key[mp[i]] + 0.0001
+            order = [i for _, i in sorted(zip(key, range(n)))]
+            tabu[(b, a)] = it + 8 + int(opt["keep"] * rnd())
+    if opt["cycles"]:
+        return make_order(ops, dict(opt, cycles=opt["cycles"] - 1, leads=(), seed=seed[0], **opt["more"]), best)
     return best[1], best[3], best[2]
 
 
@@ -175,6 +363,7 @@ def rank_program(g, core, T, topo):
         a = used[pool]
         used[pool] = a + (n + 15) // 16 * 16
         tok[0] += 1
+        assert used[pool] <= SCRATCH[pool][1][1], pool
         return (T[pool], a, n, "t%d" % tok[0])
 
     def ap(x, a=0, b=None, s=1):
@@ -268,18 +457,20 @@ def rank_program(g, core, T, topo):
     rt, RA = me * D + RAW, OPT["early"]
 
     beg, sal = new("pi", W), new("pi", W)
-    wts, kds = (T.wts, 0, B + H, "wts"), (T.kds, 0, B + H, "kds")
+    wts, kds = (T.wts, 0, B + 2 * MORE, "wts"), (T.kds, 0, B + 2 * MORE, "kds")
     nzs, nds = (T.nzs, 0, H, "nzs"), (T.nds, 0, O, "nds")
     loads = {"tri": (R[:, rt:rt + 3 * TRI], T.room[:, RAW:D], ["Rt%d" % me], 3 * TRI),
              "ra": (R[:, me * D:me * D + RA], T.room[:, 0:RA], ["r0_%d" % me, "r1_%d" % me], RA),
              "rb": (R[:, me * D + RA:rt], T.room[:, RA:RAW], ["s0_%d" % me, "s1_%d" % me], RAW - RA),
              "nz": (ap(nzs), T.noise[:], [nzs], H), "wt": (ap(wts, 0, B), T.wt[:], [wts], B), "kd": (ap(kds, 0, B), T.kid[:], [kds], B),
-             "nd": (ap(nds), T.need[:], [nds], O), "wx": (ap(wts, B, B + H), T.wt[:, 0:H], ["wx"], H),
-             "kx": (ap(kds, B, B + H), T.kid[:, 0:H], ["kx"], H)}
+             "nd": (ap(nds), T.need[:], [nds], O), "wx": (ap(wts, B, B + MORE), T.wt[:, 0:MORE], ["wx"], MORE),
+             "kx": (ap(kds, B, B + MORE), T.kid[:, 0:MORE], ["kx"], MORE)}
     dma("a", ap(beg), T.begin[:], (), [beg], 2100)
     dma("a", ap(sal), T.salt[:], (), [sal], 2200)
     due, prev = 2100.0, []
     for name in OPT["loads"]:
+        if name in ("wx", "kx") and OPT["one"][1][0]:
+            continue
         o_, i_, wr, n = loads[name]
         due += 0.69 * n - 60
         prev = [dma("s", o_, i_, (), wr, due, prev)]
@@ -308,7 +499,7 @@ def rank_program(g, core, T, topo):
 
     def diag(v, wide=128):
         if (v, wide) not in consts:
-            m = abs(v) * 4096
+            m = abs(v) * 2 ** 20
             while m % 2 == 0:
                 m //= 2
             x = new("pb" if m < 256 else "ph", wide)
@@ -319,15 +510,12 @@ def rank_program(g, core, T, topo):
     pick, pickb = new("pb", 144), new("pb", 144)
     ts(ap(pick), ap(col), ap(gcol), None, ALU.is_equal, None, [col, gcol], [pick], 144)
     lin(ap(pickb), ap(pick), OFF, 0, [pick], [pickb], 144, 0.5)
-    j_, r_, m8, t1, t2, ta, tb, rx = [new("pi", 8) for _ in range(8)]
-    lin(ap(t1), ap(col, 0, 8), 16, 0, [col], [t1], 8)
-    tt(ap(j_), ap(t1), ap(plo), ALU.add, [t1, plo], [j_], 8)
-    ts(ap(r_), ap(j_), 7, None, ALU.bitwise_and, None, [j_], [r_], 8)
-    tt(ap(m8), ap(j_), ap(r_), ALU.subtract, [j_, r_], [m8], 8)
-    tt(ap(t2), ap(phi), ap(r_), ALU.subtract, [phi, r_], [t2], 8)
-    lin(ap(ta), ap(t2), 1, 8, [t2], [ta], 8)
-    ts(ap(tb), ap(ta), 7, None, ALU.bitwise_and, None, [ta], [tb], 8)
-    tt(ap(rx), ap(tb), ap(m8), ALU.add, [tb, m8], [rx], 8)
+    i8, t1, t2, rx, rb = new("pi", 1), new("pi", 1), new("pi", 1), new("pi", 8), new("pf", 1)
+    ts(ap(i8), ap(prt, 0, 1), 8, None, ALU.bitwise_and, None, [prt], [i8], 1)
+    ts(ap(t1), ap(phi, 0, 1), ap(pcol), 128.0, ALU.subtract, ALU.add, [phi, pcol], [t1], 1)
+    ts(ap(t2), ap(t1), 7, None, ALU.bitwise_and, None, [t1], [t2], 1)
+    tt(ap(rb), ap(t2), ap(i8), ALU.add, [t2, i8], [rb], 1)
+    lin(ap(rx), ap(col, 0, 8), 16, ap(rb), [col, rb], [rx], 8)
     mirror = {}
 
     def lref(w, mul=1, add=0, twice=False):
@@ -346,42 +534,42 @@ def rank_program(g, core, T, topo):
         x = mirror[(w, mul, twice)]
         return x, ap(x, 0, ((1 + twice) * w + 15) // 16)
 
-    pat, c1536 = new("pf", 512), new("ph", 128)
+    pat, c1536 = new("pb", 512), new("ph", 128)
     if not all(all(x) for x in OPT["pairs"]):
         nmax = 128 * max(max(c[1]) for c in CH)
-        fill(ap(pat, 0, nmax), 0.0, [pat], nmax)
-        fill(ap(pat, 0, nmax, 16), -2.0 ** 25, [pat], 32)
+        fill(ap(pat, 0, nmax), 0.0, [pat], nmax // 2)
+        fill(ap(pat, 0, nmax, 16), -2.0 ** 13, [pat], 32)
     fill(ap(c1536), 1536.0, [c1536], 64)
     bon = [new("pf", 1), new("pf", 1)]
     for x, step, v in zip(bon, (256.0, 128.0), (-2047.0, -160.0)):
         lin(ap(x), ap(plo, 0, 1), -step, 15 * step + v, [plo], [x], 1)
-    blk, tri, ta, tb, tc, td = new("pb", 128), new("pb", 128), new("pi", 128), new("pf", 1), new("pb", 128), new("pb", 128)
-    ts(ap(ta), ap(col, 0, 128), 4, None, ALU.logical_shift_right, None, [col], [ta], 128)
-    lin(ap(tb), ap(phi, 0, 1), 1, 0, [phi], [tb], 1)
-    ts(ap(blk), ap(ta), ap(tb), None, ALU.is_equal, None, [ta, tb], [blk], 128)
-    ts(ap(tc), ap(col, 0, 128), ap(pcol), -1.0, ALU.is_lt, ALU.mult, [col, pcol], [tc], 128)
-    tt(ap(td), ap(tc), ap(blk), ALU.mult, [tc, blk], [td], 128)
-    d512 = diag(-512)
-    tt(ap(tri), ap(td), ap(d512), ALU.add, [td, d512], [tri], 128)
-    nblk, ntri = new("pb", 128), new("pb", 128)
+    blk, tri, nblk, ntri, ta, tb, gmid = [new("pb", 128) for _ in range(6)] + [new("pf", 1)]
+    lin(ap(gmid), ap(phi, 0, 1), -16, -7.5, [phi], [gmid], 1)
+    act(ap(ta), ap(col, 0, 128), ap(gmid), [col, gmid], [ta], 128, AF.Abs)
+    ts(ap(blk), ap(ta), 8.0, None, ALU.is_lt, None, [ta], [blk], 128, 0.5)
+    op("g", lambda: g.affine_select(ap(tb), ap(blk), [[-1, 128]], ALU.is_gt, 0.0, 0, 1), [blk], [tb], cost=(170.0, 256, 0, 0))
+    op("g", lambda: g.affine_select(ap(ntri), ap(tb), [[-1, 128]], ALU.not_equal, 512.0, 0, 1), [tb], [ntri], cost=(170.0, 256, 0, 0))
     lin(ap(nblk), ap(blk), -1, 0, [blk], [nblk], 128, 0.5)
-    lin(ap(ntri), ap(tri), -1, 0, [tri], [ntri], 128, 0.5)
-    sgn, run, rst = [], [], []
+    lin(ap(tri), ap(ntri), -1, 0, [ntri], [tri], 128, 0.5)
+    sgn, run, rst = [], [], {}
+
+    def steps(out, v, first, n, name):
+        op("g", lambda: g.iota(out, [[v, n]], v * first, 0, allow_small_or_imprecise_dtypes=True), (), [name], cost=(130.0, 2 * n, 0, 0))
     for c, ch in enumerate(CH):
         u = 8 * sum(ch[1]) + 1
-        a, b, z = new("pb", (N + 1) * u), new("pb", (N + 1) * u), new("pb", N * u)
-        fill(ap(z), 1.0, [z], N * u // 2)
-        fill(ap(z, 0, N * u, u), 0.0, [z], 4)
+        a, b = new("pb", (N + 1) * u), new("pb", (N + 1) * u)
+        if u not in rst:
+            rst[u] = new("pb", N * u)
+            fill(ap(rst[u]), 1.0, [rst[u]], N * u // 2)
+            fill(ap(rst[u], 0, N * u, u), 0.0, [rst[u]], 4)
         if c == 0:
-            fill(ap(a, u, N * u, u), 0.0, ["carry0"], 4)
-        for j, v in ((0, 1.0), (N, -1.0)):
-            fill(ap(a, j * u, (j + 1) * u), v, ["sgn%d_%d" % (j, c)], 40)
-            fill(ap(a, j * u, j * u + 1), v * 8 * ch[0], ["sgn%d_%d" % (j, c)], 1)
-            scan(ap(b, j * u, (j + 1) * u), ap(z, 0, u), ap(a, j * u, (j + 1) * u), ALU.mult, ALU.add, ["sgn%d_%d" % (j, c), z],
-                 ["run%d_%d" % (j, c)], 40)
+            fill(ap(a, 0, N * u, u), 0.0, ["carry0"], 4)
+        fill(ap(a, 1 - c, u), 1.0, ["sgn0_%d" % c], 40)
+        fill(ap(a, N * u, (N + 1) * u), -1.0, ["sgn%d_%d" % (N, c)], 40)
+        steps(ap(b, 0, u), 1, 8 * ch[0], u, "run0_%d" % c)
+        steps(ap(b, N * u, (N + 1) * u), -1, 8 * ch[0], u, "run%d_%d" % (N, c))
         sgn.append(a)
         run.append(b)
-        rst.append(z)
     if paired:
         e0, e1, em, MK, MW, MA = new("pb", 72), new("pb", 72), new("pb", 72), new("pb", 144), new("pb", 144), new("pb", 144)
         for x, v in ((e0, 0.0), (e1, 1.0), (em, -2.0)):
@@ -393,6 +581,11 @@ def rank_program(g, core, T, topo):
         fill(ap(MK, 72, 144, 9), 0.0, [MK], 8)
         lin(ap(MW), ap(MK), 131072, 0, [MK, "MKa"], [MW], 144, 0.5)
         lin(ap(MA), ap(MK), 4096, 0, [MK, "MKa"], [MA], 144, 0.5)
+        if any(any(x) for x in OPT["one"]):
+            MP, MB = new("pf", 144), new("pb", 144)
+            lin(ap(MP), ap(MK), 131072 / TINY, 0, [MK, "MKa"], [MP], 144)
+            lin(ap(MP, 72, 144, 9), ap(e0, 0, 72, 9), -2.0 ** 56, 0, [e0], [MP], 8)
+            lin(ap(MB), ap(MK), 4096 / TINY, 0, [MK, "MKa"], [MB], 144, 0.5)
         lin(ap(MK, 72, 144, 9), ap(e0, 0, 72, 9), -32768, 0, [e0], [MK], 8)
 
     s1_, sm_, hb, hbm = new("pi", W), new("pi", W), new("pi", W), new("pi", W)
@@ -405,21 +598,17 @@ def rank_program(g, core, T, topo):
     lin(ap(lh0), ap(hbm), 1, 0, [hbm], [lh0], W)
     x, xa = lref(W)
     lin(ap(salB), ap(sm_).indirect(xa), 1, 0, [sm_, x], [salB], W, gather=True)
-    lists, bsh = [], []
-    for b0, subs, kb, s0, s1 in CH:
-        k0, w = 8 * b0, 8 * sum(subs)
-        bh = new("ph", 2 * w)
-        lin(ap(bh, 0, w), ap(beg, k0, k0 + w), 1, 0, [beg], [bh[3] + "a"], w)
-        lin(ap(bh, w, 2 * w), ap(hbm, k0, k0 + w), 1, 0, [hbm], [bh], w)
-        lists.append(((lb0, k0), (lh0, k0)))
-        bsh.append(bh)
+    bsh = [new("ph", W), new("ph", W)]
+    lin(ap(bsh[0]), ap(beg), 1, 0, [beg], [bsh[0]], W)
+    lin(ap(bsh[1]), ap(hbm), 1, 0, [hbm], [bsh[1]], W)
+    lists = [((lb0, 8 * ch[0]), (lh0, 8 * ch[0])) for ch in CH]
 
     def noise(r, a, b):
         return T.N2[:, (N - 1 - r) * GAP + a:(N - 1 - r) * GAP + b]
 
-    def ntok(r, parts=("w0", "w1", "h0", "h1", "l0", "l1")):
+    def ntok(r, parts=("h0", "h1", "l0", "l1")):
         return ["N%s_%d" % (x, r) for x in parts]
-    for a, parts in ((512, ("h0", "h1", "l0", "l1")), (0, ("w0", "w1"))):
+    for a, parts in ((0, ("h0", "l0")), (512, ("h1", "l1"))):
         lin(noise(me, a, a + 512), ap(nzs).indirect(ap(lmu, a // 16, a // 16 + 32)), 1, -32, [nzs, lmu], ntok(me, parts), 512, gather=True)
 
     def word(kind, h, r, a=0, b=None):
@@ -438,21 +627,45 @@ def rank_program(g, core, T, topo):
        + group(ps[pt][:, TRI:2 * TRI], [(ap(d16), R[:, rt + TRI:rt + 2 * TRI]), (ap(I), R[:, rt + 2 * TRI:rt + 3 * TRI]),
                                         (ap(dm16), ap(rch))], TRI), ["Rt%d" % me, rch, d16, dm16, I], pt)
     for h, v in enumerate((-2208, 512)):
-        lin(word("n", h, me, 128), ps[pt][:, h * TRI:(h + 1) * TRI], 1, v, (), ["t%d_%d" % (h, me)], TRI, banks=[pt], on="V")
-    terms(ps[pn][:, 0:256], [(d64, "Nh0_%d" % me, noise(me, 512, 768)), (I, "Nl0_%d" % me, noise(me, 768, 1024))], 256, True, True, pn)
-    for h in range(2):
-        lin(word("n", h, me, 0, 128), ps[pn][:, 128 * h:128 * (h + 1)], 1, 32, (), ["n%d_%d" % (h, me)], 128, banks=[pn], on="V")
-    terms(ps[pw][:], [(I, "Nw0_%d" % me, noise(me, 0, 512))], 512, True, False, pw)
-    mm([(ps[pw][:, 128 * j:128 * (j + 1)], ap(d64), ap(wts, c, B, 16), False, j == 3, 128) for j, c in enumerate(kids(me))], [wts, d64], pw)
-    at = me * FW + PIECE["w"][0]
-    lin(F[:, at:at + 512], ps[pw][:], 1, -2016, (), ["w0_%d" % me, "w1_%d" % me], 512, banks=[pw], on="v")
-    ts(ap(big), ap(kds, me, B, N), 64.0, None, ALU.is_ge, None, [kds], [big], B // N, 0.5)
-    mm([(ps[pk_][:, 128 * (j % 2):128 * (j % 2 + 1)], ap(dm1 if j > 1 else dm64), ap(kds, c, B, 16), j == 0, False, 128)
-        for j, c in enumerate(kids(me))], [kds, dm64, dm1], pk_)
-    mm([(ps[pk_][:, 128 * (j % 2):128 * (j % 2 + 1)], ap(d64 if j > 1 else d4096), ap(big, j, B // N, N), False, j == 3, 128)
-        for j in range(N)], [big, d64, d4096], pk_)
-    at = me * FW + PIECE["k"][0]
-    lin(F[:, at:at + 256], ps[pk_][:, 0:256], 1, 2047, (), ["k0_%d" % me, "k1_%d" % me], 256, banks=[pk_], on="v")
+        lin(word("t", h, me), ps[pt][:, h * TRI:(h + 1) * TRI], 1, v, (), ["t%d_%d" % (h, me)], TRI, banks=[pt], on="V")
+    for h, b in enumerate((pn, pk_)):
+        terms(ps[b][:, 0:256], [(d64, "Nh%d_%d" % (h, me), noise(me, 512 * h, 512 * h + 256)),
+                                (I, "Nl%d_%d" % (h, me), noise(me, 512 * h + 256, 512 * h + 512))], 256, True, True, b)
+        lin(word("n", h, me, 0, 256), ps[b][:, 0:256], 1, 32, (), ["n%d_%d" % (h, me)], 256, banks=[b])
+    ONE = OPT["one"]
+    lin(ap(big), ap(kds, me, B, N), 1 / 64, 192 - 63.5 / 128, [kds], [big], B // N, 0.5, on="v")
+    if ONE[0][1]:
+        for h, b in enumerate((pw, pk_)):
+            js = [(j, kids(me)[2 * h + j], ps[b][:, 128 * j:128 * (j + 1)]) for j in range(2)]
+            mm([(o_, ap(d64), ap(wts, c, B, 16), j == 0, False, 128) for j, c, o_ in js], [wts, d64], b)
+            mm([(o_, ap(dm1), ap(kds, c, B, 16), False, False, 128) for j, c, o_ in js], [kds, dm1], b)
+            mm([(o_, ap(d64), ap(big, 2 * h + j, B // N, N), False, j == 1, 128) for j, c, o_ in js], [big, d64], b)
+            lin(word("x", h, me), ps[b][:, 0:256], 1, 63 - 2048, (), ["x%d_%d" % (h, me)], 256, banks=[b], on="va"[h])
+    else:
+        mm([(ps[pw][:, 128 * (j % 2):128 * (j % 2 + 1)], ap(I if j > 1 else d64), ap(wts, c, B, 16), j == 0, j == 3, 128)
+            for j, c in enumerate(kids(me))], [wts, d64, I], pw)
+        at = me * FW + PIECE["w"][0]
+        lin(F[:, at:at + 256], ps[pw][:, 0:256], 1, -2048, (), ["w0_%d" % me, "w1_%d" % me], 256, banks=[pw], on="v")
+        mm([(ps[pk_][:, 128 * (j % 2):128 * (j % 2 + 1)], ap(dm1 if j > 1 else dm64), ap(kds, c, B, 16), j == 0, False, 128)
+            for j, c in enumerate(kids(me))], [kds, dm64, dm1], pk_)
+        mm([(ps[pk_][:, 128 * (j % 2):128 * (j % 2 + 1)], ap(d64 if j > 1 else d4096), ap(big, j, B // N, N), False, j == 3, 128)
+            for j in range(N)], [big, d64, d4096], pk_)
+        at = me * FW + PIECE["k"][0]
+        lin(F[:, at:at + 256], ps[pk_][:, 0:256], 1, 2047 - 192 * 4160, (), ["k0_%d" % me, "k1_%d" % me], 256, banks=[pk_], on="v")
+    bone = [new("pf", 1), new("pf", 1)]
+    if any(x[0] for x in ONE):
+        lin(ap(bone[0]), ap(bon[0]), EPS * TINY, 0, [bon[0]], [bone[0]], 1)
+        for j in range(4):
+            b = OPT["build"][j % len(OPT["build"])]
+            terms(ps[b][:], [(I, wts, ap(wts, 512 * j, 512 * j + 512)), (diag(EPS), kds, ap(kds, 512 * j, 512 * j + 512))], 512, True, True, b)
+            lin(T.P1[:, 512 * j:512 * j + 512], ps[b][:], TINY, ap(bone[0]), [bone[0]], ["P1_%d" % j], 512, banks=[b])
+    if ONE[0][1]:
+        ones = new("pb", 256)
+        fill(ap(ones), 1.0, [ones], 128)
+        lin(ap(bone[1]), ap(bon[1]), EPS * TINY, (160 + 12288) * EPS * TINY, [bon[1]], [bone[1]], 1)
+    if any(any(x) for x in ONE):
+        dP = new("pf", 128)
+        lin(ap(dP), ap(I), 131072 / TINY, 0, [I], [dP], 128)
 
     out_e = topo.engines(core, cores[far[0]])
     all_e = topo.engines(core, cores[mate])
@@ -463,7 +676,7 @@ def rank_program(g, core, T, topo):
         if kind in "rs":
             a, n = (0, RA // 2) if kind == "r" else (RA, (RAW - RA) // 2)
             return R[:, r * D + a + h * n:r * D + a + (h + 1) * n]
-        return word(kind, h, r)
+        return word(kind, h, r) if h < 2 else word(kind, 0, r, 0, 2 * PIECE[kind][1])
 
     def send(items, rd):
         def fn():
@@ -471,7 +684,7 @@ def rank_program(g, core, T, topo):
             for kind, h, r, to, es in items:
                 rid, pid = topo.addr(cores[to], core)
                 tr.append(RemoteDMATransfer(dst_ids=[DstId(rid=rid, pnc=pid)], dma_engine_mask=sum(1 << e for e in es),
-                                            remote_sem=T.sem["%s%d_%d" % (kind, h, r)], src=piece(kind, h, r), dst=piece(kind, h, r)))
+                                            remote_sem=T.sem["%s%d_%d" % (kind, h % 2, r)], src=piece(kind, h, r), dst=piece(kind, h, r)))
             g.remote_dma_fused(tr, local_sem=T.sem.sent)
             return None
         sent[0] += sum(len(it[4]) for it in items)
@@ -479,121 +692,143 @@ def rank_program(g, core, T, topo):
         gorder.append(i)
         return i
 
-    def arrive(kind, h, r, n, after, lat):
-        name = "%s%d_%d" % (kind, h, r)
-        return op(None, None, (), [name], cost=(0.0, 0, 0, 0), lat=lat, sem=(name, n), after=[after])
+    def arrive(kind, h, r, n, after, lat, on=None):
+        return op(None, None, (), ["%s%d_%d" % (kind, h, r)], cost=(0.0, 0, 0, 0), lat=lat,
+                  sem=("%s%d_%d" % (kind, h if on is None else on, r), n), after=[after])
 
     def part(es, k, n):
         return es[k * len(es) // n:(k + 1) * len(es) // n]
     landed = []
     for kind, near, away in OPT["sends"]:
         if kind.islower():
-            rd = ["%s%d_%d" % (x, h, me) for x in (kind + "t" if kind == "n" else kind) for h in range(2)]
-            outs = [(h, f) for h in range(2) for f in range(2) if f == h or kind in OPT["direct"]]
+            rd = ["%s%d_%d" % (kind, h, me) for h in range(2)]
+            if kind in OPT["direct"]:
+                i = send([(kind, 2, me, far[f], part(out_e, f, 2)) for f in range(2)] + [(kind, 2, me, mate, in_e)], rd)
+                for h in range(2):
+                    arrive(kind, h, mate, len(in_e), i, near, 0)
+                for h in range(2):
+                    for f in far:
+                        arrive(kind, h, f, len(out_e) // 2, i, away, 0)
+                landed += [(kind, (0, 1), r) for r in [mate] + far]
+                continue
+            outs = [(h, h) for h in range(2)]
             i = send([(kind, h, me, far[f], part(out_e, n_, len(outs))) for n_, (h, f) in enumerate(outs)]
                      + [(kind, h, me, mate, part(in_e, h, 2)) for h in range(2)], rd)
             for h in range(2):
                 arrive(kind, h, mate, len(in_e) // 2, i, near)
             for h, f in outs:
                 arrive(kind, h, far[f], len(out_e) // len(outs), i, away)
-            landed += [(kind, (0, 1), mate)] + ([(kind, (0, 1), f) for f in far] if kind in OPT["direct"] else
-                                                [(kind, (h,), far[h]) for h in range(2)])
+            landed += [(kind, (0, 1), mate)] + [(kind, (h,), far[h]) for h in range(2)]
         else:
-            kind = kind.lower()
-            es = all_e if OPT["hand"] == "all" else in_e
-            i = send([(kind, h, far[h], mate, part(es, h, 2)) for h in range(2)], ["%s%d_%d" % (kind, h, far[h]) for h in range(2)])
-            for h in range(2):
-                arrive(kind, h, far[1 - h], len(es) // 2, i, near)
-            landed += [(kind, (h,), far[1 - h]) for h in range(2)]
-    for h, n in enumerate((H, H, 336)):
-        dma("s", T.N1[:, h * H:h * H + n], noise(me, 0, n), ntok(me) + ["s0_%d" % far[1]], ["N1_%d" % h], 3000)
+            es = all_e if kind in OPT["hand"] else in_e
+            its = [(x, h) for x in kind.lower() for h in range(2)]
+            i = send([(x, h, far[h], mate, part(es, n_, len(its))) for n_, (x, h) in enumerate(its)],
+                     ["%s%d_%d" % (x, h, far[h]) for x, h in its])
+            for x, h in its:
+                arrive(x, h, far[1 - h], len(es) // len(its), i, near)
+            landed += [(x, (h,), far[1 - h]) for x, h in its]
+    for h, n in enumerate((H, H, 384)):
+        dma("s", T.N1[:, h * H:h * H + n], noise(me, 0, n), ntok(me) + ["n0_%d" % far[1]], ["N1_%d" % h], 2700 + 700 * h)
+    if ONE[1][0]:
+        dma("s", T.P1[:, B:B + MORE], T.P1[:, 0:MORE], ["P1_0", "P1_1", "P1_2", "n0_%d" % far[1]], ["P1_4"], 6000)
+    if ONE[2][0]:
+        dma("s", T.P1[:, B + MORE:B + 2 * MORE], T.P1[:, MORE:2 * MORE], ["P1_2", "P1_3", "P1_4"], ["P1_5"], 4000)
+    else:
+        for x, y, z in ((wts, "wx", "wy"), (kds, "kx", "ky")):
+            dma("s", ap(x, B + MORE, B + 2 * MORE), ap(x, MORE, 2 * MORE), [x, y, "N1_2"], [z], 4000)
 
     turnb = [0]
 
-    def spare():
+    def spare(late):
         turnb[0] += 1
-        return OPT["spare"][turnb[0] % len(OPT["spare"])]
+        x = OPT["spare"][late]
+        return x[turnb[0] % len(x)]
 
     def block(tab, c):
         return tab[:, 256 * (15 - c):256 * (15 - c) + 128]
 
     def unpack(kind, hs, r):
-        if kind in "rs":
+        if kind in "rst":
             return
-        b, n, ks = spare(), PIECE[kind][1] if kind != "n" else 128, kids(r)
-        tm, rd = [], [I, dm64]
-        for n_, h in enumerate(hs):
-            src = "%s%d_%d" % (kind, h, r)
-            tm.append((ps[b][:, n_ * n:(n_ + 1) * n], ap(I), word(kind, h, r, 0, n), n_ == 0, False, n))
-            rd.append(src)
-            for y in range(n // 128):
-                if kind == "n":
-                    z = new("pb", 128)
-                    hi, name = ap(z), z
-                else:
-                    j = 2 * h + y if kind == "w" else h
-                    hi, name = block(T.W2 if kind == "w" else T.KK, ks[j]), "%s%d_%d" % (kind.upper(), j, r)
-                lin(hi, word(kind, h, r, 128 * y, 128 * (y + 1)), 1 / 64, 192 - 31.5 / 64, [src], [name], 128, 0.5, on="v")
-                if kind == "n":
-                    lin(noise(r, 512 + 128 * h, 640 + 128 * h), hi, 1, -192, [z], ["Nh%d_%d" % (h, r)], 128, 0.5, on="v")
-                tm.append((ps[b][:, n_ * n + 128 * y:n_ * n + 128 * (y + 1)], ap(dm64), hi, False, False, 128))
-                rd.append(name)
+        ks, tab = kids(r), T.W2 if kind == "w" else T.KK
+        if kind == "x":
+            for h in hs:
+                b, hi, src = spare(r != me), new("pb", 256), "x%d_%d" % (h, r)
+                lin(ap(hi), word("x", h, r), 1 / 64, 192 - 31.5 / 64, [src], [hi], 256, 0.5, on="v")
+                terms(ps[b][:, 0:256], [(diag(-160), ones, ap(ones))], 256, True, False, b)
+                terms(ps[b][:, 0:256], [(diag(2047 / 2048), hi, ap(hi)), (diag(EPS), src, word("x", h, r))], 256, False, True, b)
+                for j in range(2):
+                    lin(block(T.P2, ks[2 * h + j]), ps[b][:, 128 * j:128 * (j + 1)], TINY, ap(bone[1]), [bone[1]],
+                        ["Q%d_%d" % (2 * h + j, r)], 128, banks=[b], on="AV"[(h + r - me) % 2])
+            return
         if kind == "w" and r == me:
+            for j, c in enumerate(ks):
+                lin(block(tab, c), ap(wts, c, B, 16), 1, 160, [wts], ["W%d_%d" % (j, r)], 128, 0.5)
             return
-        mm(tm[:-1] + [tm[-1][:4] + (True, 128)], rd, b)
-        if kind == "k":
-            for n_, h in enumerate(hs):
-                lin(block(T.KK, ks[h + 2]), ps[b][:, 128 * n_:128 * (n_ + 1)], 1, 12448, (), ["K%d_%d" % (h + 2, r)], 128, banks=[b])
-        else:
-            a = (0 if kind == "w" else 768) + n * hs[0]
-            lin(noise(r, a, a + n * len(hs)), ps[b][:, 0:n * len(hs)], 1, 12256, (),
-                ["N%s%d_%d" % ("w" if kind == "w" else "l", h, r) for h in hs], n * len(hs), banks=[b])
+        for h in hs:
+            b, n, src = spare(r != me and not (kind == "n" and r in (mate, far[h]))), 256 if kind == "n" else 128, "%s%d_%d" % (kind, h, r)
+            if kind == "n":
+                name = new("pb", n)
+                hi = ap(name)
+            else:
+                hi, name = block(tab, ks[h]), "%s%d_%d" % (kind.upper(), h, r)
+            lin(hi, word(kind, h, r, 0, n), 1 / 64, 192 - 31.5 / 64, [src], [name], n, 0.5, on="v")
+            mm(group(ps[b][:, 0:n], [(ap(I), word(kind, h, r, 0, n)), (ap(dm64), hi)], n), [I, dm64, src, name], b)
+            if kind == "n":
+                lin(noise(r, 512 * h, 512 * h + n), hi, 1, -192, [name], ["Nh%d_%d" % (h, r)], n, 0.5, on="v")
+                lin(noise(r, 512 * h + n, 512 * h + 2 * n), ps[b][:, 0:n], 1, 12256, (), ["Nl%d_%d" % (h, r)], n, banks=[b])
+            else:
+                lin(block(tab, ks[h + 2]), ps[b][:, 0:n], 1, 12448, (), ["%s%d_%d" % (kind.upper(), h + 2, r)], n, banks=[b])
 
     def unpack_rooms(r):
-        b, hh = spare(), new("ph", 2 * TRI)
-        x = [word("n", h, r, 128) for h in range(2)]
+        b, hh = spare(0), new("ph", 2 * TRI)
+        x = [word("t", h, r) for h in range(2)]
         for h in range(2):
-            lin(ap(hh, h * TRI, (h + 1) * TRI), x[h], 1 / 16, 1408 - 7.5 / 16, ["n%d_%d" % (h, r)], [hh[3] + str(h)], TRI, 0.5, on="v")
+            lin(ap(hh, h * TRI, (h + 1) * TRI), x[h], 1 / 16, 1408 - 7.5 / 16, ["t%d_%d" % (h, r)], [hh[3] + str(h)], TRI, 0.5, on="v")
         dm256 = diag(-256)
         mm(group(ps[b][:, 0:2 * TRI], [(ap(I), ap(hh))], 2 * TRI)
            + group(ps[b][:, 2 * TRI:3 * TRI], [(ap(d16), x[0]), (ap(dm256), ap(hh, 0, TRI)), (ap(I), x[1]),
                                                (ap(dm16), ap(hh, TRI, 2 * TRI))], TRI),
-           [hh[3] + "0", hh[3] + "1", "n0_%d" % r, "n1_%d" % r, I, d16, dm256, dm16], b)
+           [hh[3] + "0", hh[3] + "1", "t0_%d" % r, "t1_%d" % r, I, d16, dm256, dm16], b)
         a = r * D + RAW
         lin(R[:, a:a + 2 * TRI], ps[b][:, 0:2 * TRI], 1, -1280, (), ["Rt%d" % r], 2 * TRI, banks=[b])
         lin(R[:, a + 2 * TRI:a + 3 * TRI], ps[b][:, 2 * TRI:3 * TRI], 1, 17 * 22528, (), ["Ru%d" % r], TRI, banks=[b])
 
-    d131 = diag(131072)
-    rotm, rotc = diag(-16, 240), diag(2047 if OPT["cq"] else 2047 / 128, 240)
+    rotm, rotc = diag(-16 / UNIT, 240), diag(2047, 240)
 
     def draw(c, second, pair, lb, lh, wtab, ktab, ntab, rw, rk, rn):
         b0, subs, kb = CH[c][:3]
         lead[0] = float(len(CH) - 1 - c)
         w = 8 * sum(subs)
-        wp = (w + 15) // 16 * 16 if second else 2 * w
+        wp = (w + 15) // 16 * 16
         ends = [sum(subs[:u]) for u in range(len(subs) + 1)]
-        cuts = [[(0, ends[-1], range(len(subs)))], [(ends[u], ends[u + 1], (u,)) for u in range(len(subs))]]
-        for buf, nm, tab, rd_, k in ((T.Wg, "Wg", wtab, rw, 0), (T.Kg, "Kg", ktab, rk, 1)):
-            for x0, x1, us in cuts[OPT["split"][k]]:
+        cuts = [[(sum(x[:u]), sum(x[:u + 1])) for u in range(len(x))] for x in OPT["split"][c]]
+
+        def blocks(nm, x0, x1):
+            return ["%s_%d" % (nm, b0 + m) for m in range(x0, x1)]
+        one = ktab is None
+        wbuf, wnm = (T.Pg, "Pg") if one else (T.Wg, "Wg")
+        for buf, nm, tab, rd_, k in ((wbuf, wnm, wtab, rw, 0), (T.Kg, "Kg", ktab, rk, 1))[:2 - one]:
+            for x0, x1 in cuts[k]:
                 lin(buf[:, 128 * (b0 + x0):128 * (b0 + x1)], tab.indirect(ap(lb[0], lb[1] + 8 * x0, lb[1] + 8 * x1)), 1,
-                    ap(bon[second]) if k else -160 * second, rd_ + [lb[0]] + ([bon[second]] if k else []),
-                    ["%s_%d_%d" % (nm, c, u) for u in us], 128 * (x1 - x0), gather=True)
-        for x0, x1, us in cuts[OPT["split"][2]]:
+                    ap(bon[second]) if k else -160 * (second and not one), rd_ + [lb[0]] + ([bon[second]] if k else []),
+                    blocks(nm, x0, x1), 128 * (x1 - x0), gather=True)
+        for x0, x1 in cuts[2]:
             a, e = 128 * (b0 + x0), 128 * (b0 + x1)
-            tt(T.A[:, a:e], ntab.indirect(ap(lh[0], lh[1] + 8 * x0, lh[1] + 8 * x1)), T.Wg[:, a:e], ALU.mult,
-               rn + [lh[0]] + ["Wg_%d_%d" % (c, u) for u in us], ["A_%d_%d" % (c, u) for u in us], e - a, gather=True)
+            tt(T.A[:, a:e], ntab.indirect(ap(lh[0], lh[1] + 8 * x0, lh[1] + 8 * x1)), wbuf[:, a:e], ALU.mult,
+               rn + [lh[0]] + blocks(wnm, x0, x1), blocks("A", x0, x1), e - a, gather=True)
         for u, nb in enumerate(subs):
             a, bk, tk = b0 + ends[u], kb[u], "_%d_%d" % (c, u)
-            for buf, nm, mat, mp in ((T.Wg, "Wg", d131, 0), (T.Kg, "Kg", I, 1), (T.A, "A", d4096, 2)):
-                first, last = nm == "Wg", nm == "A"
-                if pair:
-                    mat = (MW, MK, MA)[mp]
-                    mm([(ps[bk][:, 256 * y + 72 * m:256 * y + 72 * (m + 1)], buf[:, 128 * (a + m):128 * (a + m + 1)], ap(mat, 72 * y, 72 * y + 72),
-                         first and m == 0 and y == 0, last and m == nb - 1 and y == 1, 72) for m in range(nb) for y in range(2)],
-                       [nm + tk, mat, "MKa"], bk)
-                else:
-                    mm([(ps[bk][:, 128 * m:128 * (m + 1)], buf[:, 128 * (a + m):128 * (a + m + 1)], ap(mat), first and m == 0,
-                         last and m == nb - 1, 128) for m in range(nb)], [nm + tk, mat], bk)
+            if one:
+                parts = [(T.Pg, "Pg", MP if pair else dP, [m], 4) for m in range(nb)] + [(T.A, "A", MB if pair else diag(4096 / TINY), range(nb), 1)]
+            else:
+                parts = [(T.Wg, "Wg", diag(32), range(nb), 1), (T.Kg, "Kg", diag(UNIT), range(nb), 1), (T.A, "A", I, range(nb), 1)]
+            for n_, (buf, nm, mat, ms, dear) in enumerate(parts):
+                tm = [(ps[bk][:, 256 * y + 72 * m:256 * y + 72 * (m + 1)] if pair else ps[bk][:, 128 * m:128 * (m + 1)],
+                       buf[:, 128 * (a + m):128 * (a + m + 1)], ap(mat, 72 * y, 72 * y + 72) if pair else ap(mat), (72 if pair else 128) * dear)
+                      for m in ms for y in range(1 + pair)]
+                mm([(o_, l_, r_, n_ == 0 and i == 0, nm == "A" and i == len(tm) - 1, n) for i, (o_, l_, r_, n) in enumerate(tm)],
+                   blocks(nm, ends[u] + ms[0], ends[u] + ms[-1] + 1) + [mat] + ["MKa"] * pair, bk)
             if pair:
                 n = 72 * nb
                 act(T.Rl[:, 72 * a:72 * a + n], ps[bk][:, 0:n], 0.0, (), ["Rl" + tk], n, AF.Relu, banks=[bk])
@@ -604,55 +839,60 @@ def rank_program(g, core, T, topo):
                 scan(T.Z[:, 128 * a:128 * a + n], ap(pat, 0, n), ps[bk][:, 0:n], ALU.add, ALU.max, [pat], ["Z" + tk], n, banks=[bk])
         zs = ["%s_%d_%d" % ("Z9" if pair else "Z", c, u) for u in range(len(subs))]
         win = T.Z9[:, 72 * b0:72 * (b0 + ends[-1])] if pair else T.Z[:, 128 * b0:128 * (b0 + ends[-1])]
-        x, xa = lref(w, 9, 8, not second) if pair else lref(w, 16, 15, not second)
-        hn, low, cq = new("pf", wp), new("ph", wp), new("ph", wp)
-        ts(ap(hn), win.indirect(xa), BIG, -BIG, ALU.add, ALU.add, zs + [x], [hn], wp, gather=True)
+        x, xa = lref(w, 9, 8) if pair else lref(w, 16, 15)
+        hn, low, cq = new("pi", wp), new("ph", wp), new("ph", wp)
+        lin(ap(hn), win.indirect(xa), 1, 0, zs + [x], [hn], wp, gather=True)
         tt(ap(low), win.indirect(xa), ap(hn), ALU.subtract, zs + [x, hn], [low], wp, gather=True)
-        if second and OPT["cq"]:
-            lin(ap(cq), ap(low), 1 / 128, 1536, [low], [cq], wp, 0.5)
-        elif second:
-            h2 = new("pf", wp)
-            ts(ap(h2), win.indirect(xa), BIG / 32, -BIG / 32, ALU.add, ALU.add, zs + [x], [h2], wp, gather=True)
-            tt(ap(cq), ap(h2), ap(hn), ALU.subtract, [h2, hn], [cq], wp)
+        if second:
+            lin(ap(cq), ap(low), 1 / 128 / UNIT, 1536, [low], [cq], wp, 0.5)
         return low, cq
 
-    def turn(b, at, w, mat, x, stop):
-        return [(ps[b][:, at + (-r) % 8:at + w:8], ap(mat, 16 * r, 16 * r + 128), ap(x, r, w, 8), False, stop and r == 7, w // 8)
+    def turn(b, at, w, mat, x, stop, start=False):
+        return [(ps[b][:, at + (-r) % 8:at + w:8], ap(mat, 16 * r, 16 * r + 128), ap(x, r, w, 8), start and r == 0, stop and r == 7, w // 8)
                 for r in range(8)]
 
     def modulo(tm, b, at, n, m):
         z = new("pb", n)
         terms(ps[b][:, at:at + n], tm, n, True, True, b)
         lin(ap(z), ps[b][:, at:at + n], 1 / m, 191.5 + 1 / 4096, (), [z], n, banks=[b])
-        return tm + [(diag(-m), z, ap(z)), (diag(m // 8), c1536, ap(c1536, 0, n))]
+        return tm + [(diag(-m), z, ap(z)), (diag(m / 8), c1536, ap(c1536, 0, n))]
 
     st = [{"fl": [], "fb": []} for _ in CH]
     W2r, KKr = [["%s%d_%d" % (x, j, r) for r in range(N) for j in range(N)] for x in "WK"]
     N2r = [x for r in range(N) for x in ntok(r)]
     Rr = (["%s%d_%d" % (x, h, r) for x in "rs" for h in range(2) for r in range(N)] + ["Rt%d" % r for r in range(N)]
           + ["Ru%d" % r for r in range(N) if r != me])
-    unpack("w", (0, 1), me)
+    P2r = ["Q%d_%d" % (j, r) for r in range(N) for j in range(N)]
+    if not ONE[0][1]:
+        unpack("w", (0, 1), me)
+    landed = [("kx"[ONE[0][1]], (0, 1), me)] + [x for x in landed if x[0] not in "rst"]
+    for kind, hs, r in landed[:OPT["soon"]]:
+        unpack(kind, hs, r)
     for rnd in range(3):
         owns, l2 = [], []
-        for c, (b0, subs, kb, s0, s1) in enumerate(CH):
+        for c, (b0, subs, kb, s0, s1, cb) in enumerate(CH):
             k0, w = 8 * b0, 8 * sum(subs)
             wp = (w + 15) // 16 * 16
             if rnd == 0:
                 tabs = (ap(wts, 0, B), ap(kds, 0, B), noise(me, 0, H), [wts], [kds], ntok(me))
             else:
-                tabs = (ap(wts), ap(kds), T.N1[:], [wts, "wx"], [kds, "kx"], ["N1_0", "N1_1", "N1_2"])
+                tabs = (ap(wts, 0, B + rnd * MORE), ap(kds, 0, B + rnd * MORE), T.N1[:, 0:B + 384 * (rnd - 1)], [wts, "wx", "wy"][:1 + rnd],
+                        [kds, "kx", "ky"][:1 + rnd], ["N1_0", "N1_1", "N1_2"][:1 + rnd])
+            if ONE[rnd][0]:
+                tabs = (T.P1[:, 0:B + rnd * MORE], None, tabs[2], ["P1_%d" % j for j in range(4 + rnd)], None, tabs[5])
             low, _ = draw(c, 0, OPT["pairs"][rnd][0], lists[c][0], lists[c][1], *tabs)
-            tm = [(diag(1 / 16), salB, ap(salB, k0, k0 + w))]
+            u = UNIT / 16
+            tm = [(diag(u), salB, ap(salB, k0, k0 + w))]
             for fb in st[c]["fb"]:
-                tm += [(diag(KT / 16), fb, ap(fb, 0, w)), (diag(-KT / 16), fb, ap(fb, w, 2 * w))]
+                tm += [(diag(KT * u), fb, ap(fb, 0, w)), (diag(-KT * u), fb, ap(fb, w, 2 * w))]
             if rnd:
-                tm = modulo(tm, s1, 384, w, H // 16)
-            terms(ps[s0][:, 0:w], [(I, c1536, ap(c1536, 0, w))], w, True, False, s0)
-            terms(ps[s0][:, w:2 * w], tm, w, False, False, s0)
-            mm(turn(s0, 0, 2 * w, wide1, low, True), [low, wide1, "wide1b"], s0)
+                tm = modulo(tm, cb, 384, w, H * u)
+            mm(turn(s0, 0, w, wide1, low, True, True), [low, wide1, "wide1b"], s0)
+            terms(ps[cb][:, 0:w], tm, w, True, False, cb)
+            mm(turn(cb, 0, w, wide1, low, True), [low, wide1, "wide1b"], cb)
             iv, hm, lb, lh = new("pi", w), new("pi", w), new("pu", w), new("pu", w)
-            lin(ap(lb), ps[s0][:, 0:w], 1, B - 1 - 1536, (), [lb], w, banks=[s0], on="V")
-            lin(ap(iv), ps[s0][:, w:2 * w], ALPHA, (B - 1) * ALPHA + 15.373, (), [iv], w, banks=[s0], on="V")
+            lin(ap(lb), ps[s0][:, 0:w], 1 / UNIT, B - 1, (), [lb], w, banks=[s0], on="v")
+            lin(ap(iv), ps[cb][:, 0:w], ALPHA / UNIT, (B - 1) * ALPHA + 15.373, (), [iv], w, banks=[cb], on="v")
             ts(ap(hm), ap(iv), (N - 1) * GAP + H - 1, None, ALU.bitwise_and, None, [iv], [hm], w)
             lin(ap(lh), ap(hm), 1, 0, [hm], [lh], w, on="v")
             x, xa = lref(w)
@@ -662,16 +902,10 @@ def rank_program(g, core, T, topo):
             l2.append((lb, lh))
         if rnd == 0:
             lead[0] = float(len(CH) - 1)
-            unpack("k", (0, 1), me)
-            seen = {}
-            for kind, hs, r in landed:
+            for kind, hs, r in landed[OPT["soon"]:]:
                 unpack(kind, hs, r)
-                seen[(kind, r)] = seen.get((kind, r), 0) + len(hs)
-            for kind, hs, r in landed:
-                if kind == "n" and seen.pop((kind, r), 0):
-                    unpack_rooms(r)
         j0 = 0 if rnd == 2 else 1
-        for c, (b0, subs, kb, s0, cb) in enumerate(CH):
+        for c, (b0, subs, kb, s0, s1, cb) in enumerate(CH):
             w = 8 * sum(subs)
             u = w + 1
             lead[0] = float(len(CH) - 1 - c)
@@ -687,8 +921,8 @@ def rank_program(g, core, T, topo):
                     ["run%d_%d" % (j, c - 1) for j in range(j0, N)], ["carry%d" % c] + mt[:1 - j0], N)
             for j in range(j0, N):
                 act(ap(sn, j * u + 1, (j + 1) * u), ap(src, 0, w), -193.5 - j, [src], [mt[j]], w, AF.Sign)
-            scan(ap(rn, j0 * u, N * u), ap(rst[c], 0, (N - j0) * u), ap(sn, j0 * u, N * u), ALU.mult, ALU.add,
-                 mt[j0:N] + [rst[c], "carry%d" % c], rt_[j0:N], (N - j0) * u, 0.5)
+            scan(ap(rn, j0 * u, N * u), ap(rst[u], 0, (N - j0) * u), ap(sn, j0 * u, N * u), ALU.mult, ALU.add,
+                 mt[j0:N] + [rst[u], "carry%d" % c], rt_[j0:N], (N - j0) * u, 0.5)
             sg = new("pb", N * u)
             mm(group(ps[cb][:, 128:128 + N * u], [(ap(tri), ap(sn, 0, N * u)), (ap(ntri), ap(sn, u, (N + 1) * u))], N * u, True, False),
                mt + ["carry%d" % c, tri, ntri], cb)
@@ -699,18 +933,33 @@ def rank_program(g, core, T, topo):
             fl = new("pb", 2 * w)
             lin(ap(fl, 0, w), ps[cb][:, 64:64 + w], 1, 4 if rnd < 2 else -15, (), [fl[3] + "g"], w, banks=[cb])
             st[c]["fl"].append(fl)
-        for c, (b0, subs, kb, s0, s1) in enumerate(CH):
+            if rnd < 2:
+                st[c]["next"] = [[(I, bsh[y], ap(bsh[y], 8 * b0, 8 * b0 + w))]
+                                 + [(diag(2 * step % m // 2), f[3] + "g", ap(f, 0, w)) for f in st[c]["fl"]]
+                                 + [(diag(-step % m), f, ap(f, w, 2 * w)) for f in st[c]["fl"][:rnd]]
+                                 for y, (step, m) in enumerate(((K5, B), (KH, H)))]
+                if OPT["fuse"]:
+                    st[c]["lf"] = new("pf", w)
+                    terms(ps[cb][:, 384:384 + w], st[c]["next"][0], w, True, True, cb)
+                    lin(ap(st[c]["lf"]), ps[cb][:, 384:384 + w], 1, 0, (), [st[c]["lf"]], w, banks=[cb])
+        if rnd == 0:
+            lead[0] = float(len(CH) - 1)
+            for r in (mate, far[0], far[1]):
+                unpack_rooms(r)
+        for c, (b0, subs, kb, s0, s1, cb) in enumerate(CH):
             k0, w = 8 * b0, 8 * sum(subs)
             S = st[c]
             fl = S["fl"][rnd]
-            low, cq = draw(c, 1, OPT["pairs"][rnd][1], (l2[c][0], 0), (l2[c][1], 0), T.W2[:], T.KK[:], T.N2[:], W2r, KKr, N2r)
+            low, cq = draw(c, 1, OPT["pairs"][rnd][1], (l2[c][0], 0), (l2[c][1], 0),
+                           *((T.P2[:], None, T.N2[:], P2r, None, N2r) if ONE[0][1] else (T.W2[:], T.KK[:], T.N2[:], W2r, KKr, N2r)))
             lr = new("pu", w)
             dv = ps[s0][:, 128:128 + w]
-            terms(dv, [(diag(-D), owns[c], ap(owns[c], 0, w)), (diag(132 - 2047 * OPT["cq"]), c1536, ap(c1536, 0, w))], w, True, False, s0)
+            terms(dv, [(diag(-D), owns[c], ap(owns[c], 0, w)), (diag(132 - 2047), c1536, ap(c1536, 0, w))], w, True, False, s0)
             mm(turn(s0, 128, w, rotm, low, False), [low, rotm], s0)
             mm(turn(s0, 128, w, rotc, cq, True), [cq, rotc], s0)
-            lin(ap(lr), dv, 1, -1, (), [lr], w, banks=[s0], on="V")
-            one_ = I if rnd < 2 else diag(OFF)
+            lin(ap(lr), dv, 1, -1, (), [lr], w, banks=[s0], on=OPT["lr"])
+            fuse = OPT["fuse"] or rnd == 2
+            one_ = diag(OFF) if fuse else I
             extra = [(one_, fl[3] + "g", ap(fl, 0, w))]
             if rnd > 0:
                 ne = new("pb", w)
@@ -721,37 +970,52 @@ def rank_program(g, core, T, topo):
                 tt(ap(da), dv, ap(S["ha"]), ALU.add, [S["ha"]], [da], w, 1.0, banks=[s0])
                 tt(ap(db), dv, ap(S["hb"]), ALU.add, [S["hb"]], [db], w, 1.0, banks=[s0])
             else:
+                tb_, th_ = S["next"]
                 lraw = ps[s0][:, 192:192 + 2 * w]
-                z = new("pb", 2 * w)
-                for b, at in ((s1, 256), (s0, 192)):
-                    tm, rd = [(ps[b][:, at:at + 2 * w], ap(I), ap(bsh[c]), True, False, 2 * w)], [bsh[c], bsh[c][3] + "a", I]
-                    for n_, f in enumerate(S["fl"]):
-                        for y, (go, back) in enumerate(((K5, B - K5), (KH, H - KH))):
-                            o_ = ps[b][:, at + y * w:at + (y + 1) * w]
-                            tm.append((o_, ap(diag(go)), ap(f, 0, w), False, False, w))
-                            rd += [diag(go), f[3] + "g"]
-                            if n_ < rnd:
-                                tm.append((o_, ap(diag(back)), ap(f, w, 2 * w), False, False, w))
-                                rd += [diag(back), f]
-                    if b == s1:
-                        mm(tm[:-1] + [tm[-1][:4] + (True, w)], rd, b)
-                        lin(ap(z), ps[b][:, at:at + 2 * w], 1 / B, 191.5 + 1 / 4096, (), [z], 2 * w, banks=[b])
-                    else:
-                        mm(tm + [(lraw, ap(diag(-B)), ap(z), False, False, 2 * w)], rd + [diag(-B), z], b)
+                if s0 != s1:
+                    terms(ps[s0][:, 192 + w:192 + 2 * w], th_, w, True, False, s0)
+                if fuse:
+                    lf, u = S["lf"], w + 1
+                    extra = tb_ + [(diag(-96), c1536, ap(c1536, 0, w)), (diag(B - K5), "sgn0_%d" % c, ap(sgn[c], 1, u))] + extra
+                    if rnd:
+                        extra.insert(0, (one_, "sgn%d_%d" % (N, c), ap(sgn[c], N * u + 1, (N + 1) * u)))
+                else:
+                    terms(ps[s0][:, 192:192 + w], tb_, w, False, False, s0)
             a, n = 128 * b0, 16 * w
-            tt(T.Ft[:, a:a + n], R[:].indirect(ap(lr)), ap(nds, a, a + n), ALU.is_ge, Rr + [lr, nds], ["Ft%d" % c], n, gather=True)
+            x0, fts = 0, []
+            for nb in OPT["split"][c][3]:
+                e0_, e1_ = a + 128 * x0, a + 128 * (x0 + nb)
+                fts.append("Ft%d_%d" % (c, x0))
+                tt(T.Ft[:, e0_:e1_], R[:].indirect(ap(lr, 8 * x0, 8 * (x0 + nb))), ap(nds, e0_, e1_), ALU.is_ge, Rr + [lr, nds], fts[-1:],
+                   128 * nb, gather=True)
+                x0 += nb
             cnt = ps[s1][:, 0:w]
-            pk = pick if rnd < 2 else pickb
-            terms(cnt, extra, w, True, False, s1)
-            mm(group(cnt, [(ap(pk, 15 - i, 143 - i), T.Ft[:, a + i:a + n:16]) for i in range(16)], w, False, True), ["Ft%d" % c, pk], s1)
+            pk = pickb if fuse else pick
+            terms(cnt, extra[:len(extra) - (rnd > 0)], w, True, False, s1)
+            if rnd:
+                terms(cnt, extra[-1:], w, False, False, s1)
+            mm(group(cnt, [(ap(pk, 15 - i, 143 - i), T.Ft[:, a + i:a + n:16]) for i in range(16)], w, False, True), fts + [pk], s1)
             if rnd < 2:
                 k = ap(fl, w, 2 * w)
-                lin(k, cnt, 1, -17 - rnd, (), [fl], w, banks=[s1], on="v", cut=True)
-                mm([(ps[s0][:, 192 + y * w:192 + (y + 1) * w], ap(diag(back)), k, False, y == 1, w) for y, back in enumerate((B - K5, H - KH))],
-                   [fl, diag(B - K5), diag(H - KH)], s0)
                 l1, fb, x = new("pu", 2 * w), new("pb", 2 * w), new("pf", w)
-                lin(ap(l1), lraw, 1, 192 * B, (), [l1], 2 * w, banks=[s0], on="V")
-                lists[c] = ((l1, 0), (l1, w))
+                if fuse:
+                    lb = new("pu", w)
+                    if OPT["fuse"] == 1:
+                        tt(ap(lb), cnt, ap(lf), ALU.max, [lf], [lb], w, 1.0, banks=[s1])
+                    else:
+                        li = new("pf", w)
+                        tt(ap(li), cnt, ap(lf), ALU.max, [lf], [li], w, 1.0, banks=[s1])
+                        lin(ap(lb), ap(li), 1, 0, [li], [lb], w)
+                    ts(k, cnt, 0.0, None, ALU.is_ge, None, (), [fl], w, banks=[s1])
+                    terms(ps[s0][:, 192 + w:192 + 2 * w], th_ * (s0 == s1) + [(diag(H - KH), fl, k)], w, s0 == s1, True, s0)
+                    lin(ap(l1, 0, w), ps[s0][:, 192 + w:192 + 2 * w], 1, 0, (), [l1], w, banks=[s0], on=OPT["lr"])
+                    lists[c] = ((lb, 0), (l1, 0))
+                else:
+                    lin(k, cnt, 1, -17 - rnd, (), [fl], w, banks=[s1], on="v", cut=True)
+                    mm([(ps[s0][:, 192 + y * w:192 + (y + 1) * w], ap(diag(back)), k, False, y == 1, w)
+                        for y, back in enumerate((B - K5, H - KH))], [fl, diag(B - K5), diag(H - KH)], s0)
+                    lin(ap(l1), lraw, 1, 0, (), [l1], 2 * w, banks=[s0], on="V")
+                    lists[c] = ((l1, 0), (l1, w))
                 tt(ap(x), dv, k, ALU.mult, [fl], [x], w, 1.0, banks=[s0])
                 y, ya = lref(2 * w)
                 lin(ap(fb), ap(fl).indirect(ya), 1, 0, [fl, fl[3] + "g", y], [fb], 2 * w, gather=True)

from concourse.bass import DstId, RemoteDMATransfer
from concourse.mybir import AluOpType as ALU, ActivationFunctionType as AF

N, B, H, D, O, CAP = 4, 2048, 1024, 1024, 1280, 256
K2, K3, K5 = 37, 611, 1237
MU = pow(K2, -1, H)
KT = K3 * MU % H
KH = (KT + K5) % H
W = O // 16
TRI = 88
RAW = D - 3 * TRI
PIECE = {"n": (0, 256), "w": (512, 128), "k": (768, 128), "x": (512, 256), "t": (1024, TRI)}
FW = 1024 + 2 * TRI
EPS, TINY = 2.0 ** -17, 2.0 ** -24
UNIT = 2.0 ** -12
GAP = 4096
ALPHA = 4095 / 256
MORE = 1280
OFF = 8192.0

SCRATCH = {
    "wts": ("sbuf", [128, B + 2 * MORE], "bfloat16"), "kds": ("sbuf", [128, B + 2 * MORE], "bfloat16"), "nzs": ("sbuf", [128, H], "bfloat16"),
    "nds": ("sbuf", [128, O], "bfloat16"), "N2": ("sbuf", [128, (N - 1) * GAP + H], "bfloat16"), "R": ("sbuf", [128, N * D], "bfloat16"),
    "F": ("sbuf", [128, N * FW], "float16"), "W2": ("sbuf", [128, 2 * B], "bfloat16"), "KK": ("sbuf", [128, 2 * B], "bfloat16"),
    "N1": ("sbuf", [128, B + 384], "bfloat16"), "Wg": ("sbuf", [128, O], "bfloat16"), "Kg": ("sbuf", [128, O], "float16"),
    "A": ("sbuf", [128, O], "float16"), "Z": ("sbuf", [128, O], "float32"), "Ft": ("sbuf", [128, O], "bfloat16"),
    "P1": ("sbuf", [128, B + 2 * MORE], "float32"), "P2": ("sbuf", [128, 2 * B], "float32"), "Pg": ("sbuf", [128, O], "float32"),
    "Z9": ("sbuf", [128, 720], "float32"), "Rl": ("sbuf", [128, 720], "float32"),
    "pi": ("sbuf", [128, 3072], "int32"), "pf": ("sbuf", [128, 4096], "float32"), "pb": ("sbuf", [128, 16384], "bfloat16"),
    "ph": ("sbuf", [128, 4096], "float16"), "pu": ("sbuf", [128, 3072], "uint16"),
}
for _b in range(8):
    SCRATCH["ps%d" % _b] = ("psum", [128, 512], "float32")
SEMAPHORES = (["cv", "ca", "cp", "cg", "sent"] + ["d%d" % i for i in range(24)]
              + ["%s%d_%d" % (a, h, r) for a in "rstnwkx" for h in range(2) for r in range(N)])

OPT = {
    "chunks": [(0, (3, 2), (0, 1), 2, 3, 3), (5, (3, 2), (4, 5), 6, 7, 7)],
    "pack": (3, 7, 2, 6), "spare": ((3, 7), (1, 5, 0, 4)),
    "pairs": [[0, 0], [0, 0], [0, 0]],
    "split": [[(3, 2), (3, 2), (3, 2), (5,)]] * 2, "cq": 1,
    "loads": ["ra", "nz", "tri", "wt", "kd", "rb", "nd", "wx", "kx"], "early": 2 * TRI,
    "sends": [("r", 2000, 2100), ("n", 2700, 3300), ("w", 2700, 4500), ("k", 2300, 4400), ("N", 2700, 0), ("t", 2600, 3100),
              ("s", 3400, 4700), ("RT", 2300, 0), ("S", 2200, 0)],
    "direct": "wk", "hand": "S", "fuse": 1, "lr": "V", "one": [[0, 0], [0, 0], [0, 0]], "build": (2, 6), "soon": 2,
    "times": [(0.83, 1.35, 0.42, 215.0, 1.0), (1.0, 1.6, 0.5, 205.0, 1.05), (1.2, 1.9, 0.6, 200.0, 1.15)],
    "tries": 2000, "seed": 2, "leads": (500.0, 1000.0, 1500.0, 2500.0), "short": 600, "slack": 0.007, "mirror": 3, "lean": 3000.0, "aim": 0.7, "slow": 0.24, "near": 0.02, "even": 1,
    "swaps": 1500, "cycles": 4, "more": {"tries": 1800, "swaps": 300, "slack": 0.008, "even": 0.5}, "stale": 600, "keep": 20, "gain": 0.003,
}
PLAN = {}


def make_order(ops, opt, begin=None):
    n = len(ops)
    pre, above = [], []
    for o in ops:
        up = 0
        for d in o["deps"]:
            up |= above[d]
        pre.append(sorted([d for d in o["deps"] if not up >> d & 1] + [d for d in o["after"] - o["deps"] if not up >> d & 1]))
        for d in o["deps"]:
            up |= 1 << d
        above.append(up)
    sets = []
    for cy, ga, pc, hop, xl in opt["times"]:
        cost = [[c[0] + cy * (c[1] + ga * c[2]) + pc * c[3] for _, _, c in o["alt"]] for o in ops]
        lat = [o["lat"] * (xl if o["alt"][0][0] is None else 1.0) for o in ops]
        fore = [[(d, lat[d] + hop if d in ops[i]["deps"] else 0.0) for d in pre[i]] for i in range(n)]
        back = [[] for _ in ops]
        for i in range(n):
            for d, x in fore[i]:
                back[d].append((i, x))
        sets.append((cost, lat, fore, back))
    engs = [[a[0] for a in o["alt"]] for o in ops]

    def replay(order, pick, s):
        cost, lat, fore, back = sets[s]
        end, free, last = [0.0] * n, {}, 0.0
        for i in order:
            e = engs[i][pick[i]]
            t = free.get(e, 0.0)
            for d, x in fore[i]:
                if end[d] + x > t:
                    t = end[d] + x
            t += cost[i][pick[i]]
            if e is not None:
                free[e] = t
            end[i] = t
            if t + lat[i] > last:
                last = t + lat[i]
        return last

    def loads(pick):
        x = {"a": 0.0, "v": 0.0}
        for e, c, k in zip(engs, sets[-1][0], pick):
            if e[k] in x:
                x[e[k]] += c[k]
        return x["a"], x["v"]

    def chain(order, pick, s):
        cost, lat, fore, back = sets[s]
        end, free, by = [0.0] * n, {}, [None] * n
        for i in order:
            e = engs[i][pick[i]]
            t, by[i] = free.get(e, (0.0, None))
            for d, x in fore[i]:
                if end[d] + x > t:
                    t, by[i] = end[d] + x, d
            end[i] = t + cost[i][pick[i]]
            if e is not None:
                free[e] = (end[i], i)
        i, pairs = max(range(n), key=lambda j: end[j] + lat[j]), []
        while by[i] is not None:
            if by[i] not in pre[i]:
                pairs.append((by[i], i))
            i = by[i]
        return pairs or [(0, 0)]

    def place(seq, pick, s, mirrored, lean):
        cost, lat, fore, back = sets[s]
        need = back if mirrored else fore
        start, end, busy, pick = [0.0] * n, [0.0] * n, {e: [] for e in "vapsg"}, list(pick)
        for i in seq:
            t0 = lat[i] if mirrored else 0.0
            for d, x in need[i]:
                if end[d] + x > t0:
                    t0 = end[d] + x
            best = None
            if not lean or lean[i] is None:
                e, c = engs[i][pick[i]], cost[i][pick[i]]
                if e is not None:
                    l = busy[e]
                    k = m = len(l)
                    while k > 0 and l[k - 1][1] > t0:
                        k -= 1
                    while k < m and l[k][0] < t0 + c:
                        if l[k][1] > t0:
                            t0 = l[k][1]
                        k += 1
                    l.insert(k, (t0, t0 + c))
                start[i], end[i] = t0, t0 + c
                continue
            for a in range(len(engs[i])):
                e, c, t, k = engs[i][a], cost[i][a], t0, 0
                if e is not None:
                    l = busy[e]
                    k = len(l)
                    while k > 0 and l[k - 1][1] > t:
                        k -= 1
                    while k < len(l) and l[k][0] < t + c:
                        if l[k][1] > t:
                            t = l[k][1]
                        k += 1
                y = t + c + (lean[i] if a and lean and lean[i] is not None else 0.0)
                if best is None or y < best[0]:
                    best = (y, a, e, t, c, k)
            y, a, e, t, c, k = best
            if e is not None:
                busy[e].insert(k, (t, t + c))
            pick[i], start[i], end[i] = a, t, t + c
        return start, end, pick

    def sort(key, mirrored):
        need, key = sets[0][3 if mirrored else 2], list(key)
        for i in (range(n - 1, -1, -1) if mirrored else range(n)):
            for d, x in need[i]:
                if key[d] >= key[i]:
                    key[i] = key[d] + 0.001
        return [i for _, i in sorted(zip(key, range(n)))]

    cost, lat, fore, back = sets[0]
    tail = [0.0] * n
    for i in range(n - 1, -1, -1):
        tail[i] = cost[i][0] + max([tail[j] + x for j, x in back[i]] + [lat[i]])
    PLAN["tail"] = tail
    seed, best, ref, cur = [opt["seed"]], None, None, None

    def rnd():
        seed[0] = (seed[0] * 1103515245 + 12345) % 2 ** 31
        return seed[0] / 2 ** 31

    ref, found = [1.2 * max(tail) * (1.0 + y * opt["slow"]) for y in range(len(sets))], [begin] if begin else []
    turns = [(x, k, opt["short"]) for x in opt["leads"] for k in range(opt["short"])] + [(None, k, opt["tries"]) for k in range(opt["tries"])]
    for lead, k, tries in turns:
        if k == 0:
            found += [best] if best else []
            best, cur, lean = None, None, None
            if lead is None:
                key, pick = [0.0] * n, min(found)[3]
                for x, i in enumerate(min(found)[1]):
                    key[i] = float(x)
            else:
                key, pick = [-tail[i] - lead * ops[i]["lead"] for i in range(n)], [o["first"] for o in ops]
        s = k % len(sets)
        start, end, pick = place(sort(key, False), pick, s, False, lean)
        for again in range(2):
            span = max(a + b for a, b in zip(end, sets[s][1]))
            if cur is None or span < best[2][s] * (1.0 + opt["near"]):
                order = [i for _, i in sorted(zip(start, range(n)))]
                ts_ = [span if y == s else replay(order, pick, y) for y in range(len(sets))]
                score = sum(a / b for a, b in zip(ts_, ref)) + opt["even"] * max(loads(pick)) / ref[-1]
                if best is None or score < best[0]:
                    best = (score, order, ts_, pick)
                if cur is None or score < cur[0] + opt["slack"] * (1.0 - k / tries) * rnd():
                    cur = (score, start, pick, order)
            if again or k % opt["mirror"]:
                break
            bs, be, _ = place(sort([-x for x in end], True), pick, s, True, None)
            start, end, pick = place(sort([-x for x in be], False), pick, s, False, None)
        size, span = 2500.0 * rnd() ** 3 + 50.0, 12000.0 * rnd() ** 2
        lo = rnd() * max(cur[1]) - span / 2
        shift, who, pick, lean = size * (2 * rnd() - 1), float(int(rnd() * len(opt["chunks"]))), cur[2], None
        if k % 3:
            key = [x + (size * rnd() if lo <= x <= lo + span else 0.0) for x in cur[1]]
        else:
            key = [x + (shift if lo <= x <= lo + span and o["lead"] == who else 0.0) for x, o in zip(cur[1], ops)]
        if k % 4 == 0:
            lean = [opt["lean"] * (rnd() - 0.1) if lo <= x <= lo + span and rnd() < 0.5 else None for x in cur[1]]
        if rnd() < opt["aim"]:
            if len(cur) == 4:
                cur = cur + ([chain(cur[3], cur[2], y) for y in range(len(sets))],)
            pairs = cur[4][(k + 1) % len(sets)]
            key, pick, lean = list(cur[1]), list(cur[2]), None
            for _ in range(1 + int(2.5 * rnd() ** 2)):
                a, b = pairs[int(rnd() * len(pairs))]
                y = rnd()
                if y < 0.3 and len(engs[a]) > 1:
                    pick[a] = 1 - pick[a]
                elif y > 0.7 and len(engs[b]) > 1:
                    pick[b] = 1 - pick[b]
                else:
                    key[a] = key[b] + 1.0

    best = min(found + [best])
    score, order, ts_, pick = best
    pick, tabu, ns, stale = list(pick), {}, range(len(sets)), 0
    for it in range(opt["swaps"]):
        mp, ms, lastq = [None] * n, [None] * n, {}
        for i in order:
            e = engs[i][pick[i]]
            if e is not None:
                j = lastq.get(e)
                if j is not None:
                    mp[i], ms[j] = j, i
                lastq[e] = i
        P, Hd, Tl, Jh, Jt, ts_ = [], [], [], [], [], []
        for s in ns:
            cost, lat, fore, back = sets[s]
            p = [c[k] for c, k in zip(cost, pick)]
            end, jh, tl, jt = [0.0] * n, [0.0] * n, [0.0] * n, [0.0] * n
            for i in order:
                t = 0.0
                for d, x in fore[i]:
                    if end[d] + x > t:
                        t = end[d] + x
                jh[i] = t
                j = mp[i]
                if j is not None and end[j] > t:
                    t = end[j]
                end[i] = t + p[i]
            for i in reversed(order):
                t = lat[i]
                for d, x in back[i]:
                    if tl[d] + x > t:
                        t = tl[d] + x
                jt[i] = t
                j = ms[i]
                if j is not None and tl[j] > t:
                    t = tl[j]
                tl[i] = t + p[i]
            P.append(p), Hd.append(end), Tl.append(tl), Jh.append(jh), Jt.append(jt), ts_.append(max(tl))
        ld = loads(pick)
        score = sum(a / b for a, b in zip(ts_, ref)) + opt["even"] * max(ld) / ref[-1]
        stale += 1
        if score < best[0]:
            best, stale = (score, order, ts_, list(pick)), 0
        if stale > opt["stale"]:
            order, pick, stale, tabu = best[1], list(best[3]), 0, {}
            continue
        moves = {}
        for s in ns:
            for b in range(n):
                if Hd[s][b] + Tl[s][b] - P[s][b] > ts_[s] - 0.01:
                    a = mp[b]
                    if a is not None and Hd[s][a] > Jh[s][b] + 0.01 and a not in pre[b]:
                        moves[(a, b)] = 1
                    if len(engs[b]) > 1:
                        moves[(b, None)] = 1
        where = {i: k for k, i in enumerate(order)}
        choice = None
        for a, b in moves:
            v = 0.0
            if b is None:
                e, k = engs[a][1 - pick[a]], where[a]
                x, y = k - 1, k + 1
                while x >= 0 and engs[order[x]][pick[order[x]]] != e:
                    x -= 1
                while y < n and engs[order[y]][pick[order[y]]] != e:
                    y += 1
            for s in ns:
                p, end, tl, jh, jt = P[s], Hd[s], Tl[s], Jh[s], Jt[s]
                if b is None:
                    t = (max(jh[a], end[order[x]] if x >= 0 else 0.0) + sets[s][0][a][1 - pick[a]]
                         + max(jt[a], tl[order[y]] if y < n else 0.0))
                    if mp[a] is not None and ms[a] is not None:
                        t = max(t, end[mp[a]] + tl[ms[a]])
                else:
                    eb = max(jh[b], end[mp[a]] if mp[a] is not None else 0.0) + p[b]
                    ta = max(jt[a], tl[ms[b]] if ms[b] is not None else 0.0) + p[a]
                    t = max(eb + max(jt[b], ta), max(jh[a], eb) + ta)
                if end[a] + tl[a] - p[a] < ts_[s] - 0.01:
                    t = max(t, ts_[s])
                v += max(t, ts_[s] * (1.0 - opt["gain"])) / ref[s]
            if b is None:
                c = sets[-1][0][a]
                v += opt["even"] * (max(ld[0] + c[0], ld[1] - c[1]) if pick[a] else max(ld[0] - c[0], ld[1] + c[1])) / ref[-1]
            else:
                v += opt["even"] * max(ld) / ref[-1]
            v += 1e-5 * rnd()
            if (tabu.get((a, b), -1) < it or v < best[0] - 0.002) and (choice is None or v < choice[0]):
                choice = (v, a, b)
        if choice is None:
            tabu = {}
            continue
        v, a, b = choice
        if b is None:
            pick[a] = 1 - pick[a]
            tabu[(a, None)] = it + 8 + int(opt["keep"] * rnd())
        else:
            key = list(range(n))
            for k, i in enumerate(order):
                key[i] = k
            key[a] = key[b] + 0.5
            for i in order[where[a] + 1:where[b]]:
                for d, x in sets[0][2][i]:
                    if key[d] > key[i]:
                        key[i] = key[d] + 0.0001
                if mp[i] is not None and key[mp[i]] > key[i]:
                    key[i] = key[mp[i]] + 0.0001
            order = [i for _, i in sorted(zip(key, range(n)))]
            tabu[(b, a)] = it + 8 + int(opt["keep"] * rnd())
    if opt["cycles"]:
        return make_order(ops, dict(opt, cycles=opt["cycles"] - 1, leads=(), seed=seed[0], **opt["more"]), best)
    return best[1], best[3], best[2]


def rank_program(g, core, T, topo):
    me = T.rank_of(core)
    if me is None:
        return
    cores = list(T.cores)
    mate = [r for r in range(N) if r != me and cores[r] in topo.cores_of(core)][0]
    far = [r for r in range(N) if r != me and r != mate]
    far.sort(key=lambda r: topo.die(cores[r]) != topo.die(core))
    queue = {"v": g.vector, "a": g.scalar, "p": g.tensor, "s": g.sync, "g": g}
    ops, lastw, readers, bank, lastp = [], {}, {}, {}, {}
    used = {"pi": 0, "pf": 0, "pb": 0, "ph": 0, "pu": 0}
    ndma, tok, lead = [0], [0], [0.0]
    PLAN["ops"] = ops
    CH = OPT["chunks"]

    def new(pool, n):
        a = used[pool]
        used[pool] = a + (n + 15) // 16 * 16
        tok[0] += 1
        assert used[pool] <= SCRATCH[pool][1][1], pool
        return (T[pool], a, n, "t%d" % tok[0])

    def ap(x, a=0, b=None, s=1):
        b = x[2] if b is None else b
        return x[0][:, x[1] + a:x[1] + b:s] if s != 1 else x[0][:, x[1] + a:x[1] + b]

    def op(eng, fn, rd=(), wr=(), banks=(), cost=(55.0, 0, 0, 0), lat=0.0, sem=None, after=(), alt=(), first=0):
        i = len(ops)
        deps = set()
        for t in rd:
            t = t if isinstance(t, str) else t[3]
            if t in lastw:
                deps.add(lastw[t])
            readers.setdefault(t, []).append(i)
        for t in wr:
            t = t if isinstance(t, str) else t[3]
            if t in lastw:
                deps.add(lastw[t])
            deps.update(readers.get(t, []))
            lastw[t] = i
            readers[t] = []
        for b in banks:
            e, cur, prev = bank.get(b, (None, [], []))
            if e != eng or alt:
                e, cur, prev = (i if alt else eng), [], cur
            deps.update(prev)
            bank[b] = (e, cur + [i], prev)
        deps.discard(i)
        ops.append({"alt": [(eng, fn, cost)] + list(alt), "deps": deps, "lat": lat, "sem": sem, "after": set(after), "lead": lead[0],
                    "first": first, "tag": (tuple(wr), tuple(banks))})
        return i

    def vc(n, c=1.0, f=0.0):
        return (f, max(64.0, n * c), 0, 0)

    def gc_(n, f=50.0):
        return (f, 0, n, 0)

    def ts(out, in0, s1, s2, o0, o1, rd, wr, n, c=1.0, banks=(), gather=False):
        if o1 is None:
            fn = lambda: g.vector.tensor_scalar(out, in0, s1, None, o0)
        else:
            fn = lambda: g.vector.tensor_scalar(out, in0, s1, s2, o0, o1)
        return op("v", fn, rd, wr, banks, gc_(n) if gather else vc(n, c))

    def tt(out, in0, in1, o, rd, wr, n, c=2.0, banks=(), gather=False):
        return op("v", lambda: g.vector.tensor_tensor(out, in0, in1, o), rd, wr, banks, gc_(n) if gather else vc(n, c))

    def fill(out, v, wr, n):
        return op("v", lambda: g.vector.memset(out, v), (), wr, cost=vc(n))

    def scan(out, d0, d1, o0, o1, rd, wr, n, c=1.0, banks=()):
        return op("v", lambda: g.vector.tensor_tensor_scan(out, d0, d1, 0.0, o0, o1), rd, wr, banks, vc(n, c))

    def act(out, in_, bias, rd, wr, n, func, banks=(), scale=1.0):
        return op("a", lambda: g.scalar.activation(out, in_, func, bias=bias, scale=scale), rd, wr, banks, vc(n, 1.0, 30.0))

    def lin(out, in_, mul, add, rd, wr, n, c=1.0, banks=(), gather=False, on="a", cut=False):
        mul, add = float(mul), float(add) if isinstance(add, (int, float)) else add
        a = ("a", lambda: g.scalar.activation(out, in_, AF.Relu if cut else AF.Identity, bias=add, scale=mul),
             gc_(n, 65.0) if gather else vc(n, 1.0, 30.0))
        v = ("v", lambda: (g.vector.tensor_scalar(out, in_, add, 0.0, ALU.add, ALU.max) if cut else
                           g.vector.tensor_scalar(out, in_, mul, add, ALU.mult, ALU.add)), gc_(n) if gather else vc(n, c))
        if on in "AV":
            x = a if on == "A" else v
            return op(x[0], x[1], rd, wr, banks, x[2])
        return op(a[0], a[1], rd, wr, banks, a[2], alt=[v], first=int(on == "v"))

    def mm(terms, rd, b):
        def fn():
            for (o_, l_, r_, st, sp, n) in terms:
                last = g.tensor.matmul(o_, l_, r_, st, sp)
            return last
        i = op("p", fn, rd, (), [b], (30.0, 0, 0, sum(max(64, t[5]) for t in terms)), after=[lastp[b]] if b in lastp else [])
        lastp[b] = i
        return i

    def group(out, pairs, n, start=True, stop=True):
        return [(out, l_, r_, start and i == 0, stop and i == len(pairs) - 1, n) for i, (l_, r_) in enumerate(pairs)]

    def terms(out, tm, n, start, stop, b):
        mm(group(out, [(ap(m), x) for m, _, x in tm], n, start, stop), [y for m, t, _ in tm for y in (m, t)], b)

    def dma(eng, out, in_, rd, wr, lat, after=()):
        s = "d%d" % ndma[0]
        ndma[0] += 1
        return op(eng, lambda: queue[eng].dma_start(out, in_), rd, wr, (), (60.0, 0, 0, 0), lat, (s, 16), after)

    ps = [T["ps%d" % b] for b in range(8)]
    R, F = T.R, T.F
    rt, RA = me * D + RAW, OPT["early"]

    beg, sal = new("pi", W), new("pi", W)
    wts, kds = (T.wts, 0, B + 2 * MORE, "wts"), (T.kds, 0, B + 2 * MORE, "kds")
    nzs, nds = (T.nzs, 0, H, "nzs"), (T.nds, 0, O, "nds")
    loads = {"tri": (R[:, rt:rt + 3 * TRI], T.room[:, RAW:D], ["Rt%d" % me], 3 * TRI),
             "ra": (R[:, me * D:me * D + RA], T.room[:, 0:RA], ["r0_%d" % me, "r1_%d" % me], RA),
             "rb": (R[:, me * D + RA:rt], T.room[:, RA:RAW], ["s0_%d" % me, "s1_%d" % me], RAW - RA),
             "nz": (ap(nzs), T.noise[:], [nzs], H), "wt": (ap(wts, 0, B), T.wt[:], [wts], B), "kd": (ap(kds, 0, B), T.kid[:], [kds], B),
             "nd": (ap(nds), T.need[:], [nds], O), "wx": (ap(wts, B, B + MORE), T.wt[:, 0:MORE], ["wx"], MORE),
             "kx": (ap(kds, B, B + MORE), T.kid[:, 0:MORE], ["kx"], MORE)}
    dma("a", ap(beg), T.begin[:], (), [beg], 2100)
    dma("a", ap(sal), T.salt[:], (), [sal], 2200)
    due, prev = 2100.0, []
    for name in OPT["loads"]:
        if name in ("wx", "kx") and OPT["one"][1][0]:
            continue
        o_, i_, wr, n = loads[name]
        due += 0.69 * n - 60
        prev = [dma("s", o_, i_, (), wr, due, prev)]

    col, prt, mui, pu_ = new("pi", 144), new("pi", 8), new("pi", 64), new("pi", 72)
    op("g", lambda: g.iota(ap(mui), [[16 * K2, 64]], 0, K2), (), [mui], cost=(250.0, 0, 0, 0))
    op("g", lambda: g.iota(ap(prt), [[0, 8]], 0, 1), (), [prt], cost=(150.0, 0, 0, 0))
    op("g", lambda: g.iota(ap(col), [[1, 144]], 0, 0), (), [col], cost=(400.0, 0, 0, 0))
    paired = any(any(x) for x in OPT["pairs"])
    if paired:
        op("g", lambda: g.iota(ap(pu_), [[-16, 8], [-2, 9]], 0, 1), (), [pu_], cost=(270.0, 0, 0, 0))
    mum, lmu = new("pi", 64), new("pu", 64)
    ts(ap(mum), ap(mui), H - 1, None, ALU.bitwise_and, None, [mui], [mum], 64)
    lin(ap(lmu), ap(mum), 1, 0, [mum], [lmu], 64)
    pcol, gcol, gneg = new("pf", 1), new("pf", 1), new("pf", 1)
    plo, phi = new("pi", 8), new("pi", 8)
    lin(ap(pcol), ap(prt, 0, 1), 1, 0, [prt], [pcol], 1)
    ts(ap(plo), ap(prt), 15, None, ALU.bitwise_and, None, [prt], [plo], 8)
    ts(ap(phi), ap(prt), 4, None, ALU.logical_shift_right, None, [prt], [phi], 8)
    lin(ap(gcol), ap(phi, 0, 1), 16, 15, [phi], [gcol], 1)
    lin(ap(gneg), ap(phi, 0, 1), -16, H, [phi], [gneg], 1)
    wide1 = new("pb", 240)
    ts(ap(wide1, 0, 128), ap(col, 0, 128), ap(pcol), None, ALU.is_equal, None, [col, pcol], [wide1], 128)
    lin(ap(wide1, 128, 240), ap(wide1, 0, 112), 1, 0, [wide1], ["wide1b"], 112, 0.5, on="v")
    consts = {(1, 128): wide1[:2] + (128, wide1[3])}

    def diag(v, wide=128):
        if (v, wide) not in consts:
            m = abs(v) * 2 ** 20
            while m % 2 == 0:
                m //= 2
            x = new("pb" if m < 256 else "ph", wide)
            lin(ap(x), ap(wide1, 0, wide), v, 0, [wide1, "wide1b"][:1 + (wide > 128)], [x], wide, 0.5)
            consts[(v, wide)] = x
        return consts[(v, wide)]

    pick, pickb = new("pb", 144), new("pb", 144)
    ts(ap(pick), ap(col), ap(gcol), None, ALU.is_equal, None, [col, gcol], [pick], 144)
    lin(ap(pickb), ap(pick), OFF, 0, [pick], [pickb], 144, 0.5)
    i8, t1, t2, rx, rb = new("pi", 1), new("pi", 1), new("pi", 1), new("pi", 8), new("pf", 1)
    ts(ap(i8), ap(prt, 0, 1), 8, None, ALU.bitwise_and, None, [prt], [i8], 1)
    ts(ap(t1), ap(phi, 0, 1), ap(pcol), 128.0, ALU.subtract, ALU.add, [phi, pcol], [t1], 1)
    ts(ap(t2), ap(t1), 7, None, ALU.bitwise_and, None, [t1], [t2], 1)
    tt(ap(rb), ap(t2), ap(i8), ALU.add, [t2, i8], [rb], 1)
    lin(ap(rx), ap(col, 0, 8), 16, ap(rb), [col, rb], [rx], 8)
    mirror = {}

    def lref(w, mul=1, add=0, twice=False):
        if (w, mul, twice) not in mirror:
            a, b, c = new("pi", 8), new("pu", 8), new("pi", 8)
            if twice:
                ts(ap(c), ap(rx), float(w), float(w), ALU.is_ge, ALU.mult, [rx], [c], 8)
                tt(ap(a), ap(rx), ap(c), ALU.subtract, [rx, c], [a], 8)
            elif mul == 1:
                ts(ap(b), ap(rx), float(w - 1), None, ALU.min, None, [rx], [b], 8)
            else:
                ts(ap(a), ap(rx), float(w - 1), None, ALU.min, None, [rx], [a], 8)
            if mul != 1:
                lin(ap(b), ap(a), mul, add, [a], [b], 8)
            mirror[(w, mul, twice)] = b
        x = mirror[(w, mul, twice)]
        return x, ap(x, 0, ((1 + twice) * w + 15) // 16)

    pat, c1536 = new("pb", 512), new("ph", 128)
    if not all(all(x) for x in OPT["pairs"]):
        nmax = 128 * max(max(c[1]) for c in CH)
        fill(ap(pat, 0, nmax), 0.0, [pat], nmax // 2)
        fill(ap(pat, 0, nmax, 16), -2.0 ** 13, [pat], 32)
    fill(ap(c1536), 1536.0, [c1536], 64)
    bon = [new("pf", 1), new("pf", 1)]
    for x, step, v in zip(bon, (256.0, 128.0), (-2047.0, -160.0)):
        lin(ap(x), ap(plo, 0, 1), -step, 15 * step + v, [plo], [x], 1)
    blk, tri, nblk, ntri, ta, tb, gmid = [new("pb", 128) for _ in range(6)] + [new("pf", 1)]
    lin(ap(gmid), ap(phi, 0, 1), -16, -7.5, [phi], [gmid], 1)
    act(ap(ta), ap(col, 0, 128), ap(gmid), [col, gmid], [ta], 128, AF.Abs)
    ts(ap(blk), ap(ta), 8.0, None, ALU.is_lt, None, [ta], [blk], 128, 0.5)
    op("g", lambda: g.affine_select(ap(tb), ap(blk), [[-1, 128]], ALU.is_gt, 0.0, 0, 1), [blk], [tb], cost=(170.0, 256, 0, 0))
    op("g", lambda: g.affine_select(ap(ntri), ap(tb), [[-1, 128]], ALU.not_equal, 512.0, 0, 1), [tb], [ntri], cost=(170.0, 256, 0, 0))
    lin(ap(nblk), ap(blk), -1, 0, [blk], [nblk], 128, 0.5)
    lin(ap(tri), ap(ntri), -1, 0, [ntri], [tri], 128, 0.5)
    sgn, run, rst = [], [], {}

    def steps(out, v, first, n, name):
        op("g", lambda: g.iota(out, [[v, n]], v * first, 0, allow_small_or_imprecise_dtypes=True), (), [name], cost=(130.0, 2 * n, 0, 0))
    for c, ch in enumerate(CH):
        u = 8 * sum(ch[1]) + 1
        a, b = new("pb", (N + 1) * u), new("pb", (N + 1) * u)
        if u not in rst:
            rst[u] = new("pb", N * u)
            fill(ap(rst[u]), 1.0, [rst[u]], N * u // 2)
            fill(ap(rst[u], 0, N * u, u), 0.0, [rst[u]], 4)
        if c == 0:
            fill(ap(a, 0, N * u, u), 0.0, ["carry0"], 4)
        fill(ap(a, 1 - c, u), 1.0, ["sgn0_%d" % c], 40)
        fill(ap(a, N * u, (N + 1) * u), -1.0, ["sgn%d_%d" % (N, c)], 40)
        steps(ap(b, 0, u), 1, 8 * ch[0], u, "run0_%d" % c)
        steps(ap(b, N * u, (N + 1) * u), -1, 8 * ch[0], u, "run%d_%d" % (N, c))
        sgn.append(a)
        run.append(b)
    if paired:
        e0, e1, em, MK, MW, MA = new("pb", 72), new("pb", 72), new("pb", 72), new("pb", 144), new("pb", 144), new("pb", 144)
        for x, v in ((e0, 0.0), (e1, 1.0), (em, -2.0)):
            ts(ap(x), ap(pu_), v, None, ALU.is_equal, None, [pu_], [x], 72)
        fill(ap(e0, 8, 72, 9), 0.0, [e0], 8)
        fill(ap(e1, 8, 72, 9), 0.0, [e1], 8)
        tt(ap(MK, 0, 72), ap(e1), ap(e0), ALU.subtract, [e0, e1], ["MKa"], 72)
        tt(ap(MK, 72, 144), ap(em), ap(e0), ALU.subtract, [e0, em], [MK], 72)
        fill(ap(MK, 72, 144, 9), 0.0, [MK], 8)
        lin(ap(MW), ap(MK), 131072, 0, [MK, "MKa"], [MW], 144, 0.5)
        lin(ap(MA), ap(MK), 4096, 0, [MK, "MKa"], [MA], 144, 0.5)
        if any(any(x) for x in OPT["one"]):
            MP, MB = new("pf", 144), new("pb", 144)
            lin(ap(MP), ap(MK), 131072 / TINY, 0, [MK, "MKa"], [MP], 144)
            lin(ap(MP, 72, 144, 9), ap(e0, 0, 72, 9), -2.0 ** 56, 0, [e0], [MP], 8)
            lin(ap(MB), ap(MK), 4096 / TINY, 0, [MK, "MKa"], [MB], 144, 0.5)
        lin(ap(MK, 72, 144, 9), ap(e0, 0, 72, 9), -32768, 0, [e0], [MK], 8)

    s1_, sm_, hb, hbm = new("pi", W), new("pi", W), new("pi", W), new("pi", W)
    lb0, lh0, salB = new("pu", W), new("pu", W), new("ph", W)
    lin(ap(lb0), ap(beg), 1, 0, [beg], [lb0], W)
    lin(ap(s1_), ap(sal), MU, ap(gneg), [sal, gneg], [s1_], W)
    ts(ap(sm_), ap(s1_), H - 1, None, ALU.bitwise_and, None, [s1_], [sm_], W)
    tt(ap(hb), ap(sm_), ap(beg), ALU.add, [sm_, beg], [hb], W)
    ts(ap(hbm), ap(hb), H - 1, None, ALU.bitwise_and, None, [hb], [hbm], W)
    lin(ap(lh0), ap(hbm), 1, 0, [hbm], [lh0], W)
    x, xa = lref(W)
    lin(ap(salB), ap(sm_).indirect(xa), 1, 0, [sm_, x], [salB], W, gather=True)
    bsh = [new("ph", W), new("ph", W)]
    lin(ap(bsh[0]), ap(beg), 1, 0, [beg], [bsh[0]], W)
    lin(ap(bsh[1]), ap(hbm), 1, 0, [hbm], [bsh[1]], W)
    lists = [((lb0, 8 * ch[0]), (lh0, 8 * ch[0])) for ch in CH]

    def noise(r, a, b):
        return T.N2[:, (N - 1 - r) * GAP + a:(N - 1 - r) * GAP + b]

    def ntok(r, parts=("h0", "h1", "l0", "l1")):
        return ["N%s_%d" % (x, r) for x in parts]
    for a, parts in ((0, ("h0", "l0")), (512, ("h1", "l1"))):
        lin(noise(me, a, a + 512), ap(nzs).indirect(ap(lmu, a // 16, a // 16 + 32)), 1, -32, [nzs, lmu], ntok(me, parts), 512, gather=True)

    def word(kind, h, r, a=0, b=None):
        at, n = PIECE[kind]
        at += r * FW + h * n
        return F[:, at + a:at + (n if b is None else b)]

    def kids(r):
        return [r + N * j for j in range(16 // N)]
    I = diag(1)
    pn, pw, pt, pk_ = OPT["pack"]
    rch, big = new("pb", TRI), new("pb", B // N)
    lin(ap(rch), R[:, rt + 2 * TRI:rt + 3 * TRI], 1 / 16, 160 - 7.5 / 16, ["Rt%d" % me], [rch], TRI, 0.5, on="v")
    d16, dm16, d64, dm64, d4096, dm1 = diag(16), diag(-16), diag(64), diag(-64), diag(4096), diag(-1)
    mm(group(ps[pt][:, 0:TRI], [(ap(d16), R[:, rt:rt + TRI]), (ap(I), ap(rch))], TRI)
       + group(ps[pt][:, TRI:2 * TRI], [(ap(d16), R[:, rt + TRI:rt + 2 * TRI]), (ap(I), R[:, rt + 2 * TRI:rt + 3 * TRI]),
                                        (ap(dm16), ap(rch))], TRI), ["Rt%d" % me, rch, d16, dm16, I], pt)
    for h, v in enumerate((-2208, 512)):
        lin(word("t", h, me), ps[pt][:, h * TRI:(h + 1) * TRI], 1, v, (), ["t%d_%d" % (h, me)], TRI, banks=[pt], on="V")
    for h, b in enumerate((pn, pk_)):
        terms(ps[b][:, 0:256], [(d64, "Nh%d_%d" % (h, me), noise(me, 512 * h, 512 * h + 256)),
                                (I, "Nl%d_%d" % (h, me), noise(me, 512 * h + 256, 512 * h + 512))], 256, True, True, b)
        lin(word("n", h, me, 0, 256), ps[b][:, 0:256], 1, 32, (), ["n%d_%d" % (h, me)], 256, banks=[b])
    ONE = OPT["one"]
    lin(ap(big), ap(kds, me, B, N), 1 / 64, 192 - 63.5 / 128, [kds], [big], B // N, 0.5, on="v")
    if ONE[0][1]:
        for h, b in enumerate((pw, pk_)):
            js = [(j, kids(me)[2 * h + j], ps[b][:, 128 * j:128 * (j + 1)]) for j in range(2)]
            mm([(o_, ap(d64), ap(wts, c, B, 16), j == 0, False, 128) for j, c, o_ in js], [wts, d64], b)
            mm([(o_, ap(dm1), ap(kds, c, B, 16), False, False, 128) for j, c, o_ in js], [kds, dm1], b)
            mm([(o_, ap(d64), ap(big, 2 * h + j, B // N, N), False, j == 1, 128) for j, c, o_ in js], [big, d64], b)
            lin(word("x", h, me), ps[b][:, 0:256], 1, 63 - 2048, (), ["x%d_%d" % (h, me)], 256, banks=[b], on="va"[h])
    else:
        mm([(ps[pw][:, 128 * (j % 2):128 * (j % 2 + 1)], ap(I if j > 1 else d64), ap(wts, c, B, 16), j == 0, j == 3, 128)
            for j, c in enumerate(kids(me))], [wts, d64, I], pw)
        at = me * FW + PIECE["w"][0]
        lin(F[:, at:at + 256], ps[pw][:, 0:256], 1, -2048, (), ["w0_%d" % me, "w1_%d" % me], 256, banks=[pw], on="v")
        mm([(ps[pk_][:, 128 * (j % 2):128 * (j % 2 + 1)], ap(dm1 if j > 1 else dm64), ap(kds, c, B, 16), j == 0, False, 128)
            for j, c in enumerate(kids(me))], [kds, dm64, dm1], pk_)
        mm([(ps[pk_][:, 128 * (j % 2):128 * (j % 2 + 1)], ap(d64 if j > 1 else d4096), ap(big, j, B // N, N), False, j == 3, 128)
            for j in range(N)], [big, d64, d4096], pk_)
        at = me * FW + PIECE["k"][0]
        lin(F[:, at:at + 256], ps[pk_][:, 0:256], 1, 2047 - 192 * 4160, (), ["k0_%d" % me, "k1_%d" % me], 256, banks=[pk_], on="v")
    bone = [new("pf", 1), new("pf", 1)]
    if any(x[0] for x in ONE):
        lin(ap(bone[0]), ap(bon[0]), EPS * TINY, 0, [bon[0]], [bone[0]], 1)
        for j in range(4):
            b = OPT["build"][j % len(OPT["build"])]
            terms(ps[b][:], [(I, wts, ap(wts, 512 * j, 512 * j + 512)), (diag(EPS), kds, ap(kds, 512 * j, 512 * j + 512))], 512, True, True, b)
            lin(T.P1[:, 512 * j:512 * j + 512], ps[b][:], TINY, ap(bone[0]), [bone[0]], ["P1_%d" % j], 512, banks=[b])
    if ONE[0][1]:
        ones = new("pb", 256)
        fill(ap(ones), 1.0, [ones], 128)
        lin(ap(bone[1]), ap(bon[1]), EPS * TINY, (160 + 12288) * EPS * TINY, [bon[1]], [bone[1]], 1)
    if any(any(x) for x in ONE):
        dP = new("pf", 128)
        lin(ap(dP), ap(I), 131072 / TINY, 0, [I], [dP], 128)

    out_e = topo.engines(core, cores[far[0]])
    all_e = topo.engines(core, cores[mate])
    in_e = [e for e in all_e if e not in out_e]
    sent, gorder = [0], []

    def piece(kind, h, r):
        if kind in "rs":
            a, n = (0, RA // 2) if kind == "r" else (RA, (RAW - RA) // 2)
            return R[:, r * D + a + h * n:r * D + a + (h + 1) * n]
        return word(kind, h, r) if h < 2 else word(kind, 0, r, 0, 2 * PIECE[kind][1])

    def send(items, rd):
        def fn():
            tr = []
            for kind, h, r, to, es in items:
                rid, pid = topo.addr(cores[to], core)
                tr.append(RemoteDMATransfer(dst_ids=[DstId(rid=rid, pnc=pid)], dma_engine_mask=sum(1 << e for e in es),
                                            remote_sem=T.sem["%s%d_%d" % (kind, h % 2, r)], src=piece(kind, h, r), dst=piece(kind, h, r)))
            g.remote_dma_fused(tr, local_sem=T.sem.sent)
            return None
        sent[0] += sum(len(it[4]) for it in items)
        i = op("g", fn, rd, (), cost=(400.0 if gorder else 1900.0, 0, 0, 0), sem="none", after=gorder[-1:])
        gorder.append(i)
        return i

    def arrive(kind, h, r, n, after, lat, on=None):
        return op(None, None, (), ["%s%d_%d" % (kind, h, r)], cost=(0.0, 0, 0, 0), lat=lat,
                  sem=("%s%d_%d" % (kind, h if on is None else on, r), n), after=[after])

    def part(es, k, n):
        return es[k * len(es) // n:(k + 1) * len(es) // n]
    landed = []
    for kind, near, away in OPT["sends"]:
        if kind.islower():
            rd = ["%s%d_%d" % (kind, h, me) for h in range(2)]
            if kind in OPT["direct"]:
                i = send([(kind, 2, me, far[f], part(out_e, f, 2)) for f in range(2)] + [(kind, 2, me, mate, in_e)], rd)
                for h in range(2):
                    arrive(kind, h, mate, len(in_e), i, near, 0)
                for h in range(2):
                    for f in far:
                        arrive(kind, h, f, len(out_e) // 2, i, away, 0)
                landed += [(kind, (0, 1), r) for r in [mate] + far]
                continue
            outs = [(h, h) for h in range(2)]
            i = send([(kind, h, me, far[f], part(out_e, n_, len(outs))) for n_, (h, f) in enumerate(outs)]
                     + [(kind, h, me, mate, part(in_e, h, 2)) for h in range(2)], rd)
            for h in range(2):
                arrive(kind, h, mate, len(in_e) // 2, i, near)
            for h, f in outs:
                arrive(kind, h, far[f], len(out_e) // len(outs), i, away)
            landed += [(kind, (0, 1), mate)] + [(kind, (h,), far[h]) for h in range(2)]
        else:
            es = all_e if kind in OPT["hand"] else in_e
            its = [(x, h) for x in kind.lower() for h in range(2)]
            i = send([(x, h, far[h], mate, part(es, n_, len(its))) for n_, (x, h) in enumerate(its)],
                     ["%s%d_%d" % (x, h, far[h]) for x, h in its])
            for x, h in its:
                arrive(x, h, far[1 - h], len(es) // len(its), i, near)
            landed += [(x, (h,), far[1 - h]) for x, h in its]
    for h, n in enumerate((H, H, 384)):
        dma("s", T.N1[:, h * H:h * H + n], noise(me, 0, n), ntok(me) + ["n0_%d" % far[1]], ["N1_%d" % h], 2700 + 700 * h)
    if ONE[1][0]:
        dma("s", T.P1[:, B:B + MORE], T.P1[:, 0:MORE], ["P1_0", "P1_1", "P1_2", "n0_%d" % far[1]], ["P1_4"], 6000)
    if ONE[2][0]:
        dma("s", T.P1[:, B + MORE:B + 2 * MORE], T.P1[:, MORE:2 * MORE], ["P1_2", "P1_3", "P1_4"], ["P1_5"], 4000)
    else:
        for x, y, z in ((wts, "wx", "wy"), (kds, "kx", "ky")):
            dma("s", ap(x, B + MORE, B + 2 * MORE), ap(x, MORE, 2 * MORE), [x, y, "N1_2"], [z], 4000)

    turnb = [0]

    def spare(late):
        turnb[0] += 1
        x = OPT["spare"][late]
        return x[turnb[0] % len(x)]

    def block(tab, c):
        return tab[:, 256 * (15 - c):256 * (15 - c) + 128]

    def unpack(kind, hs, r):
        if kind in "rst":
            return
        ks, tab = kids(r), T.W2 if kind == "w" else T.KK
        if kind == "x":
            for h in hs:
                b, hi, src = spare(r != me), new("pb", 256), "x%d_%d" % (h, r)
                lin(ap(hi), word("x", h, r), 1 / 64, 192 - 31.5 / 64, [src], [hi], 256, 0.5, on="v")
                terms(ps[b][:, 0:256], [(diag(-160), ones, ap(ones))], 256, True, False, b)
                terms(ps[b][:, 0:256], [(diag(2047 / 2048), hi, ap(hi)), (diag(EPS), src, word("x", h, r))], 256, False, True, b)
                for j in range(2):
                    lin(block(T.P2, ks[2 * h + j]), ps[b][:, 128 * j:128 * (j + 1)], TINY, ap(bone[1]), [bone[1]],
                        ["Q%d_%d" % (2 * h + j, r)], 128, banks=[b], on="AV"[(h + r - me) % 2])
            return
        if kind == "w" and r == me:
            for j, c in enumerate(ks):
                lin(block(tab, c), ap(wts, c, B, 16), 1, 160, [wts], ["W%d_%d" % (j, r)], 128, 0.5)
            return
        for h in hs:
            b, n, src = spare(r != me and not (kind == "n" and r in (mate, far[h]))), 256 if kind == "n" else 128, "%s%d_%d" % (kind, h, r)
            if kind == "n":
                name = new("pb", n)
                hi = ap(name)
            else:
                hi, name = block(tab, ks[h]), "%s%d_%d" % (kind.upper(), h, r)
            lin(hi, word(kind, h, r, 0, n), 1 / 64, 192 - 31.5 / 64, [src], [name], n, 0.5, on="v")
            mm(group(ps[b][:, 0:n], [(ap(I), word(kind, h, r, 0, n)), (ap(dm64), hi)], n), [I, dm64, src, name], b)
            if kind == "n":
                lin(noise(r, 512 * h, 512 * h + n), hi, 1, -192, [name], ["Nh%d_%d" % (h, r)], n, 0.5, on="v")
                lin(noise(r, 512 * h + n, 512 * h + 2 * n), ps[b][:, 0:n], 1, 12256, (), ["Nl%d_%d" % (h, r)], n, banks=[b])
            else:
                lin(block(tab, ks[h + 2]), ps[b][:, 0:n], 1, 12448, (), ["%s%d_%d" % (kind.upper(), h + 2, r)], n, banks=[b])

    def unpack_rooms(r):
        b, hh = spare(0), new("ph", 2 * TRI)
        x = [word("t", h, r) for h in range(2)]
        for h in range(2):
            lin(ap(hh, h * TRI, (h + 1) * TRI), x[h], 1 / 16, 1408 - 7.5 / 16, ["t%d_%d" % (h, r)], [hh[3] + str(h)], TRI, 0.5, on="v")
        dm256 = diag(-256)
        mm(group(ps[b][:, 0:2 * TRI], [(ap(I), ap(hh))], 2 * TRI)
           + group(ps[b][:, 2 * TRI:3 * TRI], [(ap(d16), x[0]), (ap(dm256), ap(hh, 0, TRI)), (ap(I), x[1]),
                                               (ap(dm16), ap(hh, TRI, 2 * TRI))], TRI),
           [hh[3] + "0", hh[3] + "1", "t0_%d" % r, "t1_%d" % r, I, d16, dm256, dm16], b)
        a = r * D + RAW
        lin(R[:, a:a + 2 * TRI], ps[b][:, 0:2 * TRI], 1, -1280, (), ["Rt%d" % r], 2 * TRI, banks=[b])
        lin(R[:, a + 2 * TRI:a + 3 * TRI], ps[b][:, 2 * TRI:3 * TRI], 1, 17 * 22528, (), ["Ru%d" % r], TRI, banks=[b])

    rotm, rotc = diag(-16 / UNIT, 240), diag(2047, 240)

    def draw(c, second, pair, lb, lh, wtab, ktab, ntab, rw, rk, rn):
        b0, subs, kb = CH[c][:3]
        lead[0] = float(len(CH) - 1 - c)
        w = 8 * sum(subs)
        wp = (w + 15) // 16 * 16
        ends = [sum(subs[:u]) for u in range(len(subs) + 1)]
        cuts = [[(sum(x[:u]), sum(x[:u + 1])) for u in range(len(x))] for x in OPT["split"][c]]

        def blocks(nm, x0, x1):
            return ["%s_%d" % (nm, b0 + m) for m in range(x0, x1)]
        one = ktab is None
        wbuf, wnm = (T.Pg, "Pg") if one else (T.Wg, "Wg")
        for buf, nm, tab, rd_, k in ((wbuf, wnm, wtab, rw, 0), (T.Kg, "Kg", ktab, rk, 1))[:2 - one]:
            for x0, x1 in cuts[k]:
                lin(buf[:, 128 * (b0 + x0):128 * (b0 + x1)], tab.indirect(ap(lb[0], lb[1] + 8 * x0, lb[1] + 8 * x1)), 1,
                    ap(bon[second]) if k else -160 * (second and not one), rd_ + [lb[0]] + ([bon[second]] if k else []),
                    blocks(nm, x0, x1), 128 * (x1 - x0), gather=True)
        for x0, x1 in cuts[2]:
            a, e = 128 * (b0 + x0), 128 * (b0 + x1)
            tt(T.A[:, a:e], ntab.indirect(ap(lh[0], lh[1] + 8 * x0, lh[1] + 8 * x1)), wbuf[:, a:e], ALU.mult,
               rn + [lh[0]] + blocks(wnm, x0, x1), blocks("A", x0, x1), e - a, gather=True)
        for u, nb in enumerate(subs):
            a, bk, tk = b0 + ends[u], kb[u], "_%d_%d" % (c, u)
            if one:
                parts = [(T.Pg, "Pg", MP if pair else dP, [m], 4) for m in range(nb)] + [(T.A, "A", MB if pair else diag(4096 / TINY), range(nb), 1)]
            else:
                parts = [(T.Wg, "Wg", diag(32), range(nb), 1), (T.Kg, "Kg", diag(UNIT), range(nb), 1), (T.A, "A", I, range(nb), 1)]
            for n_, (buf, nm, mat, ms, dear) in enumerate(parts):
                tm = [(ps[bk][:, 256 * y + 72 * m:256 * y + 72 * (m + 1)] if pair else ps[bk][:, 128 * m:128 * (m + 1)],
                       buf[:, 128 * (a + m):128 * (a + m + 1)], ap(mat, 72 * y, 72 * y + 72) if pair else ap(mat), (72 if pair else 128) * dear)
                      for m in ms for y in range(1 + pair)]
                mm([(o_, l_, r_, n_ == 0 and i == 0, nm == "A" and i == len(tm) - 1, n) for i, (o_, l_, r_, n) in enumerate(tm)],
                   blocks(nm, ends[u] + ms[0], ends[u] + ms[-1] + 1) + [mat] + ["MKa"] * pair, bk)
            if pair:
                n = 72 * nb
                act(T.Rl[:, 72 * a:72 * a + n], ps[bk][:, 0:n], 0.0, (), ["Rl" + tk], n, AF.Relu, banks=[bk])
                scan(T.Z9[:, 72 * a:72 * a + n], ps[bk][:, 256:256 + n], T.Rl[:, 72 * a:72 * a + n], ALU.add, ALU.max, ["Rl" + tk],
                     ["Z9" + tk], n, banks=[bk])
            else:
                n = 128 * nb
                scan(T.Z[:, 128 * a:128 * a + n], ap(pat, 0, n), ps[bk][:, 0:n], ALU.add, ALU.max, [pat], ["Z" + tk], n, banks=[bk])
        zs = ["%s_%d_%d" % ("Z9" if pair else "Z", c, u) for u in range(len(subs))]
        win = T.Z9[:, 72 * b0:72 * (b0 + ends[-1])] if pair else T.Z[:, 128 * b0:128 * (b0 + ends[-1])]
        x, xa = lref(w, 9, 8) if pair else lref(w, 16, 15)
        hn, low, cq = new("pi", wp), new("ph", wp), new("ph", wp)
        lin(ap(hn), win.indirect(xa), 1, 0, zs + [x], [hn], wp, gather=True)
        tt(ap(low), win.indirect(xa), ap(hn), ALU.subtract, zs + [x, hn], [low], wp, gather=True)
        if second:
            lin(ap(cq), ap(low), 1 / 128 / UNIT, 1536, [low], [cq], wp, 0.5)
        return low, cq

    def turn(b, at, w, mat, x, stop, start=False):
        return [(ps[b][:, at + (-r) % 8:at + w:8], ap(mat, 16 * r, 16 * r + 128), ap(x, r, w, 8), start and r == 0, stop and r == 7, w // 8)
                for r in range(8)]

    def modulo(tm, b, at, n, m):
        z = new("pb", n)
        terms(ps[b][:, at:at + n], tm, n, True, True, b)
        lin(ap(z), ps[b][:, at:at + n], 1 / m, 191.5 + 1 / 4096, (), [z], n, banks=[b])
        return tm + [(diag(-m), z, ap(z)), (diag(m / 8), c1536, ap(c1536, 0, n))]

    st = [{"fl": [], "fb": []} for _ in CH]
    W2r, KKr = [["%s%d_%d" % (x, j, r) for r in range(N) for j in range(N)] for x in "WK"]
    N2r = [x for r in range(N) for x in ntok(r)]
    Rr = (["%s%d_%d" % (x, h, r) for x in "rs" for h in range(2) for r in range(N)] + ["Rt%d" % r for r in range(N)]
          + ["Ru%d" % r for r in range(N) if r != me])
    P2r = ["Q%d_%d" % (j, r) for r in range(N) for j in range(N)]
    if not ONE[0][1]:
        unpack("w", (0, 1), me)
    landed = [("kx"[ONE[0][1]], (0, 1), me)] + [x for x in landed if x[0] not in "rst"]
    for kind, hs, r in landed[:OPT["soon"]]:
        unpack(kind, hs, r)
    for rnd in range(3):
        owns, l2 = [], []
        for c, (b0, subs, kb, s0, s1, cb) in enumerate(CH):
            k0, w = 8 * b0, 8 * sum(subs)
            wp = (w + 15) // 16 * 16
            if rnd == 0:
                tabs = (ap(wts, 0, B), ap(kds, 0, B), noise(me, 0, H), [wts], [kds], ntok(me))
            else:
                tabs = (ap(wts, 0, B + rnd * MORE), ap(kds, 0, B + rnd * MORE), T.N1[:, 0:B + 384 * (rnd - 1)], [wts, "wx", "wy"][:1 + rnd],
                        [kds, "kx", "ky"][:1 + rnd], ["N1_0", "N1_1", "N1_2"][:1 + rnd])
            if ONE[rnd][0]:
                tabs = (T.P1[:, 0:B + rnd * MORE], None, tabs[2], ["P1_%d" % j for j in range(4 + rnd)], None, tabs[5])
            low, _ = draw(c, 0, OPT["pairs"][rnd][0], lists[c][0], lists[c][1], *tabs)
            u = UNIT / 16
            tm = [(diag(u), salB, ap(salB, k0, k0 + w))]
            for fb in st[c]["fb"]:
                tm += [(diag(KT * u), fb, ap(fb, 0, w)), (diag(-KT * u), fb, ap(fb, w, 2 * w))]
            if rnd:
                tm = modulo(tm, cb, 384, w, H * u)
            mm(turn(s0, 0, w, wide1, low, True, True), [low, wide1, "wide1b"], s0)
            terms(ps[cb][:, 0:w], tm, w, True, False, cb)
            mm(turn(cb, 0, w, wide1, low, True), [low, wide1, "wide1b"], cb)
            iv, hm, lb, lh = new("pi", w), new("pi", w), new("pu", w), new("pu", w)
            lin(ap(lb), ps[s0][:, 0:w], 1 / UNIT, B - 1, (), [lb], w, banks=[s0], on="v")
            lin(ap(iv), ps[cb][:, 0:w], ALPHA / UNIT, (B - 1) * ALPHA + 15.373, (), [iv], w, banks=[cb], on="v")
            ts(ap(hm), ap(iv), (N - 1) * GAP + H - 1, None, ALU.bitwise_and, None, [iv], [hm], w)
            lin(ap(lh), ap(hm), 1, 0, [hm], [lh], w, on="v")
            x, xa = lref(w)
            own = new("pb", wp)
            lin(ap(own), ap(hm).indirect(xa), 1 / GAP, 194 - 0.125, [hm, x], [own], wp, gather=True)
            owns.append(own)
            l2.append((lb, lh))
        if rnd == 0:
            lead[0] = float(len(CH) - 1)
            for kind, hs, r in landed[OPT["soon"]:]:
                unpack(kind, hs, r)
        j0 = 0 if rnd == 2 else 1
        for c, (b0, subs, kb, s0, s1, cb) in enumerate(CH):
            w = 8 * sum(subs)
            u = w + 1
            lead[0] = float(len(CH) - 1 - c)
            src, sn, rn = owns[c], sgn[c], run[c]
            if rnd == 2:
                src = new("pb", w)
                tt(ap(src), ap(owns[c], 0, w), ap(st[c]["takes"]), ALU.mult, [owns[c], st[c]["takes"]], [src], w)
            mt = ["sgn%d_%d" % (j, c) for j in range(N + 1)]
            rt_ = ["run%d_%d" % (j, c) for j in range(N + 1)]
            if c:
                up = 8 * sum(CH[c - 1][1]) + 1
                lin(ap(sn, j0 * u, N * u, u), ap(run[c - 1], (j0 + 1) * up - 1, N * up, up), 1, 0,
                    ["run%d_%d" % (j, c - 1) for j in range(j0, N)], ["carry%d" % c] + mt[:1 - j0], N)
            for j in range(j0, N):
                act(ap(sn, j * u + 1, (j + 1) * u), ap(src, 0, w), -193.5 - j, [src], [mt[j]], w, AF.Sign)
            scan(ap(rn, j0 * u, N * u), ap(rst[u], 0, (N - j0) * u), ap(sn, j0 * u, N * u), ALU.mult, ALU.add,
                 mt[j0:N] + [rst[u], "carry%d" % c], rt_[j0:N], (N - j0) * u, 0.5)
            sg = new("pb", N * u)
            mm(group(ps[cb][:, 128:128 + N * u], [(ap(tri), ap(sn, 0, N * u)), (ap(ntri), ap(sn, u, (N + 1) * u))], N * u, True, False),
               mt + ["carry%d" % c, tri, ntri], cb)
            mm(group(ps[cb][:, 128:128 + N * u], [(ap(blk), ap(rn, 0, N * u)), (ap(nblk), ap(rn, u, (N + 1) * u))], N * u, False, True),
               rt_ + [blk, nblk], cb)
            act(ap(sg), ps[cb][:, 128:128 + N * u], 1.0 - 2 * CAP, (), [sg], N * u, AF.Sign, banks=[cb], scale=-1.0)
            mm(group(ps[cb][:, 64:64 + w], [(ap(I), ap(sg, r * u + 1, (r + 1) * u)) for r in range(N)], w), [sg, I], cb)
            fl = new("pb", 2 * w)
            lin(ap(fl, 0, w), ps[cb][:, 64:64 + w], 1, 4 if rnd < 2 else -15, (), [fl[3] + "g"], w, banks=[cb])
            st[c]["fl"].append(fl)
            if rnd < 2:
                st[c]["next"] = [[(I, bsh[y], ap(bsh[y], 8 * b0, 8 * b0 + w))]
                                 + [(diag(2 * step % m // 2), f[3] + "g", ap(f, 0, w)) for f in st[c]["fl"]]
                                 + [(diag(-step % m), f, ap(f, w, 2 * w)) for f in st[c]["fl"][:rnd]]
                                 for y, (step, m) in enumerate(((K5, B), (KH, H)))]
                if OPT["fuse"]:
                    st[c]["lf"] = new("pf", w)
                    terms(ps[cb][:, 384:384 + w], st[c]["next"][0], w, True, True, cb)
                    lin(ap(st[c]["lf"]), ps[cb][:, 384:384 + w], 1, 0, (), [st[c]["lf"]], w, banks=[cb])
        if rnd == 0:
            lead[0] = float(len(CH) - 1)
            for r in (mate, far[0], far[1]):
                unpack_rooms(r)
        for c, (b0, subs, kb, s0, s1, cb) in enumerate(CH):
            k0, w = 8 * b0, 8 * sum(subs)
            S = st[c]
            fl = S["fl"][rnd]
            low, cq = draw(c, 1, OPT["pairs"][rnd][1], (l2[c][0], 0), (l2[c][1], 0),
                           *((T.P2[:], None, T.N2[:], P2r, None, N2r) if ONE[0][1] else (T.W2[:], T.KK[:], T.N2[:], W2r, KKr, N2r)))
            lr = new("pu", w)
            dv = ps[s0][:, 128:128 + w]
            terms(dv, [(diag(-D), owns[c], ap(owns[c], 0, w)), (diag(132 - 2047), c1536, ap(c1536, 0, w))], w, True, False, s0)
            mm(turn(s0, 128, w, rotm, low, False), [low, rotm], s0)
            mm(turn(s0, 128, w, rotc, cq, True), [cq, rotc], s0)
            lin(ap(lr), dv, 1, -1, (), [lr], w, banks=[s0], on=OPT["lr"])
            fuse = OPT["fuse"] or rnd == 2
            one_ = diag(OFF) if fuse else I
            extra = [(one_, fl[3] + "g", ap(fl, 0, w))]
            if rnd > 0:
                ne = new("pb", w)
                tt(ap(ne), dv, ap(S["one"]), ALU.not_equal, [S["one"]], [ne], w, 1.0, banks=[s0])
                extra.append((one_, ne, ap(ne)))
            if rnd == 2:
                da, db = new("pf", w), new("pf", w)
                tt(ap(da), dv, ap(S["ha"]), ALU.add, [S["ha"]], [da], w, 1.0, banks=[s0])
                tt(ap(db), dv, ap(S["hb"]), ALU.add, [S["hb"]], [db], w, 1.0, banks=[s0])
            else:
                tb_, th_ = S["next"]
                lraw = ps[s0][:, 192:192 + 2 * w]
                if s0 != s1:
                    terms(ps[s0][:, 192 + w:192 + 2 * w], th_, w, True, False, s0)
                if fuse:
                    lf, u = S["lf"], w + 1
                    extra = tb_ + [(diag(-96), c1536, ap(c1536, 0, w)), (diag(B - K5), "sgn0_%d" % c, ap(sgn[c], 1, u))] + extra
                    if rnd:
                        extra.insert(0, (one_, "sgn%d_%d" % (N, c), ap(sgn[c], N * u + 1, (N + 1) * u)))
                else:
                    terms(ps[s0][:, 192:192 + w], tb_, w, False, False, s0)
            a, n = 128 * b0, 16 * w
            x0, fts = 0, []
            for nb in OPT["split"][c][3]:
                e0_, e1_ = a + 128 * x0, a + 128 * (x0 + nb)
                fts.append("Ft%d_%d" % (c, x0))
                tt(T.Ft[:, e0_:e1_], R[:].indirect(ap(lr, 8 * x0, 8 * (x0 + nb))), ap(nds, e0_, e1_), ALU.is_ge, Rr + [lr, nds], fts[-1:],
                   128 * nb, gather=True)
                x0 += nb
            cnt = ps[s1][:, 0:w]
            pk = pickb if fuse else pick
            terms(cnt, extra[:len(extra) - (rnd > 0)], w, True, False, s1)
            if rnd:
                terms(cnt, extra[-1:], w, False, False, s1)
            mm(group(cnt, [(ap(pk, 15 - i, 143 - i), T.Ft[:, a + i:a + n:16]) for i in range(16)], w, False, True), fts + [pk], s1)
            if rnd < 2:
                k = ap(fl, w, 2 * w)
                l1, fb, x = new("pu", 2 * w), new("pb", 2 * w), new("pf", w)
                if fuse:
                    lb = new("pu", w)
                    if OPT["fuse"] == 1:
                        tt(ap(lb), cnt, ap(lf), ALU.max, [lf], [lb], w, 1.0, banks=[s1])
                    else:
                        li = new("pf", w)
                        tt(ap(li), cnt, ap(lf), ALU.max, [lf], [li], w, 1.0, banks=[s1])
                        lin(ap(lb), ap(li), 1, 0, [li], [lb], w)
                    ts(k, cnt, 0.0, None, ALU.is_ge, None, (), [fl], w, banks=[s1])
                    terms(ps[s0][:, 192 + w:192 + 2 * w], th_ * (s0 == s1) + [(diag(H - KH), fl, k)], w, s0 == s1, True, s0)
                    lin(ap(l1, 0, w), ps[s0][:, 192 + w:192 + 2 * w], 1, 0, (), [l1], w, banks=[s0], on=OPT["lr"])
                    lists[c] = ((lb, 0), (l1, 0))
                else:
                    lin(k, cnt, 1, -17 - rnd, (), [fl], w, banks=[s1], on="v", cut=True)
                    mm([(ps[s0][:, 192 + y * w:192 + (y + 1) * w], ap(diag(back)), k, False, y == 1, w)
                        for y, back in enumerate((B - K5, H - KH))], [fl, diag(B - K5), diag(H - KH)], s0)
                    lin(ap(l1), lraw, 1, 0, (), [l1], 2 * w, banks=[s0], on="V")
                    lists[c] = ((l1, 0), (l1, w))
                tt(ap(x), dv, k, ALU.mult, [fl], [x], w, 1.0, banks=[s0])
                y, ya = lref(2 * w)
                lin(ap(fb), ap(fl).indirect(ya), 1, 0, [fl, fl[3] + "g", y], [fb], 2 * w, gather=True)
                S["fb"].append(fb)
            if rnd == 0:
                S["one"] = x
            elif rnd == 1:
                two, sm, one, has, om, tm_, ha_, hb_ = [new("pf", w) for _ in range(8)]
                tk_ = new("pb", w)
                tt(ap(two), ap(x), ap(S["fl"][0], w, 2 * w), ALU.mult, [x, S["fl"][0]], [two], w)
                tt(ap(sm), ap(x), ap(S["one"]), ALU.add, [x, S["one"]], [sm], w)
                tt(ap(one), ap(sm), ap(two), ALU.subtract, [sm, two], [one], w)
                ts(ap(tk_), ap(two), 0.0, None, ALU.is_equal, None, [two], [tk_], w)
                act(ap(has), ap(one), 0.0, [one], [has], w, AF.Sign)
                lin(ap(ha_), ap(has), -OFF, -1, [has], [ha_], w)
                lin(ap(hb_), ap(has), OFF, -1 - OFF, [has], [hb_], w)
                lin(ap(om), ap(one), 1, -1, [one], [om], w)
                lin(ap(tm_), ap(two), 1, -1, [two], [tm_], w)
                S.update({"one": one, "takes": tk_, "ha": ha_, "hb": hb_, "om": om, "tm": tm_})
            else:
                for n_, (dd, old, out) in enumerate([(da, S["om"], T.ya), (db, S["tm"], T.yb)]):
                    u, y = new("pf", w), new("pf", w)
                    tt(ap(u), cnt, ap(dd), ALU.add, [dd], [u], w, 1.0, banks=[s1])
                    tt(ap(y), ap(u), ap(old), ALU.max, [u, old], [y], w)
                    dma("sa"[n_], out[:, k0:k0 + w], ap(y), [y], ["out%d%d" % (c, n_)], 2000)

    if PLAN.get("n") != len(ops):
        PLAN["n"] = len(ops)
        PLAN["order"], PLAN["pick"], PLAN["times"] = make_order(ops, OPT)
    order = PLAN["order"]

    count = {e: 0 for e in queue}
    known = {e: {} for e in queue}
    mark, total = {}, {}
    needed = set()
    for o_ in ops:
        needed |= o_["deps"]
    place = {i: n_ for n_, i in enumerate(order)}
    for i in order:
        o_ = ops[i]
        e, fn, _c = o_["alt"][PLAN["pick"][i]]
        if e is not None:
            want = {}
            for d_ in o_["deps"]:
                s, v, _k = mark[d_]
                if v > want.get(s, (0, None))[0]:
                    want[s] = (v, d_)
            for s, (v, d_) in sorted(want.items(), key=lambda x: -place[x[1][1]]):
                if known[e].get(s, 0) < v:
                    queue[e].wait_ge(T.sem[s], v)
                    known[e][s] = v
                    for s2, v2 in mark[d_][2].items():
                        known[e][s2] = max(known[e].get(s2, 0), v2)
            inst = fn()
        if o_["sem"] == "none":
            continue
        if o_["sem"] is not None:
            s, v = o_["sem"]
            if e is not None:
                inst.then_inc(T.sem[s], v)
        else:
            if i not in needed:
                continue
            count[e] += 1
            s, v = "c" + e, count[e]
            inst.then_inc(T.sem[s], 1)
        mark[i] = (s, v, dict(known[e]) if e is not None else {})
        total[s] = v
    total["sent"] = sent[0]
    for s, v in total.items():
        g.wait_ge(T.sem[s], v)
